import numpy as np, ml_dtypes
CORES = [2,3,42,43,82,83,122,123]
N = 8
BF = ml_dtypes.bfloat16
C, L, B, S, P, VOTE = 1536, 192, 3, 5, 4, 60
R = B * L
M = N * R
def parts(rng):
    z = rng.integers(0, 256, (N, 8, 16, C)) + rng.integers(-64, 65, (N, 8, 1, C))
    return {"cd": rng.integers(0, 16, (N, 8, 16, C)), "zt": np.clip(z, 0, 255), "kid": rng.integers(0, C, (N, 8, C)), "ky": rng.integers(0, C, (N, 8, C)),
            "e0": rng.integers(0, M, (N, 8, 16, L)), "c0": rng.integers(0, C, (N, 8, L)), "x0": rng.integers(0, 256, (N, 8, 16, R)),
            "ce0": rng.integers(0, M, (N, 8, 16, R)), "cc0": rng.integers(0, C, (N, 8, R))}
def pack(d):
    o = {}
    for k in ("cd", "zt", "kid", "ky", "e0", "c0", "x0", "ce0", "cc0"):
        v = np.ascontiguousarray(d[k].reshape(N, -1, d[k].shape[-1]))
        o[k] = v.astype(np.float32).astype(BF) if k in ("zt", "x0") else v.astype(np.int32)
    return o
def setup_inputs(rng):
    return pack(parts(rng))
def uneven(rng, n, shape, coin):
    v = np.minimum(np.exp2(rng.random(shape) * np.log2(n + 1.0)).astype(np.int64) - 1, n - 1)
    return np.where(rng.random(coin) < 0.5, v, n - 1 - v)
def setup_inputs_spread(rng):
    return pack({"cd": uneven(rng, 16, (N, 8, 16, C), (N, 8, 1, C)), "zt": uneven(rng, 256, (N, 8, 16, C), (N, 8, 1, C)),
                 "kid": uneven(rng, C, (N, 8, C), (N, 8, C)), "ky": uneven(rng, C, (N, 8, C), (N, 8, C)),
                 "e0": uneven(rng, M, (N, 8, 16, L), (N, 8, 1, L)), "c0": uneven(rng, C, (N, 8, L), (N, 8, L)),
                 "x0": uneven(rng, 256, (N, 8, 16, R), (N, 8, 1, R)), "ce0": uneven(rng, M, (N, 8, 16, R), (N, 8, 1, R)), "cc0": uneven(rng, C, (N, 8, R), (N, 8, R))})
def mix(rng, hi, *shape):
    v = np.where(rng.random(shape) < 0.5, 0, hi)
    return np.where(rng.random(shape) < 0.72, v, rng.integers(0, hi + 1, shape))
def setup_inputs_ends(rng):
    d = {"cd": mix(rng, 15, N, 8, 16, C), "zt": mix(rng, 255, N, 8, 16, C), "kid": mix(rng, C - 1, N, 8, C), "ky": mix(rng, C - 1, N, 8, C),
         "e0": mix(rng, M - 1, N, 8, 16, L), "c0": mix(rng, C - 1, N, 8, L), "x0": mix(rng, 255, N, 8, 16, R), "ce0": mix(rng, M - 1, N, 8, 16, R), "cc0": mix(rng, C - 1, N, 8, R)}
    rec = rng.random((N, 8, 1, R)); d["x0"] = np.where(rec < 0.15, 0, np.where(rec < 0.3, 255, d["x0"]))
    d["e0"][:, :, 0] = np.where(rng.random((N, 8, L)) < 0.8, rng.integers(0, M, (N, 8, L)), d["e0"][:, :, 0])
    d["ce0"][:, :, 0] = np.where(rng.random((N, 8, R)) < 0.8, rng.integers(0, M, (N, 8, R)), d["ce0"][:, :, 0])
    d["cd"][:, :, 0] = np.where(rng.random((N, 8, C)) < 0.7, 0, d["cd"][:, :, 0])
    d["x0"][0, :, :, 0] = 0; d["x0"][N - 1, :, :, R - 1] = 255
    cd, zt, c0 = d["cd"], d["zt"], d["c0"]
    cd[:, :, :8, C - 1] = 0; cd[:, :, 8:, C - 1] = 15
    cd[:, :, :, 0] = 0; cd[:, :, 15, 0] = 15
    cd[:, :, :, C - 2] = 0
    zt[..., 0] = np.where(rng.random((N, 8, 16)) < 0.5, 255, 0); zt[..., C - 2] = 255
    for q in range(N):
        v = np.full(128, 255); v[rng.permutation(128)[:VOTE - q % 2]] = 0; zt[q, :, :, C - 1] = v.reshape(8, 16)
    c0[..., 0] = C - 1; c0[..., L - 1] = C - 1; c0[..., 1] = 0; c0[..., L - 2] = 0; c0[..., 2] = C - 2; c0[..., L - 3] = C - 2
    for i in (0, 1, 2, L - 3, L - 2, L - 1): d["e0"][:, :, 0, i] = 0; d["e0"][:, :, 15, i] = M - 1
    return pack(d)
def setup_inputs_corners(rng):
    d = parts(rng); own = lambda n, top, *lead: 16 * rng.integers(0, top // 16, lead + (n,)) + np.arange(n) % 16
    d["kid"] = own(C, C, N, 8); d["ky"] = own(C, C, N, 8); d["e0"] = own(L, M, N, 8, 16); d["c0"] = own(L, C, N, 8); d["ce0"] = own(R, M, N, 8, 16); d["cc0"] = own(R, C, N, 8)
    d["x0"] = 2 * rng.integers(0, 128, (N, 8, 16, R)); d["e0"][:, :, 0, 0] = 0; d["e0"][:, :, 15, L - 1] = M - 1; d["c0"][..., 0] = 0; d["c0"][..., L - 1] = C - 1
    want = (0, 1, 2, 3, VOTE - 16, VOTE - 2, VOTE - 1, VOTE - 1, VOTE, VOTE, VOTE + 1, VOTE + 16, 112, 126, 127, 128)
    need = np.zeros((N, 8, 16), np.int64)
    for q in range(N):
        for k in range(16): need[q, :, k] = np.bincount(rng.permutation(128)[:want[(k + 5 * q) % 16]] // 16, minlength=8)
    place = np.argsort(np.argsort(rng.random((N, 8, 16, C)), axis=2), axis=2)
    d["zt"] = np.where(place < need[:, :, np.arange(C) % 16][:, :, None, :], 0, 255)
    return pack(d)
def setup_inputs_crowd(rng):
    d = parts(rng); mode = rng.permutation(8); s = np.arange(R)
    one = rng.choice(np.array([0, M - 1, M // 2, R - 1]), 8); lane = int(rng.integers(0, L))
    for q in range(N):
        for g in range(8):
            m = mode[g]
            if m < 2:
                ke, kc = d["e0"][q, g, :, lane].copy(), d["c0"][q, g, lane]
                d["e0"][q, g] = one[g]; d["c0"][q, g] = (0, C - 1)[q % 2]
                if m == 1: d["e0"][q, g, :, lane] = ke; d["c0"][q, g, lane] = (kc + (kc == 0)) % (C - 1)
            elif m == 2: d["e0"][q, g] = np.where(rng.random((16, L)) < 0.5, 0, M - 1)
            elif m == 3: d["e0"][q, g] = q * R + np.arange(L); d["ce0"][q, g] = q * R + s
            elif m == 4: d["cd"][q, g] = 0
            elif m == 5: d["cd"][q, g] = 15
            elif m == 6: d["ce0"][q, g] = (q * R + s + 1) % M; d["cd"][q, g] = np.arange(16)[:, None]
            else:
                for k in ("c0", "kid", "ky", "cc0"): d[k][q, g] = rng.choice(np.array([0, C - 1, C // 2]), d[k][q, g].shape)
    return pack(d)
def setup_inputs_full(rng):
    d = parts(rng); K = 16 // N; kind = rng.permutation(np.arange(N) % 4)[:, None, None]; o = int(rng.integers(0, N))
    cd = np.argsort(rng.random((N, 8, 16, C)), axis=2); u = (np.arange(N) + int(rng.integers(0, N))).reshape(N, 1, 1, 1)
    cd = (cd + (u - cd[:, :, :1]) % N) % 16
    s = np.argsort(rng.random((N, 8, B, N, R)), axis=4)[..., :K * L].reshape(N, 8, B, N, K, L)
    s = s + R * ((np.arange(8)[:, None] + np.arange(N)[None, :]) % N).reshape(1, 8, 1, N, 1, 1)
    c0 = 2 * np.argsort(rng.random((N, 8, C // 2)), axis=2)[..., :L] + np.where(kind < 2, rng.integers(0, 2, (N, 8, L)), kind - 2)
    kid = np.argsort(rng.random((N, 8, C)), axis=2); kk = kind[..., None]
    e0 = o * R + rng.integers(0, R, (N, 8, 16, L))
    t0 = o * R + L * rng.integers(0, B, (N, 8, 1)) + np.argsort(rng.random((N, 8, L)), axis=2)
    np.put_along_axis(e0, np.take_along_axis(cd[:, :, 0], c0, 2)[:, :, None, :], t0[:, :, None, :], 2)
    d["cd"] = cd; d["ce0"] = s.transpose(0, 1, 4, 3, 2, 5).reshape(N, 8, 16, R); d["c0"] = c0; d["e0"] = e0
    d["kid"] = np.where(kind < 2, kid, kid | 1); d["ky"] = d["ky"] & -2; d["cc0"] = d["cc0"] & -2; d["x0"] = d["x0"] & -2
    z = np.where(kk == 0, 0, np.where(kk == 1, 255, 255 * (np.arange(C) % 2)))
    d["zt"] = np.array(np.broadcast_to(z, (N, 8, 16, C)))
    return pack(d)
def check_inputs(d):
    bad = []
    for k, hi in (("cd", 15), ("zt", 255), ("kid", C - 1), ("ky", C - 1), ("e0", M - 1), ("c0", C - 1), ("x0", 255), ("ce0", M - 1), ("cc0", C - 1)):
        v = np.asarray(d[k]).astype(np.float64)
        if not (np.min(v) >= 0 and np.max(v) <= hi): bad.append("range of " + k)
        elif np.any(v != np.floor(v)): bad.append("whole numbers of " + k)
    return bad
def reference(cd, zt, kid, ky, e0, c0, x0, ce0, cc0):
    row = cd.astype(np.int64).reshape(N, 8, 16, C); z = zt.astype(np.float32).astype(np.int64).reshape(N, 8, 16, C)
    kd = kid.astype(np.int64); kc = ky.astype(np.int64); e = e0.astype(np.int64).reshape(N, 8, 16, L); c = c0.astype(np.int64)
    hx = np.array(x0.astype(np.float32).astype(np.int64).reshape(N, 8, 16, R).transpose(1, 2, 0, 3)).reshape(8, 16, M)
    he = np.array(ce0.astype(np.int64).reshape(N, 8, 16, R).transpose(1, 2, 0, 3)).reshape(8, 16, M)
    hc = np.array(cc0.astype(np.int64).transpose(1, 0, 2)).reshape(8, M)
    out = []
    for t in range(S):
        nm = np.take_along_axis(e, np.take_along_axis(row, c[:, :, None, :], 3), 2)
        w = []
        for q in range(N):
            v = np.take_along_axis(hx, nm[q].reshape(8, 1, 16 * L), 2).reshape(8, 16, 16 // P, P, L)
            w.append(np.add.reduce(np.maximum.reduce(v, axis=2), axis=2) & 255)
        w = np.stack(w)
        yes = (w >= np.take_along_axis(z, c[:, :, None, :], 3)).astype(np.int64)
        binds = np.add.reduce(yes.reshape(N, 128, L), axis=1) >= VOTE
        place = np.arange(N)[:, None] * R + L * (t % B) + np.arange(L)[None, :]
        first = np.broadcast_to(place[:, None, None, :], (N, 8, 1, L))
        eb = np.concatenate([first, e[:, :, :15]], axis=2)
        ea = np.stack([np.take_along_axis(he, nm[q][:, 0:1, :], 2) for q in range(N)])
        ca = np.stack([np.take_along_axis(hc, nm[q][:, 0, :], 1) for q in range(N)])
        en = np.where(binds[:, None, None, :], eb, ea); cn = np.where(binds[:, None, :], np.take_along_axis(kd, c, 2), ca)
        if t < S - 1:
            kq = np.take_along_axis(kc, c, 2)
            for q in range(N):
                lo = q * R + L * (t % B)
                hx[:, :, lo:lo + L] = w[q]; he[:, :, lo:lo + L] = e[q]; hc[:, lo:lo + L] = kq[q]
        e = en; c = cn; out.append(w.reshape(N, 128, L))
    return {"ye": e.reshape(N, 128, L).astype(np.float32), "yc": c.astype(np.float32), "yx": np.concatenate(out, axis=2).astype(np.float32).astype(BF)}

@@ -1,0 +1,471 @@
+from concourse.bass import DstId, RemoteDMATransfer
+from concourse.mybir import AluOpType as A, ActivationFunctionType as F
+
+N, C, L, R, M, S = 8, 1536, 192, 576, 4608, 5
+NB = N * L
+W = M + (S - 1) * NB
+CORES_ALL = 128
+LS, LS1 = 112, 80
+ENV32 = True
+ROUTE = {"xi": "split0", "ei": "split1", "e": "split0", "w": "own"}
+BIG = 262144.0
+MAGIC = 12582912.0
+
+SCRATCH = {
+    "XW": ("sbuf", [128, W], "bfloat16"), "EW": ("sbuf", [128, W], "float32"), "EU": ("sbuf", [128, W], "uint16"),
+    "cdt": ("sbuf", [128, C], "int32"), "ztt": ("sbuf", [128, C], "bfloat16"), "kk": ("sbuf", [128, C], "int32"),
+    "cei": ("sbuf", [128, R], "int32"), "cci": ("sbuf", [128, R], "int32"), "cef": ("sbuf", [128, R], "float32"),
+    "e0i": ("sbuf", [128, L], "int32"), "c0i": ("sbuf", [128, L], "int32"),
+    "G": ("sbuf", [128, 16 * L], "bfloat16"), "H": ("sbuf", [128, 16 * L], "bfloat16"), "X": ("sbuf", [128, 16 * L], "bfloat16"),
+    "keep": ("sbuf", [128, 16 * LS1], "bfloat16"),
+    "sci": ("sbuf", [128, 8], "int32"), "sc": ("sbuf", [128, 32], "float32"),
+    "wl": ("sbuf", [128, L], "bfloat16"),
+    "qL": ("sbuf", [128, 16], "uint16"), "tL": ("sbuf", [128, 16], "uint16"),
+    "eo": ("sbuf", [128, L], "uint16"), "vo": ("sbuf", [128, L], "uint16"),
+}
+for _n in ("col", "a16", "rst", "Ef", "Eo", "Ra", "dR", "Rn", "tmp", "msk", "scn", "scq", "Pp", "oh", "oha", "Ff", "Fg", "Fh", "qf", "mm", "c0f"):
+    SCRATCH[_n] = ("sbuf", [128, L], "float32")
+for _n in ("colb", "pen", "base", "ones", "Vb", "zg", "yes", "tq", "Dg", "ub", "rb"):
+    SCRATCH[_n] = ("sbuf", [128, L], "bfloat16")
+for _n in ("dif", "g16", "I32", "Blk", "Sh", "MY", "MK", "m1", "m2"):
+    SCRATCH[_n] = ("sbuf", [128, 128], "float32")
+for _n in ("Ib", "Perm", "Bc0", "Wq", "I0", "In0", "In1", "In2", "Iu", "Ir", "I3", "Id", "k384", "k8192", "kd"):
+    SCRATCH[_n] = ("sbuf", [128, 128], "bfloat16")
+for _k in range(8):
+    SCRATCH["p%d" % _k] = ("psum", [128, 512], "float32")
+
+PHASES = ["xi", "ei"]
+PHASES += ["w0", "e0"]
+for _t in range(1, S - 1):
+    PHASES += ["e%d" % _t, "w%d" % _t]
+SEMAPHORES = ["sv", "ss", "sp", "sg", "ls", "lx", "so", "dx", "dce", "dcc", "de", "dc", "dcd", "dz", "dk"]
+SEMAPHORES += ["a" + p for p in PHASES] + ["v%s_%d" % (p, k) for p in PHASES for k in range(2)]
+
+
+def piece(T, ph, r):
+    if ph == "xi":
+        return T.XW[:, r * R:(r + 1) * R]
+    if ph == "ei":
+        return T.EU[:, r * R:(r + 1) * R]
+    lo = M + NB * int(ph[1]) + L * r
+    if ph[0] == "w":
+        return T.XW[:, lo:lo + L]
+    return T.EW[:, lo:lo + L] if ENV32 else T.EU[:, lo:lo + L]
+
+
+def routes(T, topo):
+    cores = list(T.cores)
+    chips = {}
+    for c in cores:
+        chips.setdefault(topo.chip(c), []).append(c)
+    via = {}
+    for ch, rk in chips.items():
+        near = lambda c: (topo.die(c) != topo.die(rk[0]), c)
+        own = sorted([c for c in topo.cores_of(rk[0]) if c not in cores], key=near)
+        rel = sorted([c for c in range(CORES_ALL) if topo.mates(topo.chip(c), ch) and c not in cores
+                      and all(topo.may_write(c, d) for d in rk)], key=near)
+        src = [r for r in range(N) if topo.chip(cores[r]) != ch]
+        for ph in PHASES:
+            mode = ROUTE[ph] if ph in ROUTE else ROUTE[ph[0]]
+            for n, r in enumerate(src):
+                if mode == "direct":
+                    v = None
+                elif mode == "own":
+                    v = own[n]
+                elif mode == "fwd":
+                    v = rk[r % 2]
+                elif mode[0] == "h":
+                    order = list(chips)
+                    back = (order.index(ch) - order.index(topo.chip(cores[r]))) % len(order)
+                    v = own[2 * (back - 1) + r % 2] if back <= int(mode[1]) else None
+                elif mode == "split0":
+                    v = own[n // 2] if r % 2 == 0 else rel[n // 2]
+                else:
+                    v = own[3 + n // 2] if r % 2 == 1 else rel[len(rel) - 1 - n // 2]
+                via[(ph, r, ch)] = v
+    return chips, via
+
+
+def bits(m):
+    return bin(m).count("1")
+
+
+def dst_id(topo, c):
+    a = topo.addr(c)
+    return DstId(rid=a[0], pnc=a[1])
+
+
+def helper_program(g, core, T, topo, chips, via):
+    sent = 0
+    for ph in PHASES:
+        for r in range(N):
+            for ch, rk in chips.items():
+                if via.get((ph, r, ch)) == core:
+                    g.wait_ge(T.sem["v%s_%d" % (ph, r % 2)], bits(topo.mask(T.cores[r], core)))
+                    m = topo.mask(core, rk[0])
+                    ap = piece(T, ph, r)
+                    g.remote_dma_fused([RemoteDMATransfer(dst_ids=[dst_id(topo, d) for d in rk], dma_engine_mask=m,
+                                                          remote_sem=T.sem["a" + ph], src=ap, dsts=[ap for d in rk])],
+                                       local_sem=T.sem.ls)
+                    sent += bits(m)
+    if sent:
+        g.wait_ge(T.sem.ls, sent)
+
+
+def rank_program(g, core, T, topo):
+    chips, via = routes(T, topo)
+    rank = T.rank_of(core)
+    if rank is None:
+        helper_program(g, core, T, topo, chips, via)
+        return
+    cores = list(T.cores)
+    chip = topo.chip(core)
+    sib = [c for c in chips[chip] if c != core][0]
+    far = [c for c in cores if topo.chip(c) != chip][0]
+    off_mask = topo.mask(core, far)
+    on_mask = topo.mask(core, sib) & ~off_mask
+
+    Q = {"v": g.vector, "s": g.scalar, "p": g.tensor, "g": g, "y": g.sync}
+    SEM = {"v": "sv", "s": "ss", "p": "sp", "g": "sg"}
+    count = {"sv": 0, "ss": 0, "sp": 0, "sg": 0, "ls": 0, "lx": 0, "so": 0}
+    seen = {k: {} for k in Q}
+    wrote, read = {}, {}
+
+    def need(e, rd, wr):
+        toks = {}
+        for r in rd:
+            for s, v in wrote.get(r, []):
+                toks[s] = max(toks.get(s, 0), v)
+        for r in wr:
+            for s, v in wrote.get(r, []) + read.get(r, []):
+                toks[s] = max(toks.get(s, 0), v)
+        for s, v in toks.items():
+            if seen[e].get(s, 0) < v:
+                Q[e].wait_ge(T.sem[s], v)
+                seen[e][s] = v
+
+    def done(tok, rd, wr):
+        for r in rd:
+            read.setdefault(r, []).append(tok)
+        for r in wr:
+            wrote[r] = [tok]
+            read[r] = []
+
+    def op(e, fn, rd, wr):
+        wr = list(wr) + [r for r in rd if r[0] == "p" and r[1:].isdigit()]
+        need(e, rd, wr)
+        count[SEM[e]] += 1
+        fn(Q[e]).then_inc(T.sem[SEM[e]], 1)
+        done((SEM[e], count[SEM[e]]), rd, wr)
+
+    def mms(bank, out, terms):
+        need("p", [], [bank])
+        rd = []
+        for n, (a, b, names) in enumerate(terms):
+            need("p", names, [])
+            rd += names
+            ins = g.tensor.matmul(out, a, b, n == 0, n == len(terms) - 1)
+        count["sp"] += 1
+        ins.then_inc(T.sem.sp, 1)
+        done(("sp", count["sp"]), rd, [bank])
+
+    def dmas(e, sem, pairs, rd, wr):
+        need(e, rd, wr)
+        for o, i in pairs:
+            Q[e].dma_start(o, i).then_inc(T.sem[sem], 16)
+            count[sem] = count.get(sem, 0) + 16
+        if sem != "so":
+            done((sem, count[sem]), rd, wr)
+
+    def send(ph, name):
+        need("g", [name], [])
+        ap = piece(T, ph, rank)
+        handed, direct = [], []
+        for ch, rk in chips.items():
+            if ch != chip:
+                v = via[(ph, rank, ch)]
+                if v is None:
+                    direct += rk
+                else:
+                    handed.append(v)
+        ls = "lx" if ph == "xi" else "ls"
+        near = [RemoteDMATransfer(dst_ids=[dst_id(topo, sib)], dma_engine_mask=on_mask, remote_sem=T.sem["a" + ph], src=ap, dsts=[ap])]
+        count[ls] += bits(on_mask)
+        for out, sem in ((handed, "v%s_%d" % (ph, rank % 2)), (direct, "a" + ph)):
+            if out:
+                g.remote_dma_fused([RemoteDMATransfer(dst_ids=[dst_id(topo, d) for d in out], dma_engine_mask=off_mask,
+                                                      remote_sem=T.sem[sem], src=ap, dsts=[ap for d in out])] + near,
+                                   local_sem=T.sem[ls])
+                count[ls] += bits(off_mask)
+                near = []
+        if ph == "xi":
+            wrote["sentx"] = [("lx", count["lx"])]
+        mine = [r for r in range(N) if via.get((ph, r, chip)) == core]
+        if mine:
+            g.wait_ge(T.sem["v%s_%d" % (ph, rank % 2)], bits(off_mask) * len(mine))
+            eng = topo.engines(core, sib)[::-1]
+            k = len(eng) // 4
+            g.remote_dma_fused([RemoteDMATransfer(dst_ids=[dst_id(topo, sib)], dma_engine_mask=sum(1 << e for e in eng[k * n:k * n + k]),
+                                                  remote_sem=T.sem["a" + ph], src=piece(T, ph, r), dsts=[piece(T, ph, r)])
+                                for n, r in enumerate(mine)], local_sem=T.sem.ls)
+            count["ls"] += k * len(mine)
+
+    for ph in PHASES:
+        n, here = bits(on_mask), 0
+        for r in range(N):
+            if topo.chip(cores[r]) != chip:
+                v = via[(ph, r, chip)]
+                if v == core:
+                    here += bits(off_mask)
+                elif v == sib:
+                    n += bits(topo.mask(sib, core)) // 4
+                else:
+                    n += bits(topo.mask(cores[r] if v is None else v, core))
+        wrote["in" + ph] = [("a" + ph, n)] + ([("v%s_%d" % (ph, rank % 2), here)] if here else [])
+
+    def ts(out, in0, s1, s2, o0, o1, rd, wr):
+        if s2 is None:
+            op("v", lambda q: q.tensor_scalar(out, in0, s1, None, o0), rd, wr)
+        else:
+            op("v", lambda q: q.tensor_scalar(out, in0, s1, s2, o0, o1), rd, wr)
+
+    def tt(out, in0, in1, o, rd, wr):
+        op("v", lambda q: q.tensor_tensor(out, in0, in1, o), rd, wr)
+
+    def cp(out, in0, rd, wr):
+        op("v", lambda q: q.tensor_copy(out, in0), rd, wr)
+
+    def ms(ap, val, wr):
+        op("v", lambda q: q.memset(ap, val), [], wr)
+
+    def act(out, in0, fn, rd, wr, bias=0.0, scale=1.0):
+        if fn == F.Copy:
+            op("s", lambda q: q.activation(out, in0, fn), rd, wr)
+        else:
+            op("s", lambda q: q.activation(out, in0, fn, bias=bias, scale=scale), rd, wr)
+
+    def iota(out, pat, base, cm, wr, flt=True):
+        if flt:
+            op("g", lambda q: q.iota(out, pat, base, cm, allow_small_or_imprecise_dtypes=True), [], wr)
+        else:
+            op("g", lambda q: q.iota(out, pat, base, cm), [], wr)
+
+    P = [T["p%d" % k][:, 0:L] for k in range(8)]
+    sc = lambda k: T.sc[:, k:k + 1]
+    qL, tL = T.qL[:, 0:L // 16], T.tL[:, 0:L // 16]
+
+    dmas("y", "dx", [(piece(T, "xi", rank), T.x0[:])], [], ["xi"])
+    dmas("y", "dce", [(T.cei[:], T.ce0[:])], [], ["cei"])
+    iota(T.sci[:, 0:1], [[0, 1]], 0, 1, ["pi"], flt=False)
+    iota(T.dif[:], [[1, 128]], 0, -1, ["dif"])
+    iota(T.g16[:], [[1, 8], [0, 16]], 0, 0, ["g16"])
+    iota(T.a16[:], [[0, L // 16], [1, 16]], 0, 0, ["a16"])
+    iota(T.col[:], [[1, L]], 0, 0, ["col"])
+    send("xi", "xi")
+    ms(T.cci[:], 0, ["cci"])
+    ms(T.c0i[:], 0, ["c0i"])
+    dmas("y", "dcc", [(T.cci[j::16, :], T.cc0[:]) for j in range(4)], [], ["cci"])
+    dmas("s", "dc", [(T.c0i[0::16, :], T.c0[:])], [], ["c0i"])
+    dmas("s", "de", [(T.e0i[:], T.e0[:])], [], ["e0i"])
+    dmas("s", "dcd", [(T.cdt[:], T.cd[:])], [], ["cdt"])
+    ts(T.sci[:, 1:2], T.sci[:, 0:1], 15, None, A.bitwise_and, None, ["pi"], ["i1"])
+    ts(T.sci[:, 2:3], T.sci[:, 0:1], 3, None, A.bitwise_and, None, ["pi"], ["i2"])
+    ts(T.sci[:, 3:4], T.sci[:, 0:1], 1, None, A.bitwise_and, None, ["pi"], ["i3"])
+    ts(T.sci[:, 4:5], T.sci[:, 0:1], 1, 1, A.logical_shift_right, A.bitwise_and, ["pi"], ["i4"])
+    cp(T.sc[:, 0:5], T.sci[:, 0:5], ["pi", "i1", "i2", "i3", "i4"], ["c0"])
+    ts(sc(5), sc(3), -0.875, 1.0, A.mult, A.add, ["c0"], ["c5"])
+    ts(sc(6), sc(4), -63.0 / 64.0, 1.0, A.mult, A.add, ["c0"], ["c6"])
+    ts(sc(7), sc(1), 4.0, 8192.0, A.is_lt, A.mult, ["c0"], ["c7"])
+    ts(sc(8), sc(5), sc(6), None, A.mult, None, ["c5", "c6"], ["c8"])
+    ts(sc(9), sc(8), sc(7), None, A.mult, None, ["c8", "c7"], ["c9"])
+    ms(T.kk[:], 0, ["kk"])
+    dmas("y", "dk", [(T.kk[j::16, :], T.ky[:] if j < 4 else T.kid[:]) for j in range(8)], ["sentx"], ["kk"])
+    dmas("y", "dz", [(T.ztt[:], T.zt[:])], [], ["ztt"])
+    ts(sc(10), sc(0), sc(1), 1.0 / 16.0, A.subtract, A.mult, ["c0"], ["c10"])
+    ts(sc(11), sc(2), 3.75, sc(0), A.mult, A.add, ["c0"], ["c11"])
+    ts(sc(12), sc(1), -0.75, sc(11), A.mult, A.add, ["c0", "c11"], ["c12"])
+    ts(sc(13), sc(1), 0.0, None, A.is_equal, None, ["c0"], ["c13"])
+    ts(sc(14), sc(1), -1.0, None, A.mult, None, ["c0"], ["c14"])
+    ts(T.I32[:], T.dif[:], 0.0, None, A.is_equal, None, ["dif"], ["I32"])
+    ts(T.Blk[:], T.g16[:], sc(10), None, A.is_equal, None, ["g16", "c10"], ["Blk"])
+    ts(T.pen[:], T.a16[:], sc(1), -BIG, A.not_equal, A.mult, ["a16", "c0"], ["pen"])
+    ts(T.cci[:], T.cci[:], sc(9), None, A.mult, None, ["cci", "c9"], ["cci"])
+    ts(T.cci[:], T.cci[:], 7 * 8192, None, A.bitwise_and, None, ["cci"], ["cci"])
+    tt(T.cef[:], T.cci[:], T.cei[:], A.add, ["cci", "cei"], ["cef"])
+    cp(piece(T, "ei", rank), T.cef[:], ["cef"], ["ei"])
+    send("ei", "ei")
+    act(T.Ib[:], T.I32[:], F.Copy, ["I32"], ["Ib"])
+    act(T.colb[:], T.col[:], F.Copy, ["col"], ["colb"])
+    act(T.base[:, 0:LS], T.col[:, 0:LS], F.Identity, ["col"], ["base1"], scale=16.0)
+    act(T.base[:, LS:L], T.col[:, 0:L - LS], F.Identity, ["col"], ["base2"], scale=16.0)
+    cp(T.c0f[:], T.c0i[:], ["c0i"], ["c0f"])
+    ms(T.rst[:], 0.0, ["rst"])
+    ms(T.rst[:, 0::16], -4.0 * BIG, ["rst"])
+
+    def lane_list(bank, terms, scn, name, out, shift):
+        mms("p%d" % bank, P[bank], [(T.Ib[:], T.pen[:], ["Ib", "pen"])] + terms)
+
+        def rest():
+            op("v", lambda q: q.tensor_tensor_scan(T[scn][:], T.rst[:], P[bank], 0.0, A.add, A.max), ["rst", "p%d" % bank], [scn])
+            ts(out, T[scn][:, 15::16], shift, None, A.add, None, [scn], [name])
+        return rest
+
+    fin = lane_list(3, [(T.Blk[:], T.c0f[:], ["Blk", "c0f"])], "scq", "qL", qL, 0.0)
+    ts(T.Perm[:], T.col[:, 0:128], sc(12), None, A.is_equal, None, ["col", "c12"], ["Perm"])
+    ts(T.Bc0[:], T.g16[:], sc(10), sc(13), A.is_equal, A.mult, ["g16", "c10", "c13"], ["Bc0"])
+    cp(T.Ef[:], T.e0i[:], ["e0i"], ["Ef"])
+    cp(T.eo[:], T.e0i[:], ["e0i"], ["eo"])
+    fin()
+    ms(T.keep[:], 1.0, ["keep"])
+    ms(T.keep[:, 0::4], 0.0, ["keep"])
+    ms(T.ones[:], 1.0, ["ones"])
+    ms(T.k384[:], 384.0, ["k384"])
+
+    def picks():
+        cp(T.Vb[:], T.cdt[:, 0:C].indirect(qL), ["cdt", "qL"], ["Vb"])
+        mms("p6", P[6], [(T.Ib[:], T.base[:], ["Ib", "base1", "base2"]), (T.Perm[:], T.Vb[:], ["Perm", "Vb"])])
+        mms("p2", P[2], [(T.Bc0[:], T.Vb[:], ["Bc0", "Vb"])])
+        act(T.oha[:], P[2], F.Abs, ["p2", "c14"], ["oha"], bias=sc(14))
+        act(T.oh[:], T.oha[:], F.Relu, ["oha"], ["oh"], bias=1.0, scale=-1.0)
+
+    def codes():
+        ts(T.Ff[:], T.kk[:, 0:C].indirect(qL), sc(8), -0.499, A.mult, A.add, ["kk", "qL", "c8"], ["Ff"])
+        act(T.Fg[:], T.Ff[:], F.Identity, ["Ff"], ["Fg"], bias=MAGIC)
+        act(T.Fh[:], T.Fg[:], F.Identity, ["Fg"], ["Fh"], bias=-MAGIC)
+        act(T.zg[:], T.ztt[:, 0:C].indirect(qL), F.Copy, ["ztt", "qL"], ["zg"])
+
+    def record(t):
+        if t < S - 1:
+            mms("p7", P[7], [(T.I32[:], T.Ef[:], ["I32", "Ef"]), (T.MY[:], T.Fh[:], ["MY", "Fh"])])
+            if ENV32:
+                act(piece(T, "e%d" % t, rank), P[7], F.Copy, ["p7"], ["e%d" % t])
+            else:
+                cp(piece(T, "e%d" % t, rank), P[7], ["p7"], ["e%d" % t])
+            send("e%d" % t, "e%d" % t)
+        b = "In%d" % (t % 3)
+        mms("p1", P[1], [(T.I0[:], T.colb[:], ["I0", "colb"]), (T[b][:], T.ones[:], [b, "ones"]),
+                         (T.Sh[:], T.Ef[:], ["Sh", "Ef"]), (T.MK[:], T.Fh[:], ["MK", "Fh"])])
+
+    def first_name(eoff):
+        tt(T.Pp[:], T.oh[:], T[eoff][:], A.mult, ["oh", eoff], ["Pp"])
+        return lane_list(3, [(T.Blk[:], T.Pp[:], ["Blk", "Pp"])], "scn", "tL", tL, 0.0)
+
+    def closure(t):
+        names = ["EWi"] + [("ine%d" % u if ENV32 else "EW%d" % u) for u in range(t)] + (["e%d" % u for u in range(t)] if ENV32 else [])
+        act(T.Ra[:], T.EW[:, 0:M + NB * t].indirect(tL), F.Copy, ["tL"] + names, ["Ra"])
+
+    def values(t):
+        names = ["xi", "inxi"] + ["w%d" % u for u in range(t)] + ["inw%d" % u for u in range(t)]
+        win = T.XW[:, 0:M + NB * t]
+        a, b = 16 * LS1, 16 * LS
+        act(T.G[:, 0:b], win.indirect(T.eo[:, 0:LS]), F.Copy, ["eo"] + names, ["Gs"])
+        cp(T.G[:, b:16 * L], win.indirect(T.eo[:, LS:L]), ["eo"] + names, ["Gv"])
+        act(T.H[:, 0:a], T.G[:, 0:b].indirect(T.vo[:, 0:LS1]), F.Copy, ["Gs", "vo"], ["H1"])
+        cp(T.H[:, b:16 * L], T.G[:, b:16 * L].indirect(T.vo[:, LS:L]), ["Gv", "vo"], ["Hv"])
+        act(T.H[:, a:b], T.G[:, 0:b].indirect(T.vo[:, LS1:LS]), F.Copy, ["Gs", "vo"], ["H2"])
+        if t > 0:
+            closure(t)
+        for nm, lo, hi in (("v", LS, L), ("1", 0, LS1), ("2", LS1, LS)):
+            op("v", lambda q: q.tensor_tensor_scan(T.X[:, 16 * lo:16 * hi], T.keep[:, 0:16 * (hi - lo)], T.H[:, 16 * lo:16 * hi],
+                                                   0.0, A.mult, A.max), ["keep", "H" + nm], ["X" + nm])
+            mms("p0", T.p0[:, lo:hi], [(T.k384[:], T.ones[:, lo:hi], ["k384", "ones"])] +
+                [(T.Ib[:], T.X[:, 16 * lo + 4 * p + 3:16 * hi:16], ["Ib", "X" + nm]) for p in range(4)])
+        w = piece(T, "w%d" % t, rank) if t < S - 1 else T.wl[:]
+        ts(T.tq[:], P[0], -127.5, None, A.add, None, ["p0"], ["tq"])
+        tt(w, P[0], T.tq[:], A.subtract, ["p0", "tq"], ["w%d" % t])
+        if t < S - 1:
+            send("w%d" % t, "w%d" % t)
+        dmas("y", "so", [(T.yx[:, t * L:(t + 1) * L], w)], ["w%d" % t], [])
+        return w
+
+    picks()
+    ts(sc(15), sc(1), 4.0, -65536.0, A.is_lt, A.mult, ["c0"], ["c15"])
+    ts(sc(16), sc(1), 8.0, 8192.0, A.is_lt, A.mult, ["c0"], ["c16"])
+    ts(sc(17), sc(1), 8.0, -65536.0, A.is_lt, A.mult, ["c0"], ["c17"])
+    ts(sc(18), sc(1), 15.0, None, A.is_lt, None, ["c0"], ["c18"])
+    cp(T.vo[:], P[6], ["p6"], ["vo"])
+    ts(sc(19), sc(1), 1.0, sc(15), A.is_ge, A.mult, ["c0", "c15"], ["c19"])
+    ts(sc(20), sc(1), 4.0, sc(16), A.is_ge, A.mult, ["c0", "c16"], ["c20"])
+    ts(sc(21), sc(1), 5.0, sc(17), A.is_ge, A.mult, ["c0", "c17"], ["c21"])
+    fin = first_name("Ef")
+    ts(T.m1[:], T.dif[:], 0.0, sc(7), A.is_equal, A.mult, ["dif", "c7"], ["m1"])
+    ts(T.m2[:], T.dif[:], -1.0, sc(19), A.is_equal, A.mult, ["dif", "c19"], ["m2"])
+    ts(T.Sh[:], T.dif[:], 1.0, sc(18), A.is_equal, A.mult, ["dif", "c18"], ["Sh"])
+    tt(T.MY[:], T.m1[:], T.m2[:], A.add, ["m1", "m2"], ["MY"])
+    ts(T.I0[:], T.dif[:], 0.0, sc(13), A.is_equal, A.mult, ["dif", "c13"], ["I0"])
+    ts(T.m1[:], T.dif[:], -4.0, sc(20), A.is_equal, A.mult, ["dif", "c20"], ["m1"])
+    ts(T.m2[:], T.dif[:], -5.0, sc(21), A.is_equal, A.mult, ["dif", "c21"], ["m2"])
+    fin()
+    tt(T.MK[:], T.m1[:], T.m2[:], A.add, ["m1", "m2"], ["MK"])
+    for b in range(3):
+        act(T["In%d" % b][:], T.I0[:], F.Identity, ["I0"], ["In%d" % b], scale=float(rank * R + L * b))
+    act(T.Id[:], T.I32[:], F.Identity, ["I32"], ["Id"], scale=-8192.0)
+    act(T.Iu[:], T.I32[:], F.Identity, ["I32"], ["Iu"], scale=1344.0)
+    act(T.Ir[:], T.I32[:], F.Identity, ["I32"], ["Ir"], scale=-4416.0)
+    act(T.I3[:], T.I32[:], F.Identity, ["I32"], ["I3"], scale=-3.0)
+    ts(sc(22), sc(3), 7.0, 1.0, A.mult, A.add, ["c0"], ["c22"])
+    ts(sc(23), sc(4), 63.0, 1.0, A.mult, A.add, ["c0"], ["c23"])
+    ts(sc(24), sc(1), 4.0, None, A.is_lt, None, ["c0"], ["c24"])
+    ms(T.k8192[:], 10240.0, ["k8192"])
+    ms(T.kd[0:64, :], 7680.0, ["kd1"])
+    ms(T.kd[64:128, :], 72.0, ["kd2"])
+    ts(sc(25), sc(22), sc(23), sc(24), A.mult, A.mult, ["c22", "c23", "c24"], ["c25"])
+    ts(T.Wq[:], T.g16[:], sc(10), sc(25), A.is_equal, A.mult, ["g16", "c10", "c25"], ["Wq"])
+
+    for t in range(S):
+        w = values(t)
+        if t == 0:
+            codes()
+            record(0)
+            cp(T.EW[:, 0:M], T.EU[:, 0:M], ["ei", "inei"], ["EWi"])
+            closure(0)
+        tt(T.yes[:], w, T.zg[:], A.is_ge, ["w%d" % t, "zg"], ["yes"])
+        mms("p5", P[5], [(T.ones[:, 0:128], T.yes[:], ["ones", "yes"])])
+        tt(T.dR[:], P[1], T.Ra[:], A.subtract, ["p1", "Ra"], ["dR"])
+        ts(T.msk[:], P[5], 59.5, None, A.is_ge, None, ["p5"], ["msk"])
+        tt(T.tmp[:], T.msk[:], T.dR[:], A.mult, ["msk", "dR"], ["tmp"])
+        tt(T.Rn[:], T.tmp[:], T.Ra[:], A.add, ["tmp", "Ra"], ["Rn"])
+        act(T.Dg[:], T.Rn[:], F.Identity, ["Rn"], ["Dg"], bias=160.0 - 0.28125, scale=1.0 / 8192.0)
+        envs = [(T.k8192[:], T.ones[:], ["k8192", "ones"]), (T.I32[:], T.Rn[:], ["I32", "Rn"]), (T.Id[:], T.Dg[:], ["Id", "Dg"])]
+        if t == S - 1:
+            mms("p3", P[3], [(T.Wq[:], T.Dg[:], ["Wq", "Dg"])])
+            mms("p2", P[2], envs)
+            ts(T.qf[:], P[3], -93600.0, None, A.add, None, ["p3"], ["qf"])
+            act(T.Ef[:], P[2], F.Copy, ["p2"], ["Ef"])
+            dmas("y", "so", [(T.yc[:], T.qf[0::16, :])], ["qf"], [])
+            dmas("s", "so", [(T.ye[:], T.Ef[:])], ["Ef"], [])
+            break
+        u = t + 1
+        fin = lane_list(3, [(T.Wq[:], T.Dg[:], ["Wq", "Dg"])], "scq", "qL", qL, -93600.0)
+        mms("p2", P[2], envs)
+        act(T.ub[:], P[2], F.Identity, ["p2"], ["ub"], bias=160.0 - 0.5 + 1.0 / 384.0, scale=1.0 / L)
+        act(T.rb[:], P[2], F.Identity, ["p2"], ["rb"], bias=160.0 - 0.5 + 1.0 / 1152.0, scale=1.0 / R)
+        act(T.Ef[:], P[2], F.Copy, ["p2"], ["Ef"])
+        if not ENV32:
+            lo = M + NB * t
+            cp(T.EW[:, lo:lo + NB], T.EU[:, lo:lo + NB], ["e%d" % t, "ine%d" % t], ["EW%d" % t])
+        fin()
+        if u != 3:
+            mms("p5", P[5], [(T.Ib[:], T.ub[:], ["Ib", "ub"]), (T.I3[:], T.rb[:], ["I3", "rb"])])
+        mms("p4", P[4], [(T.kd[:], T.ones[:], ["kd1", "kd2", "ones"]), (T.Iu[:], T.ub[:], ["Iu", "ub"]), (T.Ir[:], T.rb[:], ["Ir", "rb"])])
+        picks()
+        codes()
+        if u < 3:
+            ts(T.mm[:], P[5], u - 320.5, None, A.is_lt, None, ["p5"], ["mm"])
+            tt(T.tmp[:], P[4], T.mm[:], A.mult, ["p4", "mm"], ["tmp"])
+            tt(T.Eo[:], T.tmp[:], T.Ef[:], A.add, ["tmp", "Ef"], ["Eo"])
+        elif u == 3:
+            tt(T.Eo[:], P[4], T.Ef[:], A.add, ["p4", "Ef"], ["Eo"])
+        else:
+            ts(T.mm[:], P[5], -319.5, float(M), A.is_lt, A.mult, ["p5"], ["mm"])
+            tt(T.tmp[:], P[4], T.Ef[:], A.add, ["p4", "Ef"], ["tmp"])
+            tt(T.Eo[:], T.tmp[:], T.mm[:], A.add, ["tmp", "mm"], ["Eo"])
+        fin = first_name("Eo")
+        cp(T.eo[:], T.Eo[:], ["Eo"], ["eo"])
+        cp(T.vo[:], P[6], ["p6"], ["vo"])
+        record(u)
+        fin()
+
+    for s in ("sv", "ss", "sp", "sg", "so"):
+        g.sync.wait_ge(T.sem[s], count[s])
+    g.wait_ge(T.sem.ls, count["ls"])

@@ -5,19 +5,18 @@ N, C, L, R, M, S = 8, 1536, 192, 576, 4608, 5
 NB = N * L
 W = M + (S - 1) * NB
 CORES_ALL = 128
-LS, LS1 = 112, 80
-ENV32 = True
-ROUTE = {"xi": "split0", "ei": "split1", "e": "split0", "w": "own"}
+LV, LC = 80, 160
+ROUTE = {"xi": "split0", "ei": "split1", "e": "split1", "w": "split0"}
 BIG = 262144.0
 MAGIC = 12582912.0
 
 SCRATCH = {
-    "XW": ("sbuf", [128, W], "bfloat16"), "EW": ("sbuf", [128, W], "float32"), "EU": ("sbuf", [128, W], "uint16"),
+    "XW": ("sbuf", [128, W], "bfloat16"), "EW": ("sbuf", [128, W], "float32"), "EU": ("sbuf", [128, M], "uint16"),
     "cdt": ("sbuf", [128, C], "int32"), "ztt": ("sbuf", [128, C], "bfloat16"), "kk": ("sbuf", [128, C], "int32"),
-    "cei": ("sbuf", [128, R], "int32"), "cci": ("sbuf", [128, R], "int32"), "cef": ("sbuf", [128, R], "float32"),
+    "cei": ("sbuf", [128, R], "int32"), "cci": ("sbuf", [128, R], "int32"),
     "e0i": ("sbuf", [128, L], "int32"), "c0i": ("sbuf", [128, L], "int32"),
     "G": ("sbuf", [128, 16 * L], "bfloat16"), "H": ("sbuf", [128, 16 * L], "bfloat16"), "X": ("sbuf", [128, 16 * L], "bfloat16"),
-    "keep": ("sbuf", [128, 16 * LS1], "bfloat16"),
+    "keep": ("sbuf", [128, 16 * max(LV, LC - LV)], "bfloat16"),
     "sci": ("sbuf", [128, 8], "int32"), "sc": ("sbuf", [128, 32], "float32"),
     "wl": ("sbuf", [128, L], "bfloat16"),
     "qL": ("sbuf", [128, 16], "uint16"), "tL": ("sbuf", [128, 16], "uint16"),
@@ -35,10 +34,10 @@ for _k in range(8):
     SCRATCH["p%d" % _k] = ("psum", [128, 512], "float32")
 
 PHASES = ["xi", "ei"]
-PHASES += ["w0", "e0"]
-for _t in range(1, S - 1):
-    PHASES += ["e%d" % _t, "w%d" % _t]
+for _t in range(S - 1):
+    PHASES += ["w%d" % _t, "e%d" % _t]
 SEMAPHORES = ["sv", "ss", "sp", "sg", "ls", "lx", "so", "dx", "dce", "dcc", "de", "dc", "dcd", "dz", "dk"]
+SEMAPHORES += ["f" + p for p in PHASES if p[0] == "e"]
 SEMAPHORES += ["a" + p for p in PHASES] + ["v%s_%d" % (p, k) for p in PHASES for k in range(2)]
 
 
@@ -50,7 +49,7 @@ def piece(T, ph, r):
     lo = M + NB * int(ph[1]) + L * r
     if ph[0] == "w":
         return T.XW[:, lo:lo + L]
-    return T.EW[:, lo:lo + L] if ENV32 else T.EU[:, lo:lo + L]
+    return T.EW[:, lo:lo + L]
 
 
 def routes(T, topo):
@@ -61,33 +60,34 @@ def routes(T, topo):
     via = {}
     for ch, rk in chips.items():
         near = lambda c: (topo.die(c) != topo.die(rk[0]), c)
-        own = sorted([c for c in topo.cores_of(rk[0]) if c not in cores], key=near)
+        out = [c for c in topo.cores_of(rk[0]) if c not in cores and all(topo.may_write(c, d) for d in cores)]
+        for c in rk:
+            via[("fan", cores.index(c))] = out[rk.index(c)]
+        own = sorted([c for c in topo.cores_of(rk[0]) if c not in cores and c not in out], key=near)
         rel = sorted([c for c in range(CORES_ALL) if topo.mates(topo.chip(c), ch) and c not in cores
                       and all(topo.may_write(c, d) for d in rk)], key=near)
         src = [r for r in range(N) if topo.chip(cores[r]) != ch]
         for ph in PHASES:
             mode = ROUTE[ph] if ph in ROUTE else ROUTE[ph[0]]
             for n, r in enumerate(src):
-                if mode == "direct":
-                    v = None
-                elif mode == "own":
-                    v = own[n]
-                elif mode == "fwd":
-                    v = rk[r % 2]
-                elif mode[0] == "h":
-                    order = list(chips)
-                    back = (order.index(ch) - order.index(topo.chip(cores[r]))) % len(order)
-                    v = own[2 * (back - 1) + r % 2] if back <= int(mode[1]) else None
+                if mode == "own":
+                    v = own[n if n < len(own) else len(src) - 1 - n]
                 elif mode == "split0":
                     v = own[n // 2] if r % 2 == 0 else rel[n // 2]
                 else:
-                    v = own[3 + n // 2] if r % 2 == 1 else rel[len(rel) - 1 - n // 2]
+                    v = own[len(own) - 1 - n // 2] if r % 2 == 1 else rel[len(rel) - 1 - n // 2]
                 via[(ph, r, ch)] = v
     return chips, via
 
 
 def bits(m):
     return bin(m).count("1")
+
+
+def masks(topo, core, cores):
+    sib = [c for c in cores if c != core and topo.chip(c) == topo.chip(core)][0]
+    far = [c for c in cores if topo.chip(c) != topo.chip(core)][0]
+    return topo.mask(core, far), topo.mask(core, sib) & ~topo.mask(core, far)
 
 
 def dst_id(topo, c):
@@ -99,6 +99,15 @@ def helper_program(g, core, T, topo, chips, via):
     sent = 0
     for ph in PHASES:
         for r in range(N):
+            if ph[0] == "e" and via[("fan", r)] == core:
+                g.wait_ge(T.sem["f" + ph], bits(masks(topo, T.cores[r], T.cores)[ph == "ei"]))
+                out = [via[(ph, r, ch)] for ch in chips if ch != topo.chip(core)]
+                m = topo.mask(core, out[0])
+                ap = piece(T, ph, r)
+                g.remote_dma_fused([RemoteDMATransfer(dst_ids=[dst_id(topo, d) for d in out], dma_engine_mask=m,
+                                                      remote_sem=T.sem["v%s_%d" % (ph, r % 2)], src=ap, dsts=[ap for d in out])],
+                                   local_sem=T.sem.ls)
+                sent += bits(m)
             for ch, rk in chips.items():
                 if via.get((ph, r, ch)) == core:
                     g.wait_ge(T.sem["v%s_%d" % (ph, r % 2)], bits(topo.mask(T.cores[r], core)))
@@ -180,48 +189,27 @@ def rank_program(g, core, T, topo):
     def send(ph, name):
         need("g", [name], [])
         ap = piece(T, ph, rank)
-        handed, direct = [], []
-        for ch, rk in chips.items():
-            if ch != chip:
-                v = via[(ph, rank, ch)]
-                if v is None:
-                    direct += rk
-                else:
-                    handed.append(v)
+        if ph[0] == "e":
+            out, sem = [via[("fan", rank)]], "f" + ph
+        else:
+            out, sem = [via[(ph, rank, ch)] for ch in chips if ch != chip], "v%s_%d" % (ph, rank % 2)
+        m_out = on_mask if ph == "ei" else off_mask
         ls = "lx" if ph == "xi" else "ls"
-        near = [RemoteDMATransfer(dst_ids=[dst_id(topo, sib)], dma_engine_mask=on_mask, remote_sem=T.sem["a" + ph], src=ap, dsts=[ap])]
-        count[ls] += bits(on_mask)
-        for out, sem in ((handed, "v%s_%d" % (ph, rank % 2)), (direct, "a" + ph)):
-            if out:
-                g.remote_dma_fused([RemoteDMATransfer(dst_ids=[dst_id(topo, d) for d in out], dma_engine_mask=off_mask,
-                                                      remote_sem=T.sem[sem], src=ap, dsts=[ap for d in out])] + near,
-                                   local_sem=T.sem[ls])
-                count[ls] += bits(off_mask)
-                near = []
+        both = [RemoteDMATransfer(dst_ids=[dst_id(topo, d) for d in out], dma_engine_mask=m_out, remote_sem=T.sem[sem],
+                                  src=ap, dsts=[ap for d in out]),
+                RemoteDMATransfer(dst_ids=[dst_id(topo, sib)], dma_engine_mask=on_mask, remote_sem=T.sem["a" + ph], src=ap, dsts=[ap])]
+        for call in ([both[:1], both[1:]] if ph == "ei" else [both]):
+            g.remote_dma_fused(call, local_sem=T.sem[ls])
+        count[ls] += bits(m_out) + bits(on_mask)
         if ph == "xi":
             wrote["sentx"] = [("lx", count["lx"])]
-        mine = [r for r in range(N) if via.get((ph, r, chip)) == core]
-        if mine:
-            g.wait_ge(T.sem["v%s_%d" % (ph, rank % 2)], bits(off_mask) * len(mine))
-            eng = topo.engines(core, sib)[::-1]
-            k = len(eng) // 4
-            g.remote_dma_fused([RemoteDMATransfer(dst_ids=[dst_id(topo, sib)], dma_engine_mask=sum(1 << e for e in eng[k * n:k * n + k]),
-                                                  remote_sem=T.sem["a" + ph], src=piece(T, ph, r), dsts=[piece(T, ph, r)])
-                                for n, r in enumerate(mine)], local_sem=T.sem.ls)
-            count["ls"] += k * len(mine)
 
     for ph in PHASES:
-        n, here = bits(on_mask), 0
+        n = bits(on_mask)
         for r in range(N):
             if topo.chip(cores[r]) != chip:
-                v = via[(ph, r, chip)]
-                if v == core:
-                    here += bits(off_mask)
-                elif v == sib:
-                    n += bits(topo.mask(sib, core)) // 4
-                else:
-                    n += bits(topo.mask(cores[r] if v is None else v, core))
-        wrote["in" + ph] = [("a" + ph, n)] + ([("v%s_%d" % (ph, rank % 2), here)] if here else [])
+                n += bits(topo.mask(via[(ph, r, chip)], core))
+        wrote["in" + ph] = [("a" + ph, n)]
 
     def ts(out, in0, s1, s2, o0, o1, rd, wr):
         if s2 is None:
@@ -279,8 +267,8 @@ def rank_program(g, core, T, topo):
     ts(sc(8), sc(5), sc(6), None, A.mult, None, ["c5", "c6"], ["c8"])
     ts(sc(9), sc(8), sc(7), None, A.mult, None, ["c8", "c7"], ["c9"])
     ms(T.kk[:], 0, ["kk"])
-    dmas("y", "dk", [(T.kk[j::16, :], T.ky[:] if j < 4 else T.kid[:]) for j in range(8)], ["sentx"], ["kk"])
-    dmas("y", "dz", [(T.ztt[:], T.zt[:])], [], ["ztt"])
+    dmas("y", "dk", [(T.kk[j::16, :], T.ky[:] if j < 4 else T.kid[:]) for j in range(8)], [], ["kk"])
+    dmas("y", "dz", [(T.ztt[:], T.zt[:])], ["sentx"], ["ztt"])
     ts(sc(10), sc(0), sc(1), 1.0 / 16.0, A.subtract, A.mult, ["c0"], ["c10"])
     ts(sc(11), sc(2), 3.75, sc(0), A.mult, A.add, ["c0"], ["c11"])
     ts(sc(12), sc(1), -0.75, sc(11), A.mult, A.add, ["c0", "c11"], ["c12"])
@@ -291,13 +279,14 @@ def rank_program(g, core, T, topo):
     ts(T.pen[:], T.a16[:], sc(1), -BIG, A.not_equal, A.mult, ["a16", "c0"], ["pen"])
     ts(T.cci[:], T.cci[:], sc(9), None, A.mult, None, ["cci", "c9"], ["cci"])
     ts(T.cci[:], T.cci[:], 7 * 8192, None, A.bitwise_and, None, ["cci"], ["cci"])
-    tt(T.cef[:], T.cci[:], T.cei[:], A.add, ["cci", "cei"], ["cef"])
-    cp(piece(T, "ei", rank), T.cef[:], ["cef"], ["ei"])
+    lo = rank * R
+    tt(T.EW[:, lo:lo + R], T.cci[:], T.cei[:], A.add, ["cci", "cei"], ["EWo"])
+    cp(piece(T, "ei", rank), T.EW[:, lo:lo + R], ["EWo"], ["ei"])
     send("ei", "ei")
     act(T.Ib[:], T.I32[:], F.Copy, ["I32"], ["Ib"])
     act(T.colb[:], T.col[:], F.Copy, ["col"], ["colb"])
-    act(T.base[:, 0:LS], T.col[:, 0:LS], F.Identity, ["col"], ["base1"], scale=16.0)
-    act(T.base[:, LS:L], T.col[:, 0:L - LS], F.Identity, ["col"], ["base2"], scale=16.0)
+    act(T.base[:, 0:LV], T.col[:, 0:LV], F.Identity, ["col"], ["base1"], scale=16.0)
+    act(T.base[:, LV:L], T.col[:, 0:L - LV], F.Identity, ["col"], ["base2"], scale=16.0)
     cp(T.c0f[:], T.c0i[:], ["c0i"], ["c0f"])
     ms(T.rst[:], 0.0, ["rst"])
     ms(T.rst[:, 0::16], -4.0 * BIG, ["rst"])
@@ -325,6 +314,8 @@ def rank_program(g, core, T, topo):
         cp(T.Vb[:], T.cdt[:, 0:C].indirect(qL), ["cdt", "qL"], ["Vb"])
         mms("p6", P[6], [(T.Ib[:], T.base[:], ["Ib", "base1", "base2"]), (T.Perm[:], T.Vb[:], ["Perm", "Vb"])])
         mms("p2", P[2], [(T.Bc0[:], T.Vb[:], ["Bc0", "Vb"])])
+
+    def place0():
         act(T.oha[:], P[2], F.Abs, ["p2", "c14"], ["oha"], bias=sc(14))
         act(T.oh[:], T.oha[:], F.Relu, ["oha"], ["oh"], bias=1.0, scale=-1.0)
 
@@ -332,16 +323,14 @@ def rank_program(g, core, T, topo):
         ts(T.Ff[:], T.kk[:, 0:C].indirect(qL), sc(8), -0.499, A.mult, A.add, ["kk", "qL", "c8"], ["Ff"])
         act(T.Fg[:], T.Ff[:], F.Identity, ["Ff"], ["Fg"], bias=MAGIC)
         act(T.Fh[:], T.Fg[:], F.Identity, ["Fg"], ["Fh"], bias=-MAGIC)
-        act(T.zg[:], T.ztt[:, 0:C].indirect(qL), F.Copy, ["ztt", "qL"], ["zg"])
 
     def record(t):
         if t < S - 1:
             mms("p7", P[7], [(T.I32[:], T.Ef[:], ["I32", "Ef"]), (T.MY[:], T.Fh[:], ["MY", "Fh"])])
-            if ENV32:
-                act(piece(T, "e%d" % t, rank), P[7], F.Copy, ["p7"], ["e%d" % t])
-            else:
-                cp(piece(T, "e%d" % t, rank), P[7], ["p7"], ["e%d" % t])
+            act(piece(T, "e%d" % t, rank), P[7], F.Copy, ["p7"], ["e%d" % t])
             send("e%d" % t, "e%d" % t)
+
+    def bound(t):
         b = "In%d" % (t % 3)
         mms("p1", P[1], [(T.I0[:], T.colb[:], ["I0", "colb"]), (T[b][:], T.ones[:], [b, "ones"]),
                          (T.Sh[:], T.Ef[:], ["Sh", "Ef"]), (T.MK[:], T.Fh[:], ["MK", "Fh"])])
@@ -351,34 +340,52 @@ def rank_program(g, core, T, topo):
         return lane_list(3, [(T.Blk[:], T.Pp[:], ["Blk", "Pp"])], "scn", "tL", tL, 0.0)
 
     def closure(t):
-        names = ["EWi"] + [("ine%d" % u if ENV32 else "EW%d" % u) for u in range(t)] + (["e%d" % u for u in range(t)] if ENV32 else [])
+        names = ["EWo", "EWa", "EWb"] + ["ine%d" % u for u in range(t)] + ["e%d" % u for u in range(t)]
         act(T.Ra[:], T.EW[:, 0:M + NB * t].indirect(tL), F.Copy, ["tL"] + names, ["Ra"])
 
     def values(t):
         names = ["xi", "inxi"] + ["w%d" % u for u in range(t)] + ["inw%d" % u for u in range(t)]
         win = T.XW[:, 0:M + NB * t]
-        a, b = 16 * LS1, 16 * LS
-        act(T.G[:, 0:b], win.indirect(T.eo[:, 0:LS]), F.Copy, ["eo"] + names, ["Gs"])
-        cp(T.G[:, b:16 * L], win.indirect(T.eo[:, LS:L]), ["eo"] + names, ["Gv"])
-        act(T.H[:, 0:a], T.G[:, 0:b].indirect(T.vo[:, 0:LS1]), F.Copy, ["Gs", "vo"], ["H1"])
-        cp(T.H[:, b:16 * L], T.G[:, b:16 * L].indirect(T.vo[:, LS:L]), ["Gv", "vo"], ["Hv"])
-        act(T.H[:, a:b], T.G[:, 0:b].indirect(T.vo[:, LS1:LS]), F.Copy, ["Gs", "vo"], ["H2"])
+        a, b, c = 16 * LV, 16 * LC, 16 * L
+        act(T.G[:, a:c], win.indirect(T.eo[:, LV:L]), F.Copy, ["eo"] + names, ["Gs"])
+        cp(T.G[:, 0:a], win.indirect(T.eo[:, 0:LV]), ["eo"] + names, ["Gv"])
+        act(T.H[:, a:b], T.G[:, a:c].indirect(T.vo[:, LV:LC]), F.Copy, ["Gs", "vo"], ["H1"])
+        cp(T.H[:, 0:a], T.G[:, 0:a].indirect(T.vo[:, 0:LV]), ["Gv", "vo"], ["Hv"])
+        act(T.H[:, b:c], T.G[:, a:c].indirect(T.vo[:, LC:L]), F.Copy, ["Gs", "vo"], ["H2"])
+        act(T.zg[:], T.ztt[:, 0:C].indirect(qL), F.Copy, ["ztt", "qL"], ["zg"])
         if t > 0:
             closure(t)
-        for nm, lo, hi in (("v", LS, L), ("1", 0, LS1), ("2", LS1, LS)):
+        c0 = M + NB * t + L * rank if t < S - 1 else 0
+        wt = T.XW if t < S - 1 else T.wl
+        w = wt[:, c0:c0 + L]
+
+        def maxima(nm, lo, hi, bank):
             op("v", lambda q: q.tensor_tensor_scan(T.X[:, 16 * lo:16 * hi], T.keep[:, 0:16 * (hi - lo)], T.H[:, 16 * lo:16 * hi],
                                                    0.0, A.mult, A.max), ["keep", "H" + nm], ["X" + nm])
-            mms("p0", T.p0[:, lo:hi], [(T.k384[:], T.ones[:, lo:hi], ["k384", "ones"])] +
+            mms(bank, T[bank][:, lo:hi], [(T.k384[:], T.ones[:, lo:hi], ["k384", "ones"])] +
                 [(T.Ib[:], T.X[:, 16 * lo + 4 * p + 3:16 * hi:16], ["Ib", "X" + nm]) for p in range(4)])
-        w = piece(T, "w%d" % t, rank) if t < S - 1 else T.wl[:]
-        ts(T.tq[:], P[0], -127.5, None, A.add, None, ["p0"], ["tq"])
-        tt(w, P[0], T.tq[:], A.subtract, ["p0", "tq"], ["w%d" % t])
+
+        def down(lo, hi, bank):
+            ts(T.tq[:, lo:hi], T[bank][:, lo:hi], -127.5, None, A.add, None, [bank], ["tq" + bank])
+
+        def rest(lo, hi, bank, name):
+            tt(wt[:, c0 + lo:c0 + hi], T[bank][:, lo:hi], T.tq[:, lo:hi], A.subtract, [bank, "tq" + bank], [name])
+
+        maxima("v", 0, LV, "p0")
+        maxima("1", LV, LC, "p0")
+        maxima("2", LC, L, "p2")
+        down(0, LC, "p0")
+        down(LC, L, "p2")
+        rest(0, LC, "p0", "wa%d" % t)
+        rest(LC, L, "p2", "w%d" % t)
+        wrote["w%d" % t] = wrote["w%d" % t] + wrote["wa%d" % t]
         if t < S - 1:
             send("w%d" % t, "w%d" % t)
         dmas("y", "so", [(T.yx[:, t * L:(t + 1) * L], w)], ["w%d" % t], [])
         return w
 
     picks()
+    place0()
     ts(sc(15), sc(1), 4.0, -65536.0, A.is_lt, A.mult, ["c0"], ["c15"])
     ts(sc(16), sc(1), 8.0, 8192.0, A.is_lt, A.mult, ["c0"], ["c16"])
     ts(sc(17), sc(1), 8.0, -65536.0, A.is_lt, A.mult, ["c0"], ["c17"])
@@ -388,6 +395,7 @@ def rank_program(g, core, T, topo):
     ts(sc(20), sc(1), 4.0, sc(16), A.is_ge, A.mult, ["c0", "c16"], ["c20"])
     ts(sc(21), sc(1), 5.0, sc(17), A.is_ge, A.mult, ["c0", "c17"], ["c21"])
     fin = first_name("Ef")
+    codes()
     ts(T.m1[:], T.dif[:], 0.0, sc(7), A.is_equal, A.mult, ["dif", "c7"], ["m1"])
     ts(T.m2[:], T.dif[:], -1.0, sc(19), A.is_equal, A.mult, ["dif", "c19"], ["m2"])
     ts(T.Sh[:], T.dif[:], 1.0, sc(18), A.is_equal, A.mult, ["dif", "c18"], ["Sh"])
@@ -399,6 +407,8 @@ def rank_program(g, core, T, topo):
     tt(T.MK[:], T.m1[:], T.m2[:], A.add, ["m1", "m2"], ["MK"])
     for b in range(3):
         act(T["In%d" % b][:], T.I0[:], F.Identity, ["I0"], ["In%d" % b], scale=float(rank * R + L * b))
+    record(0)
+    bound(0)
     act(T.Id[:], T.I32[:], F.Identity, ["I32"], ["Id"], scale=-8192.0)
     act(T.Iu[:], T.I32[:], F.Identity, ["I32"], ["Iu"], scale=1344.0)
     act(T.Ir[:], T.I32[:], F.Identity, ["I32"], ["Ir"], scale=-4416.0)
@@ -414,56 +424,56 @@ def rank_program(g, core, T, topo):
 
     for t in range(S):
         w = values(t)
-        if t == 0:
-            codes()
-            record(0)
-            cp(T.EW[:, 0:M], T.EU[:, 0:M], ["ei", "inei"], ["EWi"])
-            closure(0)
         tt(T.yes[:], w, T.zg[:], A.is_ge, ["w%d" % t, "zg"], ["yes"])
         mms("p5", P[5], [(T.ones[:, 0:128], T.yes[:], ["ones", "yes"])])
-        tt(T.dR[:], P[1], T.Ra[:], A.subtract, ["p1", "Ra"], ["dR"])
+        if t == 0:
+            if rank > 0:
+                cp(T.EW[:, 0:lo], T.EU[:, 0:lo], ["inei"], ["EWa"])
+            if rank < N - 1:
+                cp(T.EW[:, lo + R:M], T.EU[:, lo + R:M], ["inei"], ["EWb"])
+            closure(0)
+        tt(P[1], P[1], T.Ra[:], A.subtract, ["p1", "Ra"], [])
         ts(T.msk[:], P[5], 59.5, None, A.is_ge, None, ["p5"], ["msk"])
-        tt(T.tmp[:], T.msk[:], T.dR[:], A.mult, ["msk", "dR"], ["tmp"])
-        tt(T.Rn[:], T.tmp[:], T.Ra[:], A.add, ["tmp", "Ra"], ["Rn"])
+        tt(P[1], P[1], T.msk[:], A.mult, ["p1", "msk"], [])
+        tt(T.Rn[:], P[1], T.Ra[:], A.add, ["p1", "Ra"], ["Rn"])
         act(T.Dg[:], T.Rn[:], F.Identity, ["Rn"], ["Dg"], bias=160.0 - 0.28125, scale=1.0 / 8192.0)
         envs = [(T.k8192[:], T.ones[:], ["k8192", "ones"]), (T.I32[:], T.Rn[:], ["I32", "Rn"]), (T.Id[:], T.Dg[:], ["Id", "Dg"])]
         if t == S - 1:
-            mms("p3", P[3], [(T.Wq[:], T.Dg[:], ["Wq", "Dg"])])
             mms("p2", P[2], envs)
+            mms("p3", P[3], [(T.Wq[:], T.Dg[:], ["Wq", "Dg"])])
             ts(T.qf[:], P[3], -93600.0, None, A.add, None, ["p3"], ["qf"])
             act(T.Ef[:], P[2], F.Copy, ["p2"], ["Ef"])
             dmas("y", "so", [(T.yc[:], T.qf[0::16, :])], ["qf"], [])
             dmas("s", "so", [(T.ye[:], T.Ef[:])], ["Ef"], [])
             break
         u = t + 1
-        fin = lane_list(3, [(T.Wq[:], T.Dg[:], ["Wq", "Dg"])], "scq", "qL", qL, -93600.0)
         mms("p2", P[2], envs)
+        fin = lane_list(3, [(T.Wq[:], T.Dg[:], ["Wq", "Dg"])], "scq", "qL", qL, -93600.0)
         act(T.ub[:], P[2], F.Identity, ["p2"], ["ub"], bias=160.0 - 0.5 + 1.0 / 384.0, scale=1.0 / L)
         act(T.rb[:], P[2], F.Identity, ["p2"], ["rb"], bias=160.0 - 0.5 + 1.0 / 1152.0, scale=1.0 / R)
         act(T.Ef[:], P[2], F.Copy, ["p2"], ["Ef"])
-        if not ENV32:
-            lo = M + NB * t
-            cp(T.EW[:, lo:lo + NB], T.EU[:, lo:lo + NB], ["e%d" % t, "ine%d" % t], ["EW%d" % t])
         fin()
         if u != 3:
             mms("p5", P[5], [(T.Ib[:], T.ub[:], ["Ib", "ub"]), (T.I3[:], T.rb[:], ["I3", "rb"])])
         mms("p4", P[4], [(T.kd[:], T.ones[:], ["kd1", "kd2", "ones"]), (T.Iu[:], T.ub[:], ["Iu", "ub"]), (T.Ir[:], T.rb[:], ["Ir", "rb"])])
         picks()
         codes()
+        place0()
         if u < 3:
             ts(T.mm[:], P[5], u - 320.5, None, A.is_lt, None, ["p5"], ["mm"])
-            tt(T.tmp[:], P[4], T.mm[:], A.mult, ["p4", "mm"], ["tmp"])
-            tt(T.Eo[:], T.tmp[:], T.Ef[:], A.add, ["tmp", "Ef"], ["Eo"])
+            tt(P[4], P[4], T.mm[:], A.mult, ["p4", "mm"], [])
+            tt(T.Eo[:], P[4], T.Ef[:], A.add, ["p4", "Ef"], ["Eo"])
         elif u == 3:
             tt(T.Eo[:], P[4], T.Ef[:], A.add, ["p4", "Ef"], ["Eo"])
         else:
             ts(T.mm[:], P[5], -319.5, float(M), A.is_lt, A.mult, ["p5"], ["mm"])
-            tt(T.tmp[:], P[4], T.Ef[:], A.add, ["p4", "Ef"], ["tmp"])
-            tt(T.Eo[:], T.tmp[:], T.mm[:], A.add, ["tmp", "mm"], ["Eo"])
-        fin = first_name("Eo")
-        cp(T.eo[:], T.Eo[:], ["Eo"], ["eo"])
+            tt(P[4], P[4], T.Ef[:], A.add, ["p4", "Ef"], [])
+            tt(T.Eo[:], P[4], T.mm[:], A.add, ["p4", "mm"], ["Eo"])
         cp(T.vo[:], P[6], ["p6"], ["vo"])
+        cp(T.eo[:], T.Eo[:], ["Eo"], ["eo"])
         record(u)
+        fin = first_name("Eo")
+        bound(u)
         fin()
 
     for s in ("sv", "ss", "sp", "sg", "so"):

@@ -2,33 +2,52 @@ from concourse.bass import DstId, RemoteDMATransfer
 from concourse.mybir import AluOpType as A, ActivationFunctionType as F
 
 N, C, L, R, M, S = 8, 1536, 192, 576, 4608, 5
-NB = N * L
-W = M + (S - 1) * NB
 CORES_ALL = 128
-LV, LC = 80, 160
+SHARE = [(112, 72), (144, 104), (112, 72), (112, 72), (112, 72)]
 ROUTE = {"xi": "split0", "ei": "split1", "e": "split1", "w": "split0"}
 BIG = 262144.0
-MAGIC = 12582912.0
+EARLY = 1024
+START = {"v": "cci c0i i1 i2 i3 i4 i5 c0 c6 c7 c8 I32 Blk c11 cc1 cc2 own ei"}
+ORDER = {"v": "Yq Ye scq eo qL Vg oh vo Pp G1 scn H0 tL X0 X1 X2 tq xi yes msk",
+         "s": "Ef Kg zg es G0 H1 H2 Dg Ra",
+         "p": "qL E v0 vo es tL bind s0 z0 s1 z1 s2 z2 de msk dq apply",
+         "g": "sente sentg sentw senth"}
+ORDERS = [{"v": "scq qL Vg vo oh Pp scn tL wide0 G1 H0 X0 X1 X2 tq xi wide1 yes wide2 wide3 wide4 wide5 wide6 msk",
+           "s": "zg Kg es G0 H1 H2 Dg Ra",
+           "p": "qL vo v0 tL es bind s0 z0 s1 z1 s2 z2 msk de dq apply",
+           "g": "sente sentg sentw senth"},
+          dict(ORDER, v="Ye Yq eo scq qL Vg vo G1 oh H0 Pp X0 scn X1 tL X2 tq xi yes msk", s="Ef G0 zg H1 H2 Kg Dg Ra es",
+               p="E qL vo v0 bind tL s0 z0 s1 z1 s2 z2 de msk es dq apply", g="sentg sentw sente senth"),
+          ORDER, ORDER, dict(ORDER, v=ORDER["v"].replace("xi yes", "yes xi")), {"v": "Ye Yq Ef qf", "s": "", "p": "", "g": ""}]
+CYC, GAT, COL, CALL, WAKE, DMA, BYTE = 0.83e-3, 1.3, 0.42e-3, 0.05, 0.11, 1.6, 1 / 330e3
+WAY = {"xi": 8.0, "ei": 14.0, "w": 6.0, "e": 9.0, "g": 2.2}
 
 SCRATCH = {
-    "XW": ("sbuf", [128, W], "bfloat16"), "EW": ("sbuf", [128, W], "float32"), "EU": ("sbuf", [128, M], "uint16"),
-    "cdt": ("sbuf", [128, C], "int32"), "ztt": ("sbuf", [128, C], "bfloat16"), "kk": ("sbuf", [128, C], "int32"),
+    "XW": ("sbuf", [128, M], "bfloat16"), "EW": ("sbuf", [128, M], "float32"), "EU": ("sbuf", [128, M], "uint16"),
+    "ES": ("sbuf", [128, 2 * (S - 1) * L], "float32"),
+    "cdt": ("sbuf", [128, C], "int32"), "kc": ("sbuf", [128, L], "int32"), "kd4": ("sbuf", [128, 4 * L], "int32"),
+    "kb": ("sbuf", [128, 4 * L], "bfloat16"),
     "cei": ("sbuf", [128, R], "int32"), "cci": ("sbuf", [128, R], "int32"),
     "e0i": ("sbuf", [128, L], "int32"), "c0i": ("sbuf", [128, L], "int32"),
-    "G": ("sbuf", [128, 16 * L], "bfloat16"), "H": ("sbuf", [128, 16 * L], "bfloat16"), "X": ("sbuf", [128, 16 * L], "bfloat16"),
-    "keep": ("sbuf", [128, 16 * max(LV, LC - LV)], "bfloat16"),
+    "keep": ("sbuf", [128, 16 * max(max(L - a, b) for a, b in SHARE)], "bfloat16"), "base": ("sbuf", [128, S * L], "bfloat16"),
     "sci": ("sbuf", [128, 8], "int32"), "sc": ("sbuf", [128, 32], "float32"),
     "wl": ("sbuf", [128, L], "bfloat16"),
     "qL": ("sbuf", [128, 16], "uint16"), "tL": ("sbuf", [128, 16], "uint16"),
     "eo": ("sbuf", [128, L], "uint16"), "vo": ("sbuf", [128, L], "uint16"),
 }
-for _n in ("col", "a16", "rst", "Ef", "Eo", "Ra", "dR", "Rn", "tmp", "msk", "scn", "scq", "Pp", "oh", "oha", "Ff", "Fg", "Fh", "qf", "mm", "c0f"):
+for _n in ("TZ", "TK"):
+    SCRATCH[_n] = ("sbuf", [128, C], "bfloat16")
+for _n in ("G", "H", "X"):
+    SCRATCH[_n] = ("sbuf", [128, 16 * L], "bfloat16")
+for _n in ("col", "a16", "rst", "Ra", "Ye", "scn", "scq", "Ef", "qf", "Pp"):
     SCRATCH[_n] = ("sbuf", [128, L], "float32")
-for _n in ("colb", "pen", "base", "ones", "Vb", "zg", "yes", "tq", "Dg", "ub", "rb"):
+for _n in ("colb", "pen", "Vg", "zg", "Kg", "yes", "tq", "Dg", "msk", "ones"):
     SCRATCH[_n] = ("sbuf", [128, L], "bfloat16")
-for _n in ("dif", "g16", "I32", "Blk", "Sh", "MY", "MK", "m1", "m2"):
+for _n in ("Yq", "c16"):
+    SCRATCH[_n] = ("sbuf", [128, L], "float16")
+for _n in ("dif", "g16", "I32", "J32", "Sh32", "Blk"):
     SCRATCH[_n] = ("sbuf", [128, 128], "float32")
-for _n in ("Ib", "Perm", "Bc0", "Wq", "I0", "In0", "In1", "In2", "Iu", "Ir", "I3", "Id", "k384", "k8192", "kd"):
+for _n in ("Ib", "In", "Perm", "Bc0", "Wq", "Wqn", "Wk", "I0", "I4", "In0", "In1", "In2", "Id", "Ip", "k384", "kp", "kn", "kq"):
     SCRATCH[_n] = ("sbuf", [128, 128], "bfloat16")
 for _k in range(8):
     SCRATCH["p%d" % _k] = ("psum", [128, 512], "float32")
@@ -36,9 +55,10 @@ for _k in range(8):
 PHASES = ["xi", "ei"]
 for _t in range(S - 1):
     PHASES += ["w%d" % _t, "e%d" % _t]
-SEMAPHORES = ["sv", "ss", "sp", "sg", "ls", "lx", "so", "dx", "dce", "dcc", "de", "dc", "dcd", "dz", "dk"]
-SEMAPHORES += ["f" + p for p in PHASES if p[0] == "e"]
-SEMAPHORES += ["a" + p for p in PHASES] + ["v%s_%d" % (p, k) for p in PHASES for k in range(2)]
+GATE = {p: ("h" if p[0] == "e" else "g") + p[1] for p in PHASES[2:]}
+SEMAPHORES = ["sv", "ss", "sp", "sg", "ls", "lx", "so", "dx", "dce", "dcc", "de", "dc", "dcd", "dc2", "dz", "dk", "dt", "dr", "sx"]
+SEMAPHORES += ["f" + p for p in PHASES if p[0] == "e"] + sorted(set(GATE.values())) + ["aei%d" % _r for _r in range(N)]
+SEMAPHORES += ["a" + p for p in PHASES if p != "ei"] + ["v%s_%d" % (p, k) for p in PHASES for k in range(2)]
 
 
 def piece(T, ph, r):
@@ -46,10 +66,21 @@ def piece(T, ph, r):
         return T.XW[:, r * R:(r + 1) * R]
     if ph == "ei":
         return T.EU[:, r * R:(r + 1) * R]
-    lo = M + NB * int(ph[1]) + L * r
-    if ph[0] == "w":
-        return T.XW[:, lo:lo + L]
-    return T.EW[:, lo:lo + L]
+    lo = R * r + L * (int(ph[1]) % 3)
+    return (T.XW if ph[0] == "w" else T.EW)[:, lo:lo + L]
+
+
+def stage(T, ph, r, fan=False):
+    if ph[1] == "i":
+        return piece(T, ph, r)
+    t = int(ph[1])
+    if fan:
+        return T.EW[:, L * t:L * t + L]
+    return (T.G if ph[0] == "w" else T.ES)[:, L * (2 * t + r % 2):L * (2 * t + r % 2 + 1)]
+
+
+def arrival(T, ph, r):
+    return T.sem["aei%d" % r if ph == "ei" else "a" + ph]
 
 
 def routes(T, topo):
@@ -71,7 +102,7 @@ def routes(T, topo):
             mode = ROUTE[ph] if ph in ROUTE else ROUTE[ph[0]]
             for n, r in enumerate(src):
                 if mode == "own":
-                    v = own[n if n < len(own) else len(src) - 1 - n]
+                    v = (own[-1:] + out)[n // 2]
                 elif mode == "split0":
                     v = own[n // 2] if r % 2 == 0 else rel[n // 2]
                 else:
@@ -95,30 +126,88 @@ def dst_id(topo, c):
     return DstId(rid=a[0], pnc=a[1])
 
 
+def write(topo, to, mask, sem, src, dst):
+    return RemoteDMATransfer(dst_ids=[dst_id(topo, d) for d in to], dma_engine_mask=mask, remote_sem=sem, src=src, dsts=[dst for d in to])
+
+
+def writers(T, topo, chips, via, ph, core):
+    cores = list(T.cores)
+    sib = [c for c in chips[topo.chip(core)] if c != core][0]
+    return ({via[(ph, r, topo.chip(core))] for r in range(N) if topo.chip(cores[r]) != topo.chip(core)}
+            | {sib if ph[0] == "w" else via[("fan", cores.index(sib))]})
+
+
 def helper_program(g, core, T, topo, chips, via):
-    sent = 0
+    cores = list(T.cores)
+    sent, free = 0, set()
+
+    def call(transfer, mask):
+        g.remote_dma_fused([transfer], local_sem=T.sem.ls)
+        return bits(mask)
+
+    def cleared(ph):
+        if ph in GATE and GATE[ph] not in free:
+            g.wait_ge(T.sem[GATE[ph]], len([c for c in cores if core in writers(T, topo, chips, via, ph, c)]))
+            free.add(GATE[ph])
+
     for ph in PHASES:
+        mine = [r for r in range(N) if ph[0] == "e" and via[("fan", r)] == core]
+        for r in mine:
+            off, on = masks(topo, cores[r], cores)
+            g.wait_ge(T.sem["f" + ph], bits(on))
+            out = [via[(ph, r, ch)] for ch in chips if ch != topo.chip(core)]
+            sent += call(write(topo, out, off, T.sem["v%s_%d" % (ph, r % 2)], stage(T, ph, r, True), stage(T, ph, r)), off)
+            cleared(ph)
+            sent += call(write(topo, [c for c in chips[topo.chip(core)] if c != cores[r]], on, arrival(T, ph, r),
+                               stage(T, ph, r, True), piece(T, ph, r)), on)
         for r in range(N):
-            if ph[0] == "e" and via[("fan", r)] == core:
-                g.wait_ge(T.sem["f" + ph], bits(masks(topo, T.cores[r], T.cores)[ph == "ei"]))
-                out = [via[(ph, r, ch)] for ch in chips if ch != topo.chip(core)]
-                m = topo.mask(core, out[0])
-                ap = piece(T, ph, r)
-                g.remote_dma_fused([RemoteDMATransfer(dst_ids=[dst_id(topo, d) for d in out], dma_engine_mask=m,
-                                                      remote_sem=T.sem["v%s_%d" % (ph, r % 2)], src=ap, dsts=[ap for d in out])],
-                                   local_sem=T.sem.ls)
-                sent += bits(m)
             for ch, rk in chips.items():
                 if via.get((ph, r, ch)) == core:
-                    g.wait_ge(T.sem["v%s_%d" % (ph, r % 2)], bits(topo.mask(T.cores[r], core)))
+                    g.wait_ge(T.sem["v%s_%d" % (ph, r % 2)], bits(topo.mask(cores[r], core)))
+                    cleared(ph)
                     m = topo.mask(core, rk[0])
-                    ap = piece(T, ph, r)
-                    g.remote_dma_fused([RemoteDMATransfer(dst_ids=[dst_id(topo, d) for d in rk], dma_engine_mask=m,
-                                                          remote_sem=T.sem["a" + ph], src=ap, dsts=[ap for d in rk])],
-                                       local_sem=T.sem.ls)
-                    sent += bits(m)
+                    sent += call(write(topo, rk, m, arrival(T, ph, r), stage(T, ph, r), piece(T, ph, r)), m)
     if sent:
         g.wait_ge(T.sem.ls, sent)
+
+
+def lay_out(calls):
+    after = [[] for _ in calls]
+    for n, c in enumerate(calls):
+        for p, lag in c["pre"].items():
+            after[p].append((n, lag))
+    left, order = [len(c["pre"]) for c in calls], [n for n, c in enumerate(calls) if not c["pre"]]
+    for n in order:
+        for k, lag in after[n]:
+            left[k] -= 1
+            if not left[k]:
+                order.append(k)
+    assert len(order) == len(calls)
+    chain = [0.0] * len(calls)
+    for n in reversed(order):
+        chain[n] = calls[n]["busy"] + calls[n]["lat"] + max([lag + chain[k] for k, lag in after[n]] + [0.0])
+    taken = {}
+
+    def place(queue, t, d):
+        slots = taken.setdefault(queue, [])
+        k = 0
+        while k < len(slots) and slots[k][0] < t + d:
+            t = max(t, slots[k][1])
+            k += 1
+        slots.insert(k, (t, t + d))
+        return t
+
+    start, end = {}, {}
+    todo = sorted(range(len(calls)), key=lambda n: (-chain[n], n))
+    while todo:
+        n = todo.pop([all(p in end for p in calls[k]["pre"]) for k in todo].index(True))
+        c = calls[n]
+        t = max([end[p] + lag for p, lag in c["pre"].items()] + [0.0])
+        if c["bytes"]:
+            t = place("dma", t + c["busy"], c["bytes"] * BYTE) - c["busy"]
+        start[n] = place(c["q"], t, c["busy"])
+        end[n] = start[n] + c["busy"] + c["lat"] + c["bytes"] * BYTE
+    return sorted(range(len(calls)), key=lambda n: (start[n], n))
 
 
 def rank_program(g, core, T, topo):
@@ -130,352 +219,340 @@ def rank_program(g, core, T, topo):
     cores = list(T.cores)
     chip = topo.chip(core)
     sib = [c for c in chips[chip] if c != core][0]
-    far = [c for c in cores if topo.chip(c) != chip][0]
-    off_mask = topo.mask(core, far)
-    on_mask = topo.mask(core, sib) & ~off_mask
+    off_mask, on_mask = masks(topo, core, cores)
 
     Q = {"v": g.vector, "s": g.scalar, "p": g.tensor, "g": g, "y": g.sync}
-    SEM = {"v": "sv", "s": "ss", "p": "sp", "g": "sg"}
-    count = {"sv": 0, "ss": 0, "sp": 0, "sg": 0, "ls": 0, "lx": 0, "so": 0}
-    seen = {k: {} for k in Q}
-    wrote, read = {}, {}
+    calls, wrote, read, arrive, behind, tags, now = [], {}, {}, {}, [], {}, [None]
 
-    def need(e, rd, wr):
-        toks = {}
+    def follow(n, p):
+        if p not in calls[n]["pre"]:
+            calls[n]["pre"][p] = -calls[p]["lat"] - calls[p]["bytes"] * BYTE
+            calls[n]["soft"].add(p)
+
+    def note(q, fn, rd, wr, sem, inc, busy, lat=0.0, nbytes=0, tag=None):
+        pre, ext, soft = {}, [], set()
         for r in rd:
-            for s, v in wrote.get(r, []):
-                toks[s] = max(toks.get(s, 0), v)
+            if r in arrive:
+                ext.append(arrive[r][:2])
+                for p in wrote[arrive[r][3]]:
+                    if p not in pre:
+                        soft.add(p)
+                    pre[p] = max(pre.get(p, 0.0), arrive[r][2])
+            else:
+                for p in wrote[r]:
+                    pre[p] = max(pre.get(p, 0.0), WAKE)
+                    soft.discard(p)
         for r in wr:
-            for s, v in wrote.get(r, []) + read.get(r, []):
-                toks[s] = max(toks.get(s, 0), v)
-        for s, v in toks.items():
-            if seen[e].get(s, 0) < v:
-                Q[e].wait_ge(T.sem[s], v)
-                seen[e][s] = v
-
-    def done(tok, rd, wr):
+            for p in wrote.get(r, []) + read.get(r, []):
+                pre[p] = max(pre.get(p, 0.0), WAKE)
+                soft.discard(p)
+        n = len(calls)
+        tags[(now[0], q, tag or (wr[0] if wr else None))] = n
+        calls.append({"q": q, "fn": fn, "pre": pre, "soft": soft, "ext": ext, "sem": sem, "inc": inc, "busy": busy, "lat": lat, "bytes": nbytes})
+        for r in behind:
+            follow(n, wrote[r][0])
+        del behind[:]
         for r in rd:
-            read.setdefault(r, []).append(tok)
+            read.setdefault(r, []).append(n)
         for r in wr:
-            wrote[r] = [tok]
-            read[r] = []
+            wrote[r], read[r] = [n], []
 
-    def op(e, fn, rd, wr):
+    def issue():
+        count, token, seen = {}, {}, {k: {} for k in Q}
+        for q in ORDER:
+            line = [tags[(None, q, x)] for x in START.get(q, "").split()]
+            line += [tags[(t, q, x)] for t in range(S + 1) for x in ORDERS[t][q].split() if (t, q, x) in tags]
+            for p, n in zip(line, line[1:]):
+                follow(n, p)
+        for n in lay_out(calls):
+            c = calls[n]
+            for s, v in [token[p] for p in c["pre"] if p in token and p not in c["soft"]] + c["ext"]:
+                if seen[c["q"]].get(s, 0) < v:
+                    Q[c["q"]].wait_ge(T.sem[s], v)
+                    seen[c["q"]][s] = v
+            c["fn"](Q[c["q"]])
+            count[c["sem"]] = count.get(c["sem"], 0) + c["inc"]
+            if c["sem"] not in ("so", "ls"):
+                token[n] = (c["sem"], count[c["sem"]])
+        return count
+
+    def op(e, fn, rd, wr, cy):
         wr = list(wr) + [r for r in rd if r[0] == "p" and r[1:].isdigit()]
-        need(e, rd, wr)
-        count[SEM[e]] += 1
-        fn(Q[e]).then_inc(T.sem[SEM[e]], 1)
-        done((SEM[e], count[SEM[e]]), rd, wr)
+        note(e, lambda q: fn(q).then_inc(T.sem["s" + e], 1), rd, wr, "s" + e, 1, CALL + max(64, cy) * CYC)
 
-    def mms(bank, out, terms):
-        need("p", [], [bank])
-        rd = []
-        for n, (a, b, names) in enumerate(terms):
-            need("p", names, [])
-            rd += names
-            ins = g.tensor.matmul(out, a, b, n == 0, n == len(terms) - 1)
-        count["sp"] += 1
-        ins.then_inc(T.sem.sp, 1)
-        done(("sp", count["sp"]), rd, [bank])
+    def mm(tag, b, out, terms, cy, first=True, last=True):
+        def fn(q):
+            for n, (x, y, names) in enumerate(terms):
+                ins = q.matmul(out, x, y, first and n == 0, last and n == len(terms) - 1)
+            ins.then_inc(T.sem.sp, 1)
+        note("p", fn, [r for x, y, names in terms for r in names], [b], "sp", 1, cy * COL, 0.1, tag=tag)
 
-    def dmas(e, sem, pairs, rd, wr):
-        need(e, rd, wr)
-        for o, i in pairs:
-            Q[e].dma_start(o, i).then_inc(T.sem[sem], 16)
-            count[sem] = count.get(sem, 0) + 16
-        if sem != "so":
-            done((sem, count[sem]), rd, wr)
+    def dmas(e, sem, pairs, rd, wr, nbytes):
+        def fn(q):
+            for o, i in pairs:
+                q.dma_start(o, i).then_inc(T.sem[sem], 16)
+        note(e, fn, rd, wr, sem, 16 * len(pairs), 0.06 * len(pairs), DMA, nbytes)
 
-    def send(ph, name):
-        need("g", [name], [])
-        ap = piece(T, ph, rank)
+    def remote(transfers, rd, wr, engines, nbytes, ls="ls", more=0.0):
+        note("g", lambda q: q.remote_dma_fused(transfers, local_sem=T.sem[ls]), rd, wr, ls, engines, 0.35 + more, 0.8, nbytes, wr[0][:5])
+
+    def send(ph, src, rd):
         if ph[0] == "e":
-            out, sem = [via[("fan", rank)]], "f" + ph
-        else:
-            out, sem = [via[(ph, rank, ch)] for ch in chips if ch != chip], "v%s_%d" % (ph, rank % 2)
-        m_out = on_mask if ph == "ei" else off_mask
-        ls = "lx" if ph == "xi" else "ls"
-        both = [RemoteDMATransfer(dst_ids=[dst_id(topo, d) for d in out], dma_engine_mask=m_out, remote_sem=T.sem[sem],
-                                  src=ap, dsts=[ap for d in out]),
-                RemoteDMATransfer(dst_ids=[dst_id(topo, sib)], dma_engine_mask=on_mask, remote_sem=T.sem["a" + ph], src=ap, dsts=[ap])]
-        for call in ([both[:1], both[1:]] if ph == "ei" else [both]):
-            g.remote_dma_fused(call, local_sem=T.sem[ls])
-        count[ls] += bits(m_out) + bits(on_mask)
+            remote([write(topo, [via[("fan", rank)]], on_mask, T.sem["f" + ph], src, stage(T, ph, rank, True))], rd, ["sent" + ph],
+                   bits(on_mask), 256 * R * 2)
+            return
+        out = write(topo, [via[(ph, rank, ch)] for ch in chips if ch != chip], off_mask, T.sem["v%s_%d" % (ph, rank % 2)], src, stage(T, ph, rank))
+        near = write(topo, [sib], on_mask, T.sem["a" + ph], src, src)
         if ph == "xi":
-            wrote["sentx"] = [("lx", count["lx"])]
+            remote([out, near], rd, ["sentxi"], bits(off_mask) + bits(on_mask), 256 * R * 6, "lx", 2.0)
+        else:
+            remote([out, near], rd + ["ing" + ph[1]], ["sent" + ph], bits(off_mask) + bits(on_mask), 256 * L * 6)
+
+    def clear(ph, rd):
+        to = sorted(writers(T, topo, chips, via, ph, core), key=lambda d: (topo.chip(d) == chip, d))
+        engines = topo.engines(core, sib)
+        away = len([d for d in to if topo.chip(d) != chip])
+        pick = engines[:away] + engines[len(engines) - (len(to) - away):]
+        remote([RemoteDMATransfer(dst_ids=[dst_id(topo, d)], dma_engine_mask=1 << e, remote_sem=T.sem[GATE[ph]]) for d, e in zip(to, pick)],
+               rd, ["sent" + GATE[ph]], len(to), 0)
 
     for ph in PHASES:
-        n = bits(on_mask)
-        for r in range(N):
-            if topo.chip(cores[r]) != chip:
-                n += bits(topo.mask(via[(ph, r, chip)], core))
-        wrote["in" + ph] = [("a" + ph, n)]
+        each = {r: bits(on_mask if cores[r] == sib else topo.mask(via[(ph, r, chip)], core)) for r in range(N) if r != rank}
+        if ph == "ei":
+            for r, n in each.items():
+                arrive["inei%d" % r] = ("aei%d" % r, n, WAY[ph] / (2 if cores[r] == sib else 1), "sentei")
+        else:
+            arrive["in" + ph] = ("a" + ph, sum(each.values()), WAY[ph if ph in WAY else ph[0]] - 0.8, "sent" + ph)
+    for t in range(S - 1):
+        arrive["ing%d" % t] = ("g%d" % t, 1, WAY["g"] - 0.8, "sentg%d" % t)
 
-    def ts(out, in0, s1, s2, o0, o1, rd, wr):
+    def ts(out, in0, s1, s2, o0, o1, rd, wr, cy=L):
         if s2 is None:
-            op("v", lambda q: q.tensor_scalar(out, in0, s1, None, o0), rd, wr)
+            op("v", lambda q: q.tensor_scalar(out, in0, s1, None, o0), rd, wr, cy)
         else:
-            op("v", lambda q: q.tensor_scalar(out, in0, s1, s2, o0, o1), rd, wr)
+            op("v", lambda q: q.tensor_scalar(out, in0, s1, s2, o0, o1), rd, wr, cy)
 
-    def tt(out, in0, in1, o, rd, wr):
-        op("v", lambda q: q.tensor_tensor(out, in0, in1, o), rd, wr)
+    def tt(out, in0, in1, o, rd, wr, cy=L):
+        op("v", lambda q: q.tensor_tensor(out, in0, in1, o), rd, wr, cy)
 
-    def cp(out, in0, rd, wr):
-        op("v", lambda q: q.tensor_copy(out, in0), rd, wr)
+    def cp(out, in0, rd, wr, cy=L):
+        op("v", lambda q: q.tensor_copy(out, in0), rd, wr, cy)
 
-    def ms(ap, val, wr):
-        op("v", lambda q: q.memset(ap, val), [], wr)
+    def ms(ap, val, wr, cy=64):
+        op("v", lambda q: q.memset(ap, val), [], wr, cy)
 
-    def act(out, in0, fn, rd, wr, bias=0.0, scale=1.0):
-        if fn == F.Copy:
-            op("s", lambda q: q.activation(out, in0, fn), rd, wr)
+    def act(out, in0, rd, wr, cy=L, bias=None, scale=1.0):
+        if bias is None and isinstance(scale, float) and scale == 1.0:
+            op("s", lambda q: q.activation(out, in0, F.Copy), rd, wr, cy)
         else:
-            op("s", lambda q: q.activation(out, in0, fn, bias=bias, scale=scale), rd, wr)
+            op("s", lambda q: q.activation(out, in0, F.Identity, bias=0.0 if bias is None else bias, scale=scale), rd, wr, cy)
 
-    def iota(out, pat, base, cm, wr, flt=True):
+    def iota(out, pat, base, cm, wr, n, flt=True):
         if flt:
-            op("g", lambda q: q.iota(out, pat, base, cm, allow_small_or_imprecise_dtypes=True), [], wr)
+            op("g", lambda q: q.iota(out, pat, base, cm, allow_small_or_imprecise_dtypes=True), [], wr, 100 + 2 * n)
         else:
-            op("g", lambda q: q.iota(out, pat, base, cm), [], wr)
+            op("g", lambda q: q.iota(out, pat, base, cm), [], wr, 100 + 2 * n)
 
-    P = [T["p%d" % k][:, 0:L] for k in range(8)]
+    def scan(out, d0, d1, o0, rd, wr, cy):
+        op("v", lambda q: q.tensor_tensor_scan(out, d0, d1, 0.0, o0, A.max), rd, wr, cy)
+
+    copy = {"v": cp, "s": act}
     sc = lambda k: T.sc[:, k:k + 1]
     qL, tL = T.qL[:, 0:L // 16], T.tL[:, 0:L // 16]
+    PS, PZ, PV, PL, PE, P0, PR, PD = ["p%d" % k for k in range(8)]
+    P = lambda b: T[b][:, 0:L]
+    GL = GAT * L
 
-    dmas("y", "dx", [(piece(T, "xi", rank), T.x0[:])], [], ["xi"])
-    dmas("y", "dce", [(T.cei[:], T.ce0[:])], [], ["cei"])
-    iota(T.sci[:, 0:1], [[0, 1]], 0, 1, ["pi"], flt=False)
-    iota(T.dif[:], [[1, 128]], 0, -1, ["dif"])
-    iota(T.g16[:], [[1, 8], [0, 16]], 0, 0, ["g16"])
-    iota(T.a16[:], [[0, L // 16], [1, 16]], 0, 0, ["a16"])
-    iota(T.col[:], [[1, L]], 0, 0, ["col"])
-    send("xi", "xi")
-    ms(T.cci[:], 0, ["cci"])
-    ms(T.c0i[:], 0, ["c0i"])
-    dmas("y", "dcc", [(T.cci[j::16, :], T.cc0[:]) for j in range(4)], [], ["cci"])
-    dmas("s", "dc", [(T.c0i[0::16, :], T.c0[:])], [], ["c0i"])
-    dmas("s", "de", [(T.e0i[:], T.e0[:])], [], ["e0i"])
-    dmas("s", "dcd", [(T.cdt[:], T.cd[:])], [], ["cdt"])
-    ts(T.sci[:, 1:2], T.sci[:, 0:1], 15, None, A.bitwise_and, None, ["pi"], ["i1"])
-    ts(T.sci[:, 2:3], T.sci[:, 0:1], 3, None, A.bitwise_and, None, ["pi"], ["i2"])
-    ts(T.sci[:, 3:4], T.sci[:, 0:1], 1, None, A.bitwise_and, None, ["pi"], ["i3"])
-    ts(T.sci[:, 4:5], T.sci[:, 0:1], 1, 1, A.logical_shift_right, A.bitwise_and, ["pi"], ["i4"])
-    cp(T.sc[:, 0:5], T.sci[:, 0:5], ["pi", "i1", "i2", "i3", "i4"], ["c0"])
-    ts(sc(5), sc(3), -0.875, 1.0, A.mult, A.add, ["c0"], ["c5"])
-    ts(sc(6), sc(4), -63.0 / 64.0, 1.0, A.mult, A.add, ["c0"], ["c6"])
-    ts(sc(7), sc(1), 4.0, 8192.0, A.is_lt, A.mult, ["c0"], ["c7"])
-    ts(sc(8), sc(5), sc(6), None, A.mult, None, ["c5", "c6"], ["c8"])
-    ts(sc(9), sc(8), sc(7), None, A.mult, None, ["c8", "c7"], ["c9"])
-    ms(T.kk[:], 0, ["kk"])
-    dmas("y", "dk", [(T.kk[j::16, :], T.ky[:] if j < 4 else T.kid[:]) for j in range(8)], [], ["kk"])
-    dmas("y", "dz", [(T.ztt[:], T.zt[:])], ["sentx"], ["ztt"])
-    ts(sc(10), sc(0), sc(1), 1.0 / 16.0, A.subtract, A.mult, ["c0"], ["c10"])
-    ts(sc(11), sc(2), 3.75, sc(0), A.mult, A.add, ["c0"], ["c11"])
-    ts(sc(12), sc(1), -0.75, sc(11), A.mult, A.add, ["c0", "c11"], ["c12"])
-    ts(sc(13), sc(1), 0.0, None, A.is_equal, None, ["c0"], ["c13"])
-    ts(sc(14), sc(1), -1.0, None, A.mult, None, ["c0"], ["c14"])
-    ts(T.I32[:], T.dif[:], 0.0, None, A.is_equal, None, ["dif"], ["I32"])
-    ts(T.Blk[:], T.g16[:], sc(10), None, A.is_equal, None, ["g16", "c10"], ["Blk"])
+    dmas("y", "dx", [(piece(T, "xi", rank), T.x0[:])], [], ["xi"], 256 * R)
+    dmas("y", "dce", [(T.cei[:], T.ce0[:])], [], ["cei"], 512 * R)
+    ms(T.cci[:], 0, ["cci"], R)
+    ms(T.c0i[:], 0, ["c0i"], L)
+    dmas("y", "dcc", [(T.cci[j::16, :], T.cc0[:]) for j in range(4)], [], ["cci"], 128 * R)
+    dmas("s", "de", [(T.e0i[:], T.e0[:])], [], ["e0i"], 512 * L)
+    send("xi", piece(T, "xi", rank), ["xi"])
+    loads = [("dc", [(T.c0i[0::16, :], T.c0[:])], [], "c0i", 32 * L),
+             ("dk", [(T.kc[:, 0:L // 2], T.ky[:]), (T.kc[:, L // 2:L], T.kid[:])], [], "kc", 64 * C),
+             ("dcd", [(T.cdt[:, 0:EARLY], T.cd[:, 0:EARLY])], [], "cd1", 512 * EARLY),
+             ("dc2", [(T.cdt[:, EARLY:C], T.cd[:, EARLY:C])], ["sentxi"], "cd2", 512 * (C - EARLY)),
+             ("dz", [(T.TZ[:], T.zt[:])], [], "TZ", 256 * C)]
+    for n, (sem, pairs, rd, name, nbytes) in enumerate(loads):
+        behind.append(loads[n - 1][3] if n else "cci")
+        dmas("y", sem, pairs, rd, [name], nbytes)
+    wrote["cdt"] = wrote["cd1"] + wrote["cd2"]
+    iota(T.sci[:, 0:1], [[0, 1]], 0, 1, ["pi"], 1, flt=False)
+    iota(T.dif[:], [[1, 128]], 0, -1, ["dif"], 128)
+    iota(T.g16[:], [[1, 8], [0, 16]], 0, 0, ["g16"], 128)
+    iota(T.a16[:], [[0, L // 16], [1, 16]], 0, 0, ["a16"], L)
+    iota(T.col[:], [[1, L]], 0, 0, ["col"], L)
+    ts(T.sci[:, 1:2], T.sci[:, 0:1], 15, None, A.bitwise_and, None, ["pi"], ["i1"], 1)
+    ts(T.sci[:, 2:3], T.sci[:, 0:1], 3, None, A.bitwise_and, None, ["pi"], ["i2"], 1)
+    ts(T.sci[:, 3:4], T.sci[:, 0:1], 1, None, A.bitwise_and, None, ["pi"], ["i3"], 1)
+    ts(T.sci[:, 4:5], T.sci[:, 0:1], 1, 1, A.logical_shift_right, A.bitwise_and, ["pi"], ["i4"], 1)
+    ts(T.sci[:, 5:6], T.sci[:, 0:1], 4, None, A.logical_shift_right, None, ["pi"], ["i5"], 1)
+    cp(T.sc[:, 0:6], T.sci[:, 0:6], ["pi", "i1", "i2", "i3", "i4", "i5"], ["c0"], 1)
+    small = [(6, 3, -0.875, 1.0, A.mult, A.add), (7, 4, -63.0 / 64.0, 1.0, A.mult, A.add),
+             (8, 6, sc(7), 8192.0, A.mult, A.mult),
+             (9, 2, 3.75, sc(0), A.mult, A.add), (10, 1, -0.75, sc(9), A.mult, A.add),
+             (11, 1, 0.0, None, A.is_equal, None), (12, 1, 15.0, None, A.is_lt, None), (13, 1, 4.0, None, A.is_lt, None),
+             (14, 3, 7.0, 1.0, A.mult, A.add), (15, 4, 63.0, 1.0, A.mult, A.add),
+             (16, 14, sc(15), sc(13), A.mult, A.mult),
+             (17, 1, 8.0, sc(13), A.is_lt, A.subtract), (18, 14, sc(15), sc(17), A.mult, A.mult)]
+    uses = {8: [7], 10: [9], 16: [15, 13], 17: [13], 18: [15, 17]}
+    for k, src, s1, s2, o0, o1 in small:
+        ts(sc(k), sc(src), s1, s2, o0, o1, ["c0"] + ["c%d" % j for j in [src] + uses.get(k, []) if j > 5], ["c%d" % k], 1)
+    ts(T.I32[:], T.dif[:], 0.0, None, A.is_equal, None, ["dif"], ["I32"], 128)
+    for name, scale in (("Ib", 1.0), ("In", -1.0), ("Id", -8192.0), ("Ip", 8192.0), ("J32", -1.0)):
+        act(T[name][:], T.I32[:], ["I32"], [name], 128, scale=scale)
     ts(T.pen[:], T.a16[:], sc(1), -BIG, A.not_equal, A.mult, ["a16", "c0"], ["pen"])
-    ts(T.cci[:], T.cci[:], sc(9), None, A.mult, None, ["cci", "c9"], ["cci"])
-    ts(T.cci[:], T.cci[:], 7 * 8192, None, A.bitwise_and, None, ["cci"], ["cci"])
-    lo = rank * R
-    tt(T.EW[:, lo:lo + R], T.cci[:], T.cei[:], A.add, ["cci", "cei"], ["EWo"])
-    cp(piece(T, "ei", rank), T.EW[:, lo:lo + R], ["EWo"], ["ei"])
-    send("ei", "ei")
-    act(T.Ib[:], T.I32[:], F.Copy, ["I32"], ["Ib"])
-    act(T.colb[:], T.col[:], F.Copy, ["col"], ["colb"])
-    act(T.base[:, 0:LV], T.col[:, 0:LV], F.Identity, ["col"], ["base1"], scale=16.0)
-    act(T.base[:, LV:L], T.col[:, 0:L - LV], F.Identity, ["col"], ["base2"], scale=16.0)
-    cp(T.c0f[:], T.c0i[:], ["c0i"], ["c0f"])
-    ms(T.rst[:], 0.0, ["rst"])
-    ms(T.rst[:, 0::16], -4.0 * BIG, ["rst"])
-
-    def lane_list(bank, terms, scn, name, out, shift):
-        mms("p%d" % bank, P[bank], [(T.Ib[:], T.pen[:], ["Ib", "pen"])] + terms)
-
-        def rest():
-            op("v", lambda q: q.tensor_tensor_scan(T[scn][:], T.rst[:], P[bank], 0.0, A.add, A.max), ["rst", "p%d" % bank], [scn])
-            ts(out, T[scn][:, 15::16], shift, None, A.add, None, [scn], [name])
-        return rest
-
-    fin = lane_list(3, [(T.Blk[:], T.c0f[:], ["Blk", "c0f"])], "scq", "qL", qL, 0.0)
-    ts(T.Perm[:], T.col[:, 0:128], sc(12), None, A.is_equal, None, ["col", "c12"], ["Perm"])
-    ts(T.Bc0[:], T.g16[:], sc(10), sc(13), A.is_equal, A.mult, ["g16", "c10", "c13"], ["Bc0"])
-    cp(T.Ef[:], T.e0i[:], ["e0i"], ["Ef"])
-    cp(T.eo[:], T.e0i[:], ["e0i"], ["eo"])
-    fin()
-    ms(T.keep[:], 1.0, ["keep"])
-    ms(T.keep[:, 0::4], 0.0, ["keep"])
-    ms(T.ones[:], 1.0, ["ones"])
+    act(T.colb[:], T.col[:], ["col"], ["colb"])
+    cuts = sorted({a for a, b in SHARE})
+    for n, a in enumerate(cuts):
+        act(T.base[:, n * L:n * L + a], T.col[:, 0:a], ["col"], ["bs%d" % n], a, scale=16.0)
+        act(T.base[:, n * L + a:(n + 1) * L], T.col[:, 0:L - a], ["col"], ["bv%d" % n], L - a, scale=16.0)
+    ts(T.Perm[:], T.col[:, 0:128], sc(10), None, A.is_equal, None, ["col", "c10"], ["Perm"], 128)
+    ts(T.Blk[:], T.g16[:], sc(5), None, A.is_equal, None, ["g16", "c0"], ["Blk"], 128)
+    for name, k in (("Bc0", 11), ("Wq", 16), ("Wk", 18)):
+        act(T[name][:], T.Blk[:], ["Blk", "c%d" % k], [name], 128, scale=sc(k))
+    act(T.Wqn[:], T.Wq[:], ["Wq"], ["Wqn"], 128, scale=-1.0)
+    ts(T.Sh32[:], T.dif[:], 1.0, sc(12), A.is_equal, A.mult, ["dif", "c12"], ["Sh32"], 128)
+    act(T.I0[:], T.I32[:], ["I32", "c11"], ["I0"], 128, scale=sc(11))
+    act(T.I4[:], T.Ip[:], ["Ip", "c13"], ["I4"], 128, scale=sc(13))
+    for b in range(3):
+        act(T["In%d" % b][:], T.I0[:], ["I0"], ["In%d" % b], 128, scale=float(rank * R + L * b))
+    ms(T.ones[:], 1.0, ["ones"], L // 2)
+    ms(T.rst[:], 0.0, ["rst"], L)
+    ms(T.rst[:, 0::16], -4.0 * BIG, ["rst2", "rst"])
+    ms(T.keep[:], 1.0, ["keep"], 4 * L)
+    ms(T.keep[:, 0::4], 0.0, ["keep2", "keep"], L)
     ms(T.k384[:], 384.0, ["k384"])
+    ms(T.kp[:], 10240.0, ["kp"])
+    ms(T.kn[:], -10240.0, ["kn"])
+    ms(T.kq[0:64, :], 1456.0, ["kq1"])
+    ms(T.kq[64:128, :], 6.5, ["kq2"])
+    ts(T.cci[:], T.cci[:], sc(8), None, A.mult, None, ["cci", "c8"], ["cc1", "cci"], R)
+    ts(T.cci[:], T.cci[:], 7 * 8192, None, A.bitwise_and, None, ["cci"], ["cc2", "cci"], R)
+    lo = rank * R
+    tt(T.EW[:, lo:lo + R], T.cci[:], T.cei[:], A.add, ["cci", "cei"], ["own", "EW%d" % rank], 2 * R)
+    cp(piece(T, "ei", rank), T.EW[:, lo:lo + R], ["EW%d" % rank], ["ei"], R)
+    behind.append("sentxi")
+    send("ei", piece(T, "ei", rank), ["ei"])
+    for j in range(4):
+        ts(T.kd4[:, j * L:(j + 1) * L], T.kc[:], 3 * j, 7, A.logical_shift_right, A.bitwise_and, ["kc"], ["kd%d" % j])
+    cp(T.kb[:], T.kd4[:], ["kd%d" % j for j in range(4)], ["kb"], 4 * L)
+    ms(T.TK[:], 0.0, ["TK"], C // 2)
+    behind.append("TZ")
+    dmas("y", "dt", [(T.TK[4 * k + j::16, :], T.kb[:, j * L + k * L // 2:j * L + (k + 1) * L // 2]) for j in range(4) for k in range(2)],
+         ["kb"], ["TK"], 128 * 4 * L * 6)
 
-    def picks():
-        cp(T.Vb[:], T.cdt[:, 0:C].indirect(qL), ["cdt", "qL"], ["Vb"])
-        mms("p6", P[6], [(T.Ib[:], T.base[:], ["Ib", "base1", "base2"]), (T.Perm[:], T.Vb[:], ["Perm", "Vb"])])
-        mms("p2", P[2], [(T.Bc0[:], T.Vb[:], ["Bc0", "Vb"])])
+    def widen():
+        way = lambda r: (cores[r] != sib, cores[r] != sib and topo.chip(via[("ei", r, chip)]) != chip, r)
+        for n, r in enumerate(sorted([r for r in range(N) if r != rank], key=way)):
+            cp(T.EW[:, r * R:(r + 1) * R], piece(T, "ei", r), ["inei%d" % r], ["wide%d" % n, "EW%d" % r], R)
 
-    def place0():
-        act(T.oha[:], P[2], F.Abs, ["p2", "c14"], ["oha"], bias=sc(14))
-        act(T.oh[:], T.oha[:], F.Relu, ["oha"], ["oh"], bias=1.0, scale=-1.0)
+    def lane_list(terms, buf, out, name, shift, cy):
+        mm(name, PL, P(PL), [(T.Ib[:], T.pen[:], ["Ib", "pen"])] + terms, cy)
+        scan(T[buf][:], T.rst[:], P(PL), A.add, ["rst", PL], [buf], L)
+        ts(out, T[buf][:, 15::16], shift, None, A.add, None, [buf], [name], 1)
 
-    def codes():
-        ts(T.Ff[:], T.kk[:, 0:C].indirect(qL), sc(8), -0.499, A.mult, A.add, ["kk", "qL", "c8"], ["Ff"])
-        act(T.Fg[:], T.Ff[:], F.Identity, ["Ff"], ["Fg"], bias=MAGIC)
-        act(T.Fh[:], T.Fg[:], F.Identity, ["Fg"], ["Fh"], bias=-MAGIC)
+    def environments():
+        tt(T.Ye[:], T[PD][:, 0:L], T.msk[:], A.mult, [PD, "msk"], ["Ye"])
+        if now[0] == S:
+            tt(T.Ef[:], P(PE), T.Ye[:], A.add, [PE, "Ye"], ["Ef"])
+            return
+        mm("E", PE, P(PE), [(T.I32[:], T.Ye[:], ["I32", "Ye"])], 4 * L, first=False)
+        cp(T.eo[:], P(PE), [PE], ["eo"])
+        act(T.Ef[:], P(PE), [PE], ["Ef"])
 
-    def record(t):
+    def lists(t):
+        cp(T.Vg[:], T.cdt[:, 0:C].indirect(qL), ["cdt", "qL"], ["Vg"], GL)
+        n = cuts.index(SHARE[t][0])
+        mm("vo", PV, P(PV), [(T.Ib[:], T.base[:, n * L:(n + 1) * L], ["Ib", "bs%d" % n, "bv%d" % n]), (T.Perm[:], T.Vg[:], ["Perm", "Vg"])], 2 * L)
+        cp(T.vo[:], P(PV), [PV], ["vo"])
+        mm("v0", P0, P(P0), [(T.Bc0[:], T.Vg[:], ["Bc0", "Vg"])], L)
+        ts(P(P0), P(P0), sc(1), None, A.is_equal, None, [P0, "c0"], ["oh"])
+        tt(T.Pp[:], P(P0), T.Ef[:], A.mult, [P0, "Ef"], ["Pp"])
+        lane_list([(T.Blk[:], T.Pp[:], ["Blk", "Pp"])], "scn", tL, "tL", 0.0, 5 * L)
+        act(T.zg[:], T.TZ[:, 0:C].indirect(qL), ["TZ", "qL"], ["zg"], GL)
+        act(T.Kg[:], T.TK[:, 0:C].indirect(qL), ["TK", "qL"], ["Kg"], GL)
         if t < S - 1:
-            mms("p7", P[7], [(T.I32[:], T.Ef[:], ["I32", "Ef"]), (T.MY[:], T.Fh[:], ["MY", "Fh"])])
-            act(piece(T, "e%d" % t, rank), P[7], F.Copy, ["p7"], ["e%d" % t])
-            send("e%d" % t, "e%d" % t)
-
-    def bound(t):
+            es = T.ES[:, t * L:(t + 1) * L]
+            mm("es", PR, P(PR), [(T.I32[:], T.Ef[:], ["I32", "Ef"]), (T.I4[:], T.Kg[:], ["I4", "Kg"])], 5 * L)
+            act(es, P(PR), [PR], ["es", "es%d" % t])
+            send("e%d" % t, es, ["es%d" % t])
         b = "In%d" % (t % 3)
-        mms("p1", P[1], [(T.I0[:], T.colb[:], ["I0", "colb"]), (T[b][:], T.ones[:], [b, "ones"]),
-                         (T.Sh[:], T.Ef[:], ["Sh", "Ef"]), (T.MK[:], T.Fh[:], ["MK", "Fh"])])
-
-    def first_name(eoff):
-        tt(T.Pp[:], T.oh[:], T[eoff][:], A.mult, ["oh", eoff], ["Pp"])
-        return lane_list(3, [(T.Blk[:], T.Pp[:], ["Blk", "Pp"])], "scn", "tL", tL, 0.0)
+        mm("bind", PD, T[PD][:, 0:L], [(T.kn[:], T.ones[:], ["kn", "ones"]), (T.I0[:], T.colb[:], ["I0", "colb"]), (T[b][:], T.ones[:], [b]),
+                                       (T.Sh32[:], T.Ef[:], ["Sh32", "Ef"])], 7 * L, last=False)
 
     def closure(t):
-        names = ["EWo", "EWa", "EWb"] + ["ine%d" % u for u in range(t)] + ["e%d" % u for u in range(t)]
-        act(T.Ra[:], T.EW[:, 0:M + NB * t].indirect(tL), F.Copy, ["tL"] + names, ["Ra"])
+        win = T.EW[:, 0:M].indirect(tL)
+        rd = ["tL"] + ["EW%d" % r for r in range(N)] + ["ine%d" % u for u in range(t)]
+        act(T.Dg[:], win, rd, ["Dg"], GL, bias=160.0 - 0.28125, scale=1.0 / 8192.0)
+        act(T.Ra[:], win, rd, ["Ra"], GL)
+        if t < S - 1:
+            clear("e%d" % t, ["Dg", "Ra"])
+            dmas("y", "dr", [(piece(T, "e%d" % t, rank), T.ES[:, t * L:(t + 1) * L])], ["es%d" % t], ["EW%d" % rank], 512 * L)
+        mm("dq", PR, P(PR), [(T.kq[:], T.ones[:], ["kq1", "kq2", "ones"]), (T.Wk[:], T.Kg[:], ["Wk", "Kg"]),
+                             (T.Wqn[:], T.Dg[:], ["Wqn", "Dg"])], 3 * L)
+        mm("de", PD, T[PD][:, 0:L], [(T.Ip[:], T.Dg[:], ["Ip", "Dg"]), (T.J32[:], T.Ra[:], ["J32", "Ra"])], 5 * L, first=False)
+        mm("apply", PE, P(PE), [(T.kp[:], T.ones[:], ["kp", "ones"]), (T.Id[:], T.Dg[:], ["Id", "Dg"]), (T.I32[:], T.Ra[:], ["I32", "Ra"])],
+           6 * L, last=t == S - 1)
 
     def values(t):
-        names = ["xi", "inxi"] + ["w%d" % u for u in range(t)] + ["inw%d" % u for u in range(t)]
-        win = T.XW[:, 0:M + NB * t]
-        a, b, c = 16 * LV, 16 * LC, 16 * L
-        act(T.G[:, a:c], win.indirect(T.eo[:, LV:L]), F.Copy, ["eo"] + names, ["Gs"])
-        cp(T.G[:, 0:a], win.indirect(T.eo[:, 0:LV]), ["eo"] + names, ["Gv"])
-        act(T.H[:, a:b], T.G[:, a:c].indirect(T.vo[:, LV:LC]), F.Copy, ["Gs", "vo"], ["H1"])
-        cp(T.H[:, 0:a], T.G[:, 0:a].indirect(T.vo[:, 0:LV]), ["Gv", "vo"], ["Hv"])
-        act(T.H[:, b:c], T.G[:, a:c].indirect(T.vo[:, LC:L]), F.Copy, ["Gs", "vo"], ["H2"])
-        act(T.zg[:], T.ztt[:, 0:C].indirect(qL), F.Copy, ["ztt", "qL"], ["zg"])
-        if t > 0:
-            closure(t)
-        c0 = M + NB * t + L * rank if t < S - 1 else 0
-        wt = T.XW if t < S - 1 else T.wl
-        w = wt[:, c0:c0 + L]
-
-        def maxima(nm, lo, hi, bank):
-            op("v", lambda q: q.tensor_tensor_scan(T.X[:, 16 * lo:16 * hi], T.keep[:, 0:16 * (hi - lo)], T.H[:, 16 * lo:16 * hi],
-                                                   0.0, A.mult, A.max), ["keep", "H" + nm], ["X" + nm])
-            mms(bank, T[bank][:, lo:hi], [(T.k384[:], T.ones[:, lo:hi], ["k384", "ones"])] +
-                [(T.Ib[:], T.X[:, 16 * lo + 4 * p + 3:16 * hi:16], ["Ib", "X" + nm]) for p in range(4)])
-
-        def down(lo, hi, bank):
-            ts(T.tq[:, lo:hi], T[bank][:, lo:hi], -127.5, None, A.add, None, [bank], ["tq" + bank])
-
-        def rest(lo, hi, bank, name):
-            tt(wt[:, c0 + lo:c0 + hi], T[bank][:, lo:hi], T.tq[:, lo:hi], A.subtract, [bank, "tq" + bank], [name])
-
-        maxima("v", 0, LV, "p0")
-        maxima("1", LV, LC, "p0")
-        maxima("2", LC, L, "p2")
-        down(0, LC, "p0")
-        down(LC, L, "p2")
-        rest(0, LC, "p0", "wa%d" % t)
-        rest(LC, L, "p2", "w%d" % t)
-        wrote["w%d" % t] = wrote["w%d" % t] + wrote["wa%d" % t]
+        rd = ["xi", "inxi", "eo"] + ["inw%d" % u for u in range(t)]
+        for names in (["G0", "G1"], ["H0", "H1", "H2"], ["X0", "X1", "X2"]):
+            users = [p for r in names for p in wrote.get(r, []) + read.get(r, [])]
+            for r in names:
+                wrote[r], read[r] = [], list(users)
+        cut, sub = SHARE[t]
+        firsts = [("s", 0, cut), ("v", cut, L)]
+        for n, (e, a, b) in enumerate(firsts):
+            copy[e](T.G[:, 16 * a:16 * b], T.XW[:, 0:M].indirect(T.eo[:, a:b]), rd, ["G%d" % n], 16 * GAT * (b - a))
         if t < S - 1:
-            send("w%d" % t, "w%d" % t)
-        dmas("y", "so", [(T.yx[:, t * L:(t + 1) * L], w)], ["w%d" % t], [])
-        return w
+            clear("w%d" % t, ["G0", "G1"])
+        for n, (e, a, b, k) in enumerate([("v", cut, L, 1), ("s", 0, sub, 0), ("s", sub, cut, 0)]):
+            win = T.G[:, 16 * firsts[k][1]:16 * firsts[k][2]]
+            copy[e](T.H[:, 16 * a:16 * b], win.indirect(T.vo[:, a:b]), ["G%d" % k, "vo"], ["H%d" % n], 16 * GAT * (b - a))
+            scan(T.X[:, 16 * a:16 * b], T.keep[:, 0:16 * (b - a)], T.H[:, 16 * a:16 * b], A.mult, ["keep", "H%d" % n], ["X%d" % n], 8 * (b - a))
+            four = [(T.k384[:], T.ones[:, a:b], ["k384", "ones"])] + [
+                (T.Ib[:], T.X[:, 16 * a + 4 * p + 3:16 * b:16], ["Ib", "X%d" % n]) for p in range(4)]
+            mm("s%d" % n, PS, T[PS][:, a:b], four, 5 * max(64, b - a))
+            mm("z%d" % n, PZ, T[PZ][:, a:b], [(T.In[:], T.zg[:, a:b], ["In", "zg"])] + four, 6 * max(64, b - a))
+        w = piece(T, "w%d" % t, rank) if t < S - 1 else T.wl[:]
+        ts(T.tq[:], P(PS), -127.5, None, A.add, None, [PS], ["tq"])
+        tt(w, P(PS), T.tq[:], A.subtract, [PS, "tq"], ["xi"])
+        if t < S - 1:
+            send("w%d" % t, w, ["xi"])
+        dmas("y", "so" if t else "sx", [(T.yx[:, t * L:(t + 1) * L], w)], ["xi"], [], 256 * L)
+        tt(T.yes[:], P(PZ), T.tq[:], A.is_ge, [PZ, "tq"], ["yes"])
+        mm("msk", PV, P(PV), [(T.ones[:, 0:128], T.yes[:], ["ones", "yes"])], L)
+        ts(T.msk[:], P(PV), 59.5, None, A.is_ge, None, [PV], ["msk"])
 
-    picks()
-    place0()
-    ts(sc(15), sc(1), 4.0, -65536.0, A.is_lt, A.mult, ["c0"], ["c15"])
-    ts(sc(16), sc(1), 8.0, 8192.0, A.is_lt, A.mult, ["c0"], ["c16"])
-    ts(sc(17), sc(1), 8.0, -65536.0, A.is_lt, A.mult, ["c0"], ["c17"])
-    ts(sc(18), sc(1), 15.0, None, A.is_lt, None, ["c0"], ["c18"])
-    cp(T.vo[:], P[6], ["p6"], ["vo"])
-    ts(sc(19), sc(1), 1.0, sc(15), A.is_ge, A.mult, ["c0", "c15"], ["c19"])
-    ts(sc(20), sc(1), 4.0, sc(16), A.is_ge, A.mult, ["c0", "c16"], ["c20"])
-    ts(sc(21), sc(1), 5.0, sc(17), A.is_ge, A.mult, ["c0", "c17"], ["c21"])
-    fin = first_name("Ef")
-    codes()
-    ts(T.m1[:], T.dif[:], 0.0, sc(7), A.is_equal, A.mult, ["dif", "c7"], ["m1"])
-    ts(T.m2[:], T.dif[:], -1.0, sc(19), A.is_equal, A.mult, ["dif", "c19"], ["m2"])
-    ts(T.Sh[:], T.dif[:], 1.0, sc(18), A.is_equal, A.mult, ["dif", "c18"], ["Sh"])
-    tt(T.MY[:], T.m1[:], T.m2[:], A.add, ["m1", "m2"], ["MY"])
-    ts(T.I0[:], T.dif[:], 0.0, sc(13), A.is_equal, A.mult, ["dif", "c13"], ["I0"])
-    ts(T.m1[:], T.dif[:], -4.0, sc(20), A.is_equal, A.mult, ["dif", "c20"], ["m1"])
-    ts(T.m2[:], T.dif[:], -5.0, sc(21), A.is_equal, A.mult, ["dif", "c21"], ["m2"])
-    fin()
-    tt(T.MK[:], T.m1[:], T.m2[:], A.add, ["m1", "m2"], ["MK"])
-    for b in range(3):
-        act(T["In%d" % b][:], T.I0[:], F.Identity, ["I0"], ["In%d" % b], scale=float(rank * R + L * b))
-    record(0)
-    bound(0)
-    act(T.Id[:], T.I32[:], F.Identity, ["I32"], ["Id"], scale=-8192.0)
-    act(T.Iu[:], T.I32[:], F.Identity, ["I32"], ["Iu"], scale=1344.0)
-    act(T.Ir[:], T.I32[:], F.Identity, ["I32"], ["Ir"], scale=-4416.0)
-    act(T.I3[:], T.I32[:], F.Identity, ["I32"], ["I3"], scale=-3.0)
-    ts(sc(22), sc(3), 7.0, 1.0, A.mult, A.add, ["c0"], ["c22"])
-    ts(sc(23), sc(4), 63.0, 1.0, A.mult, A.add, ["c0"], ["c23"])
-    ts(sc(24), sc(1), 4.0, None, A.is_lt, None, ["c0"], ["c24"])
-    ms(T.k8192[:], 10240.0, ["k8192"])
-    ms(T.kd[0:64, :], 7680.0, ["kd1"])
-    ms(T.kd[64:128, :], 72.0, ["kd2"])
-    ts(sc(25), sc(22), sc(23), sc(24), A.mult, A.mult, ["c22", "c23", "c24"], ["c25"])
-    ts(T.Wq[:], T.g16[:], sc(10), sc(25), A.is_equal, A.mult, ["g16", "c10", "c25"], ["Wq"])
-
+    cp(T.c16[:], T.c0i[:], ["c0i"], ["c16"])
+    cp(T.Ef[:], T.e0i[:], ["e0i"], ["Ef"])
+    cp(T.eo[:], T.e0i[:], ["e0i"], ["eo"])
+    now[0] = 0
+    lane_list([(T.Bc0[:], T.c16[:], ["Bc0", "c16"])], "scq", qL, "qL", 0.0, 2 * L)
     for t in range(S):
-        w = values(t)
-        tt(T.yes[:], w, T.zg[:], A.is_ge, ["w%d" % t, "zg"], ["yes"])
-        mms("p5", P[5], [(T.ones[:, 0:128], T.yes[:], ["ones", "yes"])])
+        lists(t)
         if t == 0:
-            if rank > 0:
-                cp(T.EW[:, 0:lo], T.EU[:, 0:lo], ["inei"], ["EWa"])
-            if rank < N - 1:
-                cp(T.EW[:, lo + R:M], T.EU[:, lo + R:M], ["inei"], ["EWb"])
-            closure(0)
-        tt(P[1], P[1], T.Ra[:], A.subtract, ["p1", "Ra"], [])
-        ts(T.msk[:], P[5], 59.5, None, A.is_ge, None, ["p5"], ["msk"])
-        tt(P[1], P[1], T.msk[:], A.mult, ["p1", "msk"], [])
-        tt(T.Rn[:], P[1], T.Ra[:], A.add, ["p1", "Ra"], ["Rn"])
-        act(T.Dg[:], T.Rn[:], F.Identity, ["Rn"], ["Dg"], bias=160.0 - 0.28125, scale=1.0 / 8192.0)
-        envs = [(T.k8192[:], T.ones[:], ["k8192", "ones"]), (T.I32[:], T.Rn[:], ["I32", "Rn"]), (T.Id[:], T.Dg[:], ["Id", "Dg"])]
-        if t == S - 1:
-            mms("p2", P[2], envs)
-            mms("p3", P[3], [(T.Wq[:], T.Dg[:], ["Wq", "Dg"])])
-            ts(T.qf[:], P[3], -93600.0, None, A.add, None, ["p3"], ["qf"])
-            act(T.Ef[:], P[2], F.Copy, ["p2"], ["Ef"])
-            dmas("y", "so", [(T.yc[:], T.qf[0::16, :])], ["qf"], [])
-            dmas("s", "so", [(T.ye[:], T.Ef[:])], ["Ef"], [])
-            break
-        u = t + 1
-        mms("p2", P[2], envs)
-        fin = lane_list(3, [(T.Wq[:], T.Dg[:], ["Wq", "Dg"])], "scq", "qL", qL, -93600.0)
-        act(T.ub[:], P[2], F.Identity, ["p2"], ["ub"], bias=160.0 - 0.5 + 1.0 / 384.0, scale=1.0 / L)
-        act(T.rb[:], P[2], F.Identity, ["p2"], ["rb"], bias=160.0 - 0.5 + 1.0 / 1152.0, scale=1.0 / R)
-        act(T.Ef[:], P[2], F.Copy, ["p2"], ["Ef"])
-        fin()
-        if u != 3:
-            mms("p5", P[5], [(T.Ib[:], T.ub[:], ["Ib", "ub"]), (T.I3[:], T.rb[:], ["I3", "rb"])])
-        mms("p4", P[4], [(T.kd[:], T.ones[:], ["kd1", "kd2", "ones"]), (T.Iu[:], T.ub[:], ["Iu", "ub"]), (T.Ir[:], T.rb[:], ["Ir", "rb"])])
-        picks()
-        codes()
-        place0()
-        if u < 3:
-            ts(T.mm[:], P[5], u - 320.5, None, A.is_lt, None, ["p5"], ["mm"])
-            tt(P[4], P[4], T.mm[:], A.mult, ["p4", "mm"], [])
-            tt(T.Eo[:], P[4], T.Ef[:], A.add, ["p4", "Ef"], ["Eo"])
-        elif u == 3:
-            tt(T.Eo[:], P[4], T.Ef[:], A.add, ["p4", "Ef"], ["Eo"])
+            values(t)
+            widen()
+            closure(t)
         else:
-            ts(T.mm[:], P[5], -319.5, float(M), A.is_lt, A.mult, ["p5"], ["mm"])
-            tt(P[4], P[4], T.Ef[:], A.add, ["p4", "Ef"], [])
-            tt(T.Eo[:], P[4], T.mm[:], A.add, ["p4", "mm"], ["Eo"])
-        cp(T.vo[:], P[6], ["p6"], ["vo"])
-        cp(T.eo[:], T.Eo[:], ["Eo"], ["eo"])
-        record(u)
-        fin = first_name("Eo")
-        bound(u)
-        fin()
+            closure(t)
+            values(t)
+        now[0] = t + 1
+        tt(T.Yq[:], P(PR), T.msk[:], A.mult, [PR, "msk"], ["Yq"])
+        code = [(T.Wq[:], T.Dg[:], ["Wq", "Dg"]), (T.Ib[:], T.Yq[:], ["Ib", "Yq"])]
+        environments()
+        if t < S - 1:
+            lane_list(code, "scq", qL, "qL", -93600.0, 3 * L)
+    mm("qf", PL, P(PL), code, 2 * L)
+    ts(T.qf[:], P(PL), -93600.0, None, A.add, None, [PL], ["qf"])
+    dmas("y", "so", [(T.yc[:], T.qf[0::16, :])], ["qf"], [], 32 * L)
+    dmas("s", "so", [(T.ye[:], T.Ef[:])], ["Ef"], [], 512 * L)
 
+    count = issue()
     for s in ("sv", "ss", "sp", "sg", "so"):
         g.sync.wait_ge(T.sem[s], count[s])
     g.wait_ge(T.sem.ls, count["ls"])

@@ -3,22 +3,29 @@ from concourse.mybir import AluOpType as A, ActivationFunctionType as F
 
 N, C, L, R, M, S = 8, 1536, 192, 576, 4608, 5
 CORES_ALL = 128
-SHARE = [(112, 72), (144, 104), (112, 72), (112, 72), (112, 72)]
-ROUTE = {"xi": "split0", "ei": "split1", "e": "split1", "w": "split0"}
+ALL = (L, [("s", 0, 56), ("v", 112, 192), ("s", 56, 112)], [("s", 0, 56), ("v", 128, 192), ("s", 56, 100), ("s", 100, 128)])
+NONE = (0, [], [("v", 112, 192), ("s", 0, 72), ("s", 72, 112)])
+SOME = (96, [("s", 0, 48), ("s", 48, 96)], [("v", 140, 192), ("s", 0, 48), ("s", 48, 96), ("s", 96, 140)])
+CUT = [ALL, NONE, NONE, NONE, NONE]
+FLAT = 3072
+KEEP = 16 * 80
+ROUTE = {"x": "split0", "e": "split1", "w": "split0"}
 BIG = 262144.0
-EARLY = 1024
-START = {"v": "cci c0i i1 i2 i3 i4 i5 c0 c6 c7 c8 I32 Blk c11 cc1 cc2 own ei"}
-ORDER = {"v": "Yq Ye scq eo qL Vg oh vo Pp G1 scn H0 tL X0 X1 X2 tq xi yes msk",
-         "s": "Ef Kg zg es G0 H1 H2 Dg Ra",
-         "p": "qL E v0 vo es tL bind s0 z0 s1 z1 s2 z2 de msk dq apply",
-         "g": "sente sentg sentw senth"}
-ORDERS = [{"v": "scq qL Vg vo oh Pp scn tL wide0 G1 H0 X0 X1 X2 tq xi wide1 yes wide2 wide3 wide4 wide5 wide6 msk",
-           "s": "zg Kg es G0 H1 H2 Dg Ra",
-           "p": "qL vo v0 tL es bind s0 z0 s1 z1 s2 z2 msk de dq apply",
-           "g": "sente sentg sentw senth"},
-          dict(ORDER, v="Ye Yq eo scq qL Vg vo G1 oh H0 Pp X0 scn X1 tL X2 tq xi yes msk", s="Ef G0 zg H1 H2 Kg Dg Ra es",
-               p="E qL vo v0 bind tL s0 z0 s1 z1 s2 z2 de msk es dq apply", g="sentg sentw sente senth"),
-          ORDER, ORDER, dict(ORDER, v=ORDER["v"].replace("xi yes", "yes xi")), {"v": "Ye Yq Ef qf", "s": "", "p": "", "g": ""}]
+TURN = False
+LATER = "xi"
+EARLY = 768
+START = {"v": "cci c0i rst ones i1 i2 i3 i4 i5 c0 rst2 I32 c6 c7 Blk c8 lt Ef c1i c1j c2i c2j owni ei ownj ej q0 pen c9 c24 c10 Perm",
+         "s": "FL0 FL1 Ib Bc0 In ha FL2 FL3 FL4 FL5 lo Z0 Z1 Z2 Z3 Perw U0 U1 U2 U3 U4 U5 U6 U7"}
+ORDER = {"v": "Yq Ye scq Ef qL eo Vg oh vo Pp G0 scn H0 tL X0 X1 X2 tq xi yes msk",
+         "s": "Kg zg es G1 G2 H1 H2 Dg Ra",
+         "p": "qL vb v0 vo es tL bind s0 z0 s1 z1 s2 z2 de dq msk apply qa",
+         "g": "sente sentg sentw senth", "y": "Fh Fl out put"}
+ORDERS = [dict(ORDER, v="scq qL kd0 Vg kd1 kd2 vo kd3 T1 oh kb eo0 Pp wide0 eo1 eo2 G1 scn X0 tL X1 X2 X3 tq xi wide1 yes wide2 wide3 wide4 wide5 wide6 msk",
+               s="T0 T2 zg keep2 G0 G2 G3 Ip I0 I4 In0 Kg es kn kp J32 Id Wq Wqn Wk Dg Ra In1 In2 neg", p="qL vb vo v0 eo0 eo1 eo2 tL s0 z0 s1 z1 s2 z2 s3 z3 es bind msk dq de apply",
+               g="sentg sentw sente near senth"),
+          dict(ORDER, s="G1 G2 Kg zg H1 es H2 Dg Ra", p="qL vb v0 vo tL bind es s0 z0 s1 z1 s2 z2 de dq msk apply", g="sentg sente sentw senth"),
+          ORDER, ORDER, dict(ORDER, v=ORDER["v"].replace("xi yes", "yes xi")),
+          dict(ORDER, v="Ye Yq Ef qf")]
 CYC, GAT, COL, CALL, WAKE, DMA, BYTE = 0.83e-3, 1.3, 0.42e-3, 0.05, 0.11, 1.6, 1 / 330e3
 WAY = {"xi": 8.0, "ei": 14.0, "w": 6.0, "e": 9.0, "g": 2.2}
 
@@ -29,7 +36,9 @@ SCRATCH = {
     "kb": ("sbuf", [128, 4 * L], "bfloat16"),
     "cei": ("sbuf", [128, R], "int32"), "cci": ("sbuf", [128, R], "int32"),
     "e0i": ("sbuf", [128, L], "int32"), "c0i": ("sbuf", [128, L], "int32"),
-    "keep": ("sbuf", [128, 16 * max(max(L - a, b) for a, b in SHARE)], "bfloat16"), "base": ("sbuf", [128, S * L], "bfloat16"),
+    "keep": ("sbuf", [128, KEEP], "bfloat16"), "lt": ("sbuf", [128, 16], "float32"), "base": ("sbuf", [128, 3 * L], "bfloat16"),
+    "FL": ("sbuf", [128, 32 * L], "bfloat16"), "U": ("sbuf", [128, 16 * 128], "bfloat16"), "Perw": ("sbuf", [128, 256], "bfloat16"),
+    "hi": ("sbuf", [128, 2 * L], "bfloat16"), "lo": ("sbuf", [128, 2 * L], "bfloat16"),
     "sci": ("sbuf", [128, 8], "int32"), "sc": ("sbuf", [128, 32], "float32"),
     "wl": ("sbuf", [128, L], "bfloat16"),
     "qL": ("sbuf", [128, 16], "uint16"), "tL": ("sbuf", [128, 16], "uint16"),
@@ -41,37 +50,36 @@ for _n in ("G", "H", "X"):
     SCRATCH[_n] = ("sbuf", [128, 16 * L], "bfloat16")
 for _n in ("col", "a16", "rst", "Ra", "Ye", "scn", "scq", "Ef", "qf", "Pp"):
     SCRATCH[_n] = ("sbuf", [128, L], "float32")
-for _n in ("colb", "pen", "Vg", "zg", "Kg", "yes", "tq", "Dg", "msk", "ones"):
+for _n in ("colb", "pen", "Vg", "zg", "Kg", "yes", "tq", "Dg", "msk", "ones", "neg"):
     SCRATCH[_n] = ("sbuf", [128, L], "bfloat16")
 for _n in ("Yq", "c16"):
     SCRATCH[_n] = ("sbuf", [128, L], "float16")
 for _n in ("dif", "g16", "I32", "J32", "Sh32", "Blk"):
     SCRATCH[_n] = ("sbuf", [128, 128], "float32")
-for _n in ("Ib", "In", "Perm", "Bc0", "Wq", "Wqn", "Wk", "I0", "I4", "In0", "In1", "In2", "Id", "Ip", "k384", "kp", "kn", "kq"):
+for _n in ("Ib", "In", "IL", "Perm", "Bc0", "Wq", "Wqn", "Wk", "I0", "I4", "In0", "In1", "In2", "Id", "Ip", "k384", "kp", "kn", "kq"):
     SCRATCH[_n] = ("sbuf", [128, 128], "bfloat16")
 for _k in range(8):
     SCRATCH["p%d" % _k] = ("psum", [128, 512], "float32")
 
-PHASES = ["xi", "ei"]
+PHASES = ["xi", "xj", "ei", "ej"]
 for _t in range(S - 1):
     PHASES += ["w%d" % _t, "e%d" % _t]
-GATE = {p: ("h" if p[0] == "e" else "g") + p[1] for p in PHASES[2:]}
-SEMAPHORES = ["sv", "ss", "sp", "sg", "ls", "lx", "so", "dx", "dce", "dcc", "de", "dc", "dcd", "dc2", "dz", "dk", "dt", "dr", "sx"]
+GATE = {p: ("h" if p[0] == "e" else "g") + p[1] for p in PHASES[4:]}
+SEMAPHORES = ["sv", "ss", "sp", "sg", "ls", "lx", "lw", "so", "dx", "dce", "dcc", "de", "dc", "dcd", "dc2", "dz", "dk", "dt", "dr", "sx", "fh", "fl"]
 SEMAPHORES += ["f" + p for p in PHASES if p[0] == "e"] + sorted(set(GATE.values())) + ["aei%d" % _r for _r in range(N)]
-SEMAPHORES += ["a" + p for p in PHASES if p != "ei"] + ["v%s_%d" % (p, k) for p in PHASES for k in range(2)]
+SEMAPHORES += ["a" + p for p in PHASES if p not in ("xj", "ei", "ej")] + ["v%s_%d" % (p, k) for p in PHASES for k in range(2)]
 
 
 def piece(T, ph, r):
-    if ph == "xi":
-        return T.XW[:, r * R:(r + 1) * R]
-    if ph == "ei":
-        return T.EU[:, r * R:(r + 1) * R]
+    if ph[1] in "ij":
+        lo = r * R + "ij".index(ph[1]) * R // 2
+        return (T.XW if ph[0] == "x" else T.EU)[:, lo:lo + R // 2]
     lo = R * r + L * (int(ph[1]) % 3)
     return (T.XW if ph[0] == "w" else T.EW)[:, lo:lo + L]
 
 
 def stage(T, ph, r, fan=False):
-    if ph[1] == "i":
+    if ph[1] in "ij":
         return piece(T, ph, r)
     t = int(ph[1])
     if fan:
@@ -80,7 +88,7 @@ def stage(T, ph, r, fan=False):
 
 
 def arrival(T, ph, r):
-    return T.sem["aei%d" % r if ph == "ei" else "a" + ph]
+    return T.sem["aei%d" % r if ph in ("ei", "ej") else "axi" if ph == "xj" else "a" + ph]
 
 
 def routes(T, topo):
@@ -109,6 +117,13 @@ def routes(T, topo):
                     v = own[len(own) - 1 - n // 2] if r % 2 == 1 else rel[len(rel) - 1 - n // 2]
                 via[(ph, r, ch)] = v
     return chips, via
+
+
+def turn(chips, chip, r):
+    order = list(chips)
+    k = order.index(chip)
+    rest = order[k + 1:] + order[:k]
+    return rest if TURN else [c for c in order if c != chip]
 
 
 def bits(m):
@@ -155,7 +170,7 @@ def helper_program(g, core, T, topo, chips, via):
         for r in mine:
             off, on = masks(topo, cores[r], cores)
             g.wait_ge(T.sem["f" + ph], bits(on))
-            out = [via[(ph, r, ch)] for ch in chips if ch != topo.chip(core)]
+            out = [via[(ph, r, ch)] for ch in turn(chips, topo.chip(core), r)]
             sent += call(write(topo, out, off, T.sem["v%s_%d" % (ph, r % 2)], stage(T, ph, r, True), stage(T, ph, r)), off)
             cleared(ph)
             sent += call(write(topo, [c for c in chips[topo.chip(core)] if c != cores[r]], on, arrival(T, ph, r),
@@ -260,13 +275,14 @@ def rank_program(g, core, T, topo):
     def issue():
         count, token, seen = {}, {}, {k: {} for k in Q}
         for q in ORDER:
-            line = [tags[(None, q, x)] for x in START.get(q, "").split()]
-            line += [tags[(t, q, x)] for t in range(S + 1) for x in ORDERS[t][q].split() if (t, q, x) in tags]
+            line = [tags[(None, q, x)] for x in START.get(q, "").split() if (None, q, x) in tags]
+            line += [tags[(None if (t, q, x) not in tags else t, q, x)] for t in range(S + 1) for x in ORDERS[t][q].split()
+                     if (t, q, x) in tags or (t == 0 and (None, q, x) in tags)]
             for p, n in zip(line, line[1:]):
                 follow(n, p)
         for n in lay_out(calls):
             c = calls[n]
-            for s, v in [token[p] for p in c["pre"] if p in token and p not in c["soft"]] + c["ext"]:
+            for s, v in dict(sorted([token[p] for p in c["pre"] if p in token and p not in c["soft"]] + c["ext"])).items():
                 if seen[c["q"]].get(s, 0) < v:
                     Q[c["q"]].wait_ge(T.sem[s], v)
                     seen[c["q"]][s] = v
@@ -299,14 +315,17 @@ def rank_program(g, core, T, topo):
     def send(ph, src, rd):
         if ph[0] == "e":
             remote([write(topo, [via[("fan", rank)]], on_mask, T.sem["f" + ph], src, stage(T, ph, rank, True))], rd, ["sent" + ph],
-                   bits(on_mask), 256 * R * 2)
+                   bits(on_mask), 256 * R)
             return
-        out = write(topo, [via[(ph, rank, ch)] for ch in chips if ch != chip], off_mask, T.sem["v%s_%d" % (ph, rank % 2)], src, stage(T, ph, rank))
-        near = write(topo, [sib], on_mask, T.sem["a" + ph], src, src)
-        if ph == "xi":
-            remote([out, near], rd, ["sentxi"], bits(off_mask) + bits(on_mask), 256 * R * 6, "lx", 2.0)
+        out = write(topo, [via[(ph, rank, ch)] for ch in turn(chips, chip, rank)], off_mask, T.sem["v%s_%d" % (ph, rank % 2)], src, stage(T, ph, rank))
+        near = write(topo, [sib], on_mask, arrival(T, ph, rank), src, src)
+        if ph[0] == "x":
+            remote([out, near], rd, ["sent" + ph], bits(off_mask) + bits(on_mask), 256 * R * 3, "lx", 2.0 if ph == "xi" else 0.0)
+        elif ph == "w0":
+            remote([out], rd, ["sent" + ph], bits(off_mask), 256 * L * 6, "lw")
+            remote([near], rd + ["ing" + ph[1]], ["near"], bits(on_mask), 0)
         else:
-            remote([out, near], rd + ["ing" + ph[1]], ["sent" + ph], bits(off_mask) + bits(on_mask), 256 * L * 6)
+            remote([out, near], rd + ["ing" + ph[1]], ["sent" + ph], bits(off_mask) + bits(on_mask), 256 * L * 6, "lw")
 
     def clear(ph, rd):
         to = sorted(writers(T, topo, chips, via, ph, core), key=lambda d: (topo.chip(d) == chip, d))
@@ -320,9 +339,11 @@ def rank_program(g, core, T, topo):
         each = {r: bits(on_mask if cores[r] == sib else topo.mask(via[(ph, r, chip)], core)) for r in range(N) if r != rank}
         if ph == "ei":
             for r, n in each.items():
-                arrive["inei%d" % r] = ("aei%d" % r, n, WAY[ph] / (2 if cores[r] == sib else 1), "sentei")
-        else:
-            arrive["in" + ph] = ("a" + ph, sum(each.values()), WAY[ph if ph in WAY else ph[0]] - 0.8, "sent" + ph)
+                arrive["inei%d" % r] = ("aei%d" % r, 2 * n, WAY[ph] / (2 if cores[r] == sib else 1), "sentej")
+        elif ph == "xi":
+            arrive["inxi"] = ("axi", 2 * sum(each.values()), WAY[ph], "sentxj")
+        elif ph[1] != "j":
+            arrive["in" + ph] = ("a" + ph, sum(each.values()), WAY[ph[0]] - 0.8, "sent" + ph)
     for t in range(S - 1):
         arrive["ing%d" % t] = ("g%d" % t, 1, WAY["g"] - 0.8, "sentg%d" % t)
 
@@ -358,23 +379,26 @@ def rank_program(g, core, T, topo):
 
     copy = {"v": cp, "s": act}
     sc = lambda k: T.sc[:, k:k + 1]
+    lt = lambda k: T.lt[:, k:k + 1]
     qL, tL = T.qL[:, 0:L // 16], T.tL[:, 0:L // 16]
     PS, PZ, PV, PL, PE, P0, PR, PD = ["p%d" % k for k in range(8)]
     P = lambda b: T[b][:, 0:L]
     GL = GAT * L
 
-    dmas("y", "dx", [(piece(T, "xi", rank), T.x0[:])], [], ["xi"], 256 * R)
+    dmas("y", "dx", [(T.XW[:, rank * R:(rank + 1) * R], T.x0[:])], [], ["xi"], 256 * R)
     dmas("y", "dce", [(T.cei[:], T.ce0[:])], [], ["cei"], 512 * R)
     ms(T.cci[:], 0, ["cci"], R)
     ms(T.c0i[:], 0, ["c0i"], L)
     dmas("y", "dcc", [(T.cci[j::16, :], T.cc0[:]) for j in range(4)], [], ["cci"], 128 * R)
     dmas("s", "de", [(T.e0i[:], T.e0[:])], [], ["e0i"], 512 * L)
     send("xi", piece(T, "xi", rank), ["xi"])
+    behind.append("sentxi")
+    send("xj", piece(T, "xj", rank), ["xi"])
     loads = [("dc", [(T.c0i[0::16, :], T.c0[:])], [], "c0i", 32 * L),
              ("dk", [(T.kc[:, 0:L // 2], T.ky[:]), (T.kc[:, L // 2:L], T.kid[:])], [], "kc", 64 * C),
              ("dcd", [(T.cdt[:, 0:EARLY], T.cd[:, 0:EARLY])], [], "cd1", 512 * EARLY),
-             ("dc2", [(T.cdt[:, EARLY:C], T.cd[:, EARLY:C])], ["sentxi"], "cd2", 512 * (C - EARLY)),
-             ("dz", [(T.TZ[:], T.zt[:])], [], "TZ", 256 * C)]
+             ("dc2", [(T.cdt[:, EARLY:C], T.cd[:, EARLY:C])], [LATER], "cd2", 512 * (C - EARLY)),
+             ("dz", [(T.TZ[:], T.zt[:])], ["sentxj"], "TZ", 256 * C)]
     for n, (sem, pairs, rd, name, nbytes) in enumerate(loads):
         behind.append(loads[n - 1][3] if n else "cci")
         dmas("y", sem, pairs, rd, [name], nbytes)
@@ -393,53 +417,78 @@ def rank_program(g, core, T, topo):
     small = [(6, 3, -0.875, 1.0, A.mult, A.add), (7, 4, -63.0 / 64.0, 1.0, A.mult, A.add),
              (8, 6, sc(7), 8192.0, A.mult, A.mult),
              (9, 2, 3.75, sc(0), A.mult, A.add), (10, 1, -0.75, sc(9), A.mult, A.add),
-             (11, 1, 0.0, None, A.is_equal, None), (12, 1, 15.0, None, A.is_lt, None), (13, 1, 4.0, None, A.is_lt, None),
              (14, 3, 7.0, 1.0, A.mult, A.add), (15, 4, 63.0, 1.0, A.mult, A.add),
-             (16, 14, sc(15), sc(13), A.mult, A.mult),
-             (17, 1, 8.0, sc(13), A.is_lt, A.subtract), (18, 14, sc(15), sc(17), A.mult, A.mult)]
-    uses = {8: [7], 10: [9], 16: [15, 13], 17: [13], 18: [15, 17]}
+             (16, 14, sc(15), lt(4), A.mult, A.mult),
+             (17, 14, sc(15), lt(8), A.mult, A.mult), (18, 17, sc(16), None, A.subtract, None)]
+    ts(T.lt[:], T.col[:, 0:16], sc(1), None, A.is_gt, None, ["col", "c0"], ["lt"], 1)
+    uses = {8: ["c7"], 10: ["c9"], 16: ["c15", "lt"], 17: ["c15", "lt"], 18: ["c16"]}
     for k, src, s1, s2, o0, o1 in small:
-        ts(sc(k), sc(src), s1, s2, o0, o1, ["c0"] + ["c%d" % j for j in [src] + uses.get(k, []) if j > 5], ["c%d" % k], 1)
+        ts(sc(k), sc(src), s1, s2, o0, o1, ["c0"] + uses.get(k, []) + (["c%d" % src] if src > 5 else []), ["c%d" % k], 1)
     ts(T.I32[:], T.dif[:], 0.0, None, A.is_equal, None, ["dif"], ["I32"], 128)
     for name, scale in (("Ib", 1.0), ("In", -1.0), ("Id", -8192.0), ("Ip", 8192.0), ("J32", -1.0)):
         act(T[name][:], T.I32[:], ["I32"], [name], 128, scale=scale)
     ts(T.pen[:], T.a16[:], sc(1), -BIG, A.not_equal, A.mult, ["a16", "c0"], ["pen"])
     act(T.colb[:], T.col[:], ["col"], ["colb"])
-    cuts = sorted({a for a, b in SHARE})
-    for n, a in enumerate(cuts):
-        act(T.base[:, n * L:n * L + a], T.col[:, 0:a], ["col"], ["bs%d" % n], a, scale=16.0)
-        act(T.base[:, n * L + a:(n + 1) * L], T.col[:, 0:L - a], ["col"], ["bv%d" % n], L - a, scale=16.0)
+    kinds = [c for n, c in enumerate(CUT) if c not in CUT[:n]]
+    for k, (nt, names, pieces) in enumerate(kinds):
+        for a, b, step in [(0, nt, 1.0)] + [(a, b, 16.0) for e, a, b in pieces if a >= nt]:
+            if a < b:
+                act(T.base[:, k * L + a:k * L + b], T.col[:, 0:b - a], ["col"], ["base%d" % k], b - a, scale=step)
     ts(T.Perm[:], T.col[:, 0:128], sc(10), None, A.is_equal, None, ["col", "c10"], ["Perm"], 128)
+    act(T.Perw[:, 0:128], T.Perm[:], ["Perm"], ["Perw"], 128, scale=float(L))
+    if CUT[-1][0]:
+        act(T.Perw[:, 128:256], T.Perm[:], ["Perm", "Perw"], ["Per2", "Perw"], 128, scale=2.0 * CUT[-1][0])
+        act(T.IL[:], T.I32[:], ["I32"], ["IL"], 128, scale=float(CUT[-1][0]))
     ts(T.Blk[:], T.g16[:], sc(5), None, A.is_equal, None, ["g16", "c0"], ["Blk"], 128)
-    for name, k in (("Bc0", 11), ("Wq", 16), ("Wk", 18)):
-        act(T[name][:], T.Blk[:], ["Blk", "c%d" % k], [name], 128, scale=sc(k))
+    for name, col, nm in (("Bc0", lt(1), "lt"), ("Wq", sc(16), "c16"), ("Wk", sc(18), "c18")):
+        act(T[name][:], T.Blk[:], ["Blk", nm], [name], 128, scale=col)
     act(T.Wqn[:], T.Wq[:], ["Wq"], ["Wqn"], 128, scale=-1.0)
-    ts(T.Sh32[:], T.dif[:], 1.0, sc(12), A.is_equal, A.mult, ["dif", "c12"], ["Sh32"], 128)
-    act(T.I0[:], T.I32[:], ["I32", "c11"], ["I0"], 128, scale=sc(11))
-    act(T.I4[:], T.Ip[:], ["Ip", "c13"], ["I4"], 128, scale=sc(13))
+    ts(T.Sh32[:], T.dif[:], 1.0, lt(15), A.is_equal, A.mult, ["dif", "lt"], ["Sh32"], 128)
+    act(T.I0[:], T.I32[:], ["I32", "lt"], ["I0"], 128, scale=lt(1))
+    act(T.I4[:], T.Ip[:], ["Ip", "lt"], ["I4"], 128, scale=lt(4))
     for b in range(3):
         act(T["In%d" % b][:], T.I0[:], ["I0"], ["In%d" % b], 128, scale=float(rank * R + L * b))
     ms(T.ones[:], 1.0, ["ones"], L // 2)
+    act(T.neg[:], T.ones[:], ["ones"], ["neg"], scale=-1.0)
     ms(T.rst[:], 0.0, ["rst"], L)
     ms(T.rst[:, 0::16], -4.0 * BIG, ["rst2", "rst"])
-    ms(T.keep[:], 1.0, ["keep"], 4 * L)
-    ms(T.keep[:, 0::4], 0.0, ["keep2", "keep"], L)
-    ms(T.k384[:], 384.0, ["k384"])
-    ms(T.kp[:], 10240.0, ["kp"])
-    ms(T.kn[:], -10240.0, ["kn"])
+    for name, value in (("k384", 384.0), ("kp", 10240.0), ("kn", -10240.0)):
+        act(T[name][:], T.ones[:, 0:128], ["ones"], [name], 128, scale=value)
     ms(T.kq[0:64, :], 1456.0, ["kq1"])
     ms(T.kq[64:128, :], 6.5, ["kq2"])
-    ts(T.cci[:], T.cci[:], sc(8), None, A.mult, None, ["cci", "c8"], ["cc1", "cci"], R)
-    ts(T.cci[:], T.cci[:], 7 * 8192, None, A.bitwise_and, None, ["cci"], ["cc2", "cci"], R)
     lo = rank * R
-    tt(T.EW[:, lo:lo + R], T.cci[:], T.cei[:], A.add, ["cci", "cei"], ["own", "EW%d" % rank], 2 * R)
-    cp(piece(T, "ei", rank), T.EW[:, lo:lo + R], ["EW%d" % rank], ["ei"], R)
-    behind.append("sentxi")
-    send("ei", piece(T, "ei", rank), ["ei"])
+    for k, h in enumerate("ij"):
+        c, own = slice(k * R // 2, (k + 1) * R // 2), T.EW[:, lo + k * R // 2:lo + (k + 1) * R // 2]
+        ts(T.cci[:, c], T.cci[:, c], sc(8), None, A.mult, None, ["cci", "c8"], ["c1" + h], R // 2)
+        ts(T.cci[:, c], T.cci[:, c], 7 * 8192, None, A.bitwise_and, None, ["c1" + h], ["c2" + h], R // 2)
+        tt(own, T.cci[:, c], T.cei[:, c], A.add, ["c2" + h, "cei"], ["own" + h], R)
+        cp(piece(T, "e" + h, rank), own, ["own" + h], ["e" + h], R // 2)
+        behind.append("sentxj" if k == 0 else "sentei")
+        send("e" + h, piece(T, "e" + h, rank), ["e" + h])
+    wrote["EW%d" % rank] = wrote["owni"] + wrote["ownj"]
+    read["EW%d" % rank] = read["owni"] + read["ownj"]
+    for k in range(FLAT // 512):
+        act(T.FL[:, 512 * k:512 * (k + 1)], T.XW[:, lo:lo + 512], ["xi"], ["FL%d" % k], 512)
+    wrote["Fh"] = wrote["Fl"] = [p for k in range(FLAT // 512) for p in wrote["FL%d" % k]]
+    for k in range(4):
+        act(T.U[:, 512 * k:512 * (k + 1)], T.XW[:, lo:lo + 512], ["xi"], ["Z%d" % k], 512, scale=0.0)
+    wrote["Z"] = [p for k in range(4) for p in wrote["Z%d" % k]]
+    ts(T.sc[:, 24:32], T.col[:, 0:8], sc(5), lt(2), A.is_equal, A.mult, ["col", "c0", "lt"], ["c24"], 1)
+    for k in range(8):
+        act(T.U[:, 16 * k:16 * k + 15 * 129 + 1:129], T.ones[:, 0:16], ["ones", "c24", "Z"], ["U%d" % k], 16, scale=sc(24 + k))
+    wrote["U"] = [p for k in range(8) for p in wrote["U%d" % k]]
+    now[0] = 0
     for j in range(4):
         ts(T.kd4[:, j * L:(j + 1) * L], T.kc[:], 3 * j, 7, A.logical_shift_right, A.bitwise_and, ["kc"], ["kd%d" % j])
     cp(T.kb[:], T.kd4[:], ["kd%d" % j for j in range(4)], ["kb"], 4 * L)
-    ms(T.TK[:], 0.0, ["TK"], C // 2)
+    now[0] = None
+    behind.append("sentej")
+    iota(T.keep[:], [[0, KEEP]], 1, 0, ["keep"], KEEP)
+    behind.append("keep")
+    iota(T.TK[:], [[0, C]], 0, 0, ["TK"], C)
+    now[0] = 0
+    act(T.keep[:, 0::4], T.keep[:, 1::4], ["keep"], ["keep2", "keep"], KEEP // 4, scale=0.0)
+    now[0] = None
     behind.append("TZ")
     dmas("y", "dt", [(T.TK[4 * k + j::16, :], T.kb[:, j * L + k * L // 2:j * L + (k + 1) * L // 2]) for j in range(4) for k in range(2)],
          ["kb"], ["TK"], 128 * 4 * L * 6)
@@ -447,7 +496,7 @@ def rank_program(g, core, T, topo):
     def widen():
         way = lambda r: (cores[r] != sib, cores[r] != sib and topo.chip(via[("ei", r, chip)]) != chip, r)
         for n, r in enumerate(sorted([r for r in range(N) if r != rank], key=way)):
-            cp(T.EW[:, r * R:(r + 1) * R], piece(T, "ei", r), ["inei%d" % r], ["wide%d" % n, "EW%d" % r], R)
+            cp(T.EW[:, r * R:(r + 1) * R], T.EU[:, r * R:(r + 1) * R], ["inei%d" % r], ["wide%d" % n, "EW%d" % r], R)
 
     def lane_list(terms, buf, out, name, shift, cy):
         mm(name, PL, P(PL), [(T.Ib[:], T.pen[:], ["Ib", "pen"])] + terms, cy)
@@ -456,18 +505,45 @@ def rank_program(g, core, T, topo):
 
     def environments():
         tt(T.Ye[:], T[PD][:, 0:L], T.msk[:], A.mult, [PD, "msk"], ["Ye"])
-        if now[0] == S:
-            tt(T.Ef[:], P(PE), T.Ye[:], A.add, [PE, "Ye"], ["Ef"])
-            return
-        mm("E", PE, P(PE), [(T.I32[:], T.Ye[:], ["I32", "Ye"])], 4 * L, first=False)
-        cp(T.eo[:], P(PE), [PE], ["eo"])
-        act(T.Ef[:], P(PE), [PE], ["Ef"])
+        tt(T.Ef[:], P(PE), T.Ye[:], A.add, [PE, "Ye"], ["Ef"])
+        if now[0] < S:
+            recut(now[0])
+            nt = CUT[now[0]][0]
+            cp(T.eo[:, nt:L], T.Ef[:, nt:L], ["Ef"], ["eo"], L - nt)
+
+    def recut(t):
+        for kinds in (["eo"], ["G"], ["H", "T"], ["X"]):
+            names = [k + n for k in kinds for n in ("", "0", "1", "2", "3", "4")]
+            users = [p for r in names for p in wrote.get(r, []) + read.get(r, [])]
+            for r in names if CUT[t] != CUT[t - 1] else []:
+                wrote[r], read[r] = [], list(users)
+
+    def flatten(n):
+        dmas("y", "fh", [(T.FL[0::16, 0:16 * n], T.hi[:, 0:n])], ["ha", "hb"], ["Fh"], 256 * n)
+        dmas("y", "fl", [(T.FL[1::16, 0:16 * n], T.lo[:, 0:n])], ["la", "lb"], ["Fl"], 256 * n)
 
     def lists(t):
+        nt, names, pieces = CUT[t]
+        k = kinds.index(CUT[t])
         cp(T.Vg[:], T.cdt[:, 0:C].indirect(qL), ["cdt", "qL"], ["Vg"], GL)
-        n = cuts.index(SHARE[t][0])
-        mm("vo", PV, P(PV), [(T.Ib[:], T.base[:, n * L:(n + 1) * L], ["Ib", "bs%d" % n, "bv%d" % n]), (T.Perm[:], T.Vg[:], ["Perm", "Vg"])], 2 * L)
+        mm("vb", PV, P(PV), [(T.Ib[:], T.base[:, k * L:(k + 1) * L], ["Ib", "base%d" % k])], L, last=False)
+        if t and nt:
+            mm("vm", PV, T[PV][:, 0:nt], [(T.IL[:], T.msk[:, 0:nt], ["IL", "msk"])], nt, first=False, last=False)
+        parts = [(T.Perw[:, 128 * min(t, 1):128 * min(t, 1) + 128], 0, nt), (T.Perm[:], nt, L)]
+        parts = [x for x in parts if x[1] < x[2]]
+
+        def picks(q):
+            for n, (m, a, b) in enumerate(parts):
+                ins = q.matmul(T[PV][:, a:b], m, T.Vg[:, a:b], False, n == len(parts) - 1)
+            ins.then_inc(T.sem.sp, 1)
+        note("p", picks, ["Perw", "Perm", "Vg"], [PV], "sp", 1, L * COL, 0.1, tag="vo")
         cp(T.vo[:], P(PV), [PV], ["vo"])
+        for n, (e, a, b) in enumerate(names):
+            copy[e](T.H[:, 16 * a:16 * b], T.FL[:, 0:(32 if t else 16) * nt].indirect(T.vo[:, a:b]), ["Fh", "Fl", "vo"], ["T%d" % n], 16 * GAT * (b - a))
+            bank = (PS, PZ)[n % 2]
+            mm("eo%d" % n, bank, T[bank][:, a:b],
+               [(T.U[:, 128 * k:128 * k + 128], T.H[:, 16 * a + k:16 * b:16], ["U", "T%d" % n]) for k in range(16)], 16 * max(64, b - a))
+            cp(T.eo[:, a:b], T[bank][:, a:b], [bank], ["eo%d" % n], b - a)
         mm("v0", P0, P(P0), [(T.Bc0[:], T.Vg[:], ["Bc0", "Vg"])], L)
         ts(P(P0), P(P0), sc(1), None, A.is_equal, None, [P0, "c0"], ["oh"])
         tt(T.Pp[:], P(P0), T.Ef[:], A.mult, [P0, "Ef"], ["Pp"])
@@ -490,29 +566,46 @@ def rank_program(g, core, T, topo):
         act(T.Ra[:], win, rd, ["Ra"], GL)
         if t < S - 1:
             clear("e%d" % t, ["Dg", "Ra"])
-            dmas("y", "dr", [(piece(T, "e%d" % t, rank), T.ES[:, t * L:(t + 1) * L])], ["es%d" % t], ["EW%d" % rank], 512 * L)
+            dmas("y", "dr", [(piece(T, "e%d" % t, rank), T.ES[:, t * L:(t + 1) * L])], ["es%d" % t], ["put", "EW%d" % rank], 512 * L)
         mm("dq", PR, P(PR), [(T.kq[:], T.ones[:], ["kq1", "kq2", "ones"]), (T.Wk[:], T.Kg[:], ["Wk", "Kg"]),
                              (T.Wqn[:], T.Dg[:], ["Wqn", "Dg"])], 3 * L)
         mm("de", PD, T[PD][:, 0:L], [(T.Ip[:], T.Dg[:], ["Ip", "Dg"]), (T.J32[:], T.Ra[:], ["J32", "Ra"])], 5 * L, first=False)
         mm("apply", PE, P(PE), [(T.kp[:], T.ones[:], ["kp", "ones"]), (T.Id[:], T.Dg[:], ["Id", "Dg"]), (T.I32[:], T.Ra[:], ["I32", "Ra"])],
-           6 * L, last=t == S - 1)
+           6 * L)
+        if t == S - 1:
+            mm("qa", PL, P(PL), [(T.kq[:], T.neg[:], ["kq1", "kq2", "neg"]), (T.Wq[:], T.Dg[:], ["Wq", "Dg"])], 2 * L)
+        nt = CUT[t + 1][0] if t < S - 1 else 0
+        if nt:
+            b = "In%d" % (t % 3)
+            bind = [(T.I0[:], T.colb[:, 0:nt], ["I0", "colb"]), (T[b][:], T.ones[:, 0:nt], [b, "ones"]), (T.Sh32[:], T.Ef[:, 0:nt], ["Sh32", "Ef"])]
+            mm("hb", P0, T[P0][:, 0:nt], bind, 6 * nt)
+            act(T.hi[:, nt:2 * nt], T[P0][:, 0:nt], [P0], ["hb"], nt)
+            mm("lb", P0, T[P0][:, 0:nt], bind + [(T.In[:], T.hi[:, nt:2 * nt], ["In", "hb"])], 7 * nt)
+            act(T.lo[:, nt:2 * nt], T[P0][:, 0:nt], [P0], ["lb"], nt)
+            act(T.hi[:, 0:nt], T[PE][:, 0:nt], [PE], ["ha"], nt)
+
+    def low_parts(t):
+        nt = CUT[t][0]
+        if nt:
+            mm("la", PS, T[PS][:, 0:nt], [(T.kp[:], T.ones[:, 0:nt], ["kp", "ones"]), (T.Id[:], T.Dg[:, 0:nt], ["Id", "Dg"]),
+                                          (T.I32[:], T.Ra[:, 0:nt], ["I32", "Ra"]), (T.In[:], T.hi[:, 0:nt], ["In", "ha"])], 7 * nt)
+            act(T.lo[:, 0:nt], T[PS][:, 0:nt], [PS], ["la"], nt)
+            flatten(2 * nt)
 
     def values(t):
-        rd = ["xi", "inxi", "eo"] + ["inw%d" % u for u in range(t)]
-        for names in (["G0", "G1"], ["H0", "H1", "H2"], ["X0", "X1", "X2"]):
-            users = [p for r in names for p in wrote.get(r, []) + read.get(r, [])]
-            for r in names:
-                wrote[r], read[r] = [], list(users)
-        cut, sub = SHARE[t]
-        firsts = [("s", 0, cut), ("v", cut, L)]
-        for n, (e, a, b) in enumerate(firsts):
-            copy[e](T.G[:, 16 * a:16 * b], T.XW[:, 0:M].indirect(T.eo[:, a:b]), rd, ["G%d" % n], 16 * GAT * (b - a))
+        rd = ["xi", "inxi"] + ["inw%d" % u for u in range(t)]
+        nt, names, pieces = CUT[t]
+        for n, (e, a, b) in enumerate(pieces):
+            lists = ["eo"] if a >= nt else ["eo%d" % k for k, (e2, a2, b2) in enumerate(names) if a2 < b and a < b2]
+            copy[e](T.G[:, 16 * a:16 * b], T.XW[:, 0:M].indirect(T.eo[:, a:b]), rd + lists, ["G%d" % n], 16 * GAT * (b - a))
         if t < S - 1:
-            clear("w%d" % t, ["G0", "G1"])
-        for n, (e, a, b, k) in enumerate([("v", cut, L, 1), ("s", 0, sub, 0), ("s", sub, cut, 0)]):
-            win = T.G[:, 16 * firsts[k][1]:16 * firsts[k][2]]
-            copy[e](T.H[:, 16 * a:16 * b], win.indirect(T.vo[:, a:b]), ["G%d" % k, "vo"], ["H%d" % n], 16 * GAT * (b - a))
-            scan(T.X[:, 16 * a:16 * b], T.keep[:, 0:16 * (b - a)], T.H[:, 16 * a:16 * b], A.mult, ["keep", "H%d" % n], ["X%d" % n], 8 * (b - a))
+            clear("w%d" % t, ["G%d" % n for n in range(len(pieces))])
+        for n, (e, a, b) in enumerate(pieces):
+            src, name = T.G, "G%d" % n
+            if a >= nt:
+                src, name = T.H, "H%d" % n
+                copy[e](T.H[:, 16 * a:16 * b], T.G[:, 16 * a:16 * b].indirect(T.vo[:, a:b]), ["G%d" % n, "vo"], [name], 16 * GAT * (b - a))
+            scan(T.X[:, 16 * a:16 * b], T.keep[:, 0:16 * (b - a)], src[:, 16 * a:16 * b], A.mult, ["keep", name], ["X%d" % n], 8 * (b - a))
             four = [(T.k384[:], T.ones[:, a:b], ["k384", "ones"])] + [
                 (T.Ib[:], T.X[:, 16 * a + 4 * p + 3:16 * b:16], ["Ib", "X%d" % n]) for p in range(4)]
             mm("s%d" % n, PS, T[PS][:, a:b], four, 5 * max(64, b - a))
@@ -522,16 +615,23 @@ def rank_program(g, core, T, topo):
         tt(w, P(PS), T.tq[:], A.subtract, [PS, "tq"], ["xi"])
         if t < S - 1:
             send("w%d" % t, w, ["xi"])
-        dmas("y", "so" if t else "sx", [(T.yx[:, t * L:(t + 1) * L], w)], ["xi"], [], 256 * L)
+        dmas("y", "so" if t else "sx", [(T.yx[:, t * L:(t + 1) * L], w)], ["xi"] + (["sentw%d" % t] if t < S - 1 else []), ["out"], 256 * L)
         tt(T.yes[:], P(PZ), T.tq[:], A.is_ge, [PZ, "tq"], ["yes"])
         mm("msk", PV, P(PV), [(T.ones[:, 0:128], T.yes[:], ["ones", "yes"])], L)
         ts(T.msk[:], P(PV), 59.5, None, A.is_ge, None, [PV], ["msk"])
 
-    cp(T.c16[:], T.c0i[:], ["c0i"], ["c16"])
+    cp(T.c16[:], T.c0i[:], ["c0i"], ["q0"])
     cp(T.Ef[:], T.e0i[:], ["e0i"], ["Ef"])
-    cp(T.eo[:], T.e0i[:], ["e0i"], ["eo"])
+    act(T.hi[:, 0:L], T.Ef[:], ["Ef"], ["ha", "hb"])
+    mm("lo", PE, P(PE), [(T.I32[:], T.Ef[:], ["I32", "Ef"]), (T.In[:], T.hi[:, 0:L], ["In", "ha"])], 5 * L)
+    act(T.lo[:, 0:L], P(PE), [PE], ["lo", "la", "lb"])
+    behind.append("cd2")
+    if CUT[0][0]:
+        flatten(L)
+    else:
+        cp(T.eo[:], T.Ef[:], ["Ef"], ["eo"])
     now[0] = 0
-    lane_list([(T.Bc0[:], T.c16[:], ["Bc0", "c16"])], "scq", qL, "qL", 0.0, 2 * L)
+    lane_list([(T.Bc0[:], T.c16[:], ["Bc0", "q0"])], "scq", qL, "qL", 0.0, 2 * L)
     for t in range(S):
         lists(t)
         if t == 0:
@@ -547,8 +647,8 @@ def rank_program(g, core, T, topo):
         environments()
         if t < S - 1:
             lane_list(code, "scq", qL, "qL", -93600.0, 3 * L)
-    mm("qf", PL, P(PL), code, 2 * L)
-    ts(T.qf[:], P(PL), -93600.0, None, A.add, None, [PL], ["qf"])
+            low_parts(t + 1)
+    tt(T.qf[:], P(PL), T.Yq[:], A.add, [PL, "Yq"], ["qf"])
     dmas("y", "so", [(T.yc[:], T.qf[0::16, :])], ["qf"], [], 32 * L)
     dmas("s", "so", [(T.ye[:], T.Ef[:])], ["Ef"], [], 512 * L)
 

from concourse.bass import DstId, RemoteDMATransfer
from concourse.mybir import AluOpType as A, ActivationFunctionType as F

N, C, L, R, M, S = 8, 1536, 192, 576, 4608, 5
CORES_ALL = 128
ALL = (L, [("s", 0, 56), ("v", 112, 192), ("s", 56, 112)], [("s", 0, 56), ("v", 128, 192), ("s", 56, 100), ("s", 100, 128)])
NONE = (0, [], [("v", 112, 192), ("s", 0, 72), ("s", 72, 112)])
SOME = (96, [("s", 0, 48), ("s", 48, 96)], [("v", 140, 192), ("s", 0, 48), ("s", 48, 96), ("s", 96, 140)])
CUT = [ALL, NONE, NONE, NONE, NONE]
FLAT = 3072
KEEP = 16 * 80
ROUTE = {"x": "split0", "e": "split1", "w": "split0"}
BIG = 262144.0
TURN = False
LATER = "xi"
EARLY = 768
START = {"v": "cci c0i rst ones i1 i2 i3 i4 i5 c0 rst2 I32 c6 c7 Blk c8 lt Ef c1i c1j c2i c2j owni ei ownj ej q0 pen c9 c24 c10 Perm",
         "s": "FL0 FL1 Ib Bc0 In ha FL2 FL3 FL4 FL5 lo Z0 Z1 Z2 Z3 Perw U0 U1 U2 U3 U4 U5 U6 U7"}
ORDER = {"v": "Yq Ye scq Ef qL eo Vg oh vo Pp G0 scn H0 tL X0 X1 X2 tq xi yes msk",
         "s": "Kg zg es G1 G2 H1 H2 Dg Ra",
         "p": "qL vb v0 vo es tL bind s0 z0 s1 z1 s2 z2 de dq msk apply qa",
         "g": "sente sentg sentw senth", "y": "Fh Fl out put"}
ORDERS = [dict(ORDER, v="scq qL kd0 Vg kd1 kd2 vo kd3 T1 oh kb eo0 Pp wide0 eo1 eo2 G1 scn X0 tL X1 X2 X3 tq xi wide1 yes wide2 wide3 wide4 wide5 wide6 msk",
               s="T0 T2 zg keep2 G0 G2 G3 Ip I0 I4 In0 Kg es kn kp J32 Id Wq Wqn Wk Dg Ra In1 In2 neg", p="qL vb vo v0 eo0 eo1 eo2 tL s0 z0 s1 z1 s2 z2 s3 z3 es bind msk dq de apply",
               g="sentg sentw sente near senth"),
          dict(ORDER, s="G1 G2 Kg zg H1 es H2 Dg Ra", p="qL vb v0 vo tL bind es s0 z0 s1 z1 s2 z2 de dq msk apply", g="sentg sente sentw senth"),
          ORDER, ORDER, dict(ORDER, v=ORDER["v"].replace("xi yes", "yes xi")),
          dict(ORDER, v="Ye Yq Ef qf")]
CYC, GAT, COL, CALL, WAKE, DMA, BYTE = 0.83e-3, 1.3, 0.42e-3, 0.05, 0.11, 1.6, 1 / 330e3
WAY = {"xi": 8.0, "ei": 14.0, "w": 6.0, "e": 9.0, "g": 2.2}

SCRATCH = {
    "XW": ("sbuf", [128, M], "bfloat16"), "EW": ("sbuf", [128, M], "float32"), "EU": ("sbuf", [128, M], "uint16"),
    "ES": ("sbuf", [128, 2 * (S - 1) * L], "float32"),
    "cdt": ("sbuf", [128, C], "int32"), "kc": ("sbuf", [128, L], "int32"), "kd4": ("sbuf", [128, 4 * L], "int32"),
    "kb": ("sbuf", [128, 4 * L], "bfloat16"),
    "cei": ("sbuf", [128, R], "int32"), "cci": ("sbuf", [128, R], "int32"),
    "e0i": ("sbuf", [128, L], "int32"), "c0i": ("sbuf", [128, L], "int32"),
    "keep": ("sbuf", [128, KEEP], "bfloat16"), "lt": ("sbuf", [128, 16], "float32"), "base": ("sbuf", [128, 3 * L], "bfloat16"),
    "FL": ("sbuf", [128, 32 * L], "bfloat16"), "U": ("sbuf", [128, 16 * 128], "bfloat16"), "Perw": ("sbuf", [128, 256], "bfloat16"),
    "hi": ("sbuf", [128, 2 * L], "bfloat16"), "lo": ("sbuf", [128, 2 * L], "bfloat16"),
    "sci": ("sbuf", [128, 8], "int32"), "sc": ("sbuf", [128, 32], "float32"),
    "wl": ("sbuf", [128, L], "bfloat16"),
    "qL": ("sbuf", [128, 16], "uint16"), "tL": ("sbuf", [128, 16], "uint16"),
    "eo": ("sbuf", [128, L], "uint16"), "vo": ("sbuf", [128, L], "uint16"),
}
for _n in ("TZ", "TK"):
    SCRATCH[_n] = ("sbuf", [128, C], "bfloat16")
for _n in ("G", "H", "X"):
    SCRATCH[_n] = ("sbuf", [128, 16 * L], "bfloat16")
for _n in ("col", "a16", "rst", "Ra", "Ye", "scn", "scq", "Ef", "qf", "Pp"):
    SCRATCH[_n] = ("sbuf", [128, L], "float32")
for _n in ("colb", "pen", "Vg", "zg", "Kg", "yes", "tq", "Dg", "msk", "ones", "neg"):
    SCRATCH[_n] = ("sbuf", [128, L], "bfloat16")
for _n in ("Yq", "c16"):
    SCRATCH[_n] = ("sbuf", [128, L], "float16")
for _n in ("dif", "g16", "I32", "J32", "Sh32", "Blk"):
    SCRATCH[_n] = ("sbuf", [128, 128], "float32")
for _n in ("Ib", "In", "IL", "Perm", "Bc0", "Wq", "Wqn", "Wk", "I0", "I4", "In0", "In1", "In2", "Id", "Ip", "k384", "kp", "kn", "kq"):
    SCRATCH[_n] = ("sbuf", [128, 128], "bfloat16")
for _k in range(8):
    SCRATCH["p%d" % _k] = ("psum", [128, 512], "float32")

PHASES = ["xi", "xj", "ei", "ej"]
for _t in range(S - 1):
    PHASES += ["w%d" % _t, "e%d" % _t]
GATE = {p: ("h" if p[0] == "e" else "g") + p[1] for p in PHASES[4:]}
SEMAPHORES = ["sv", "ss", "sp", "sg", "ls", "lx", "lw", "so", "dx", "dce", "dcc", "de", "dc", "dcd", "dc2", "dz", "dk", "dt", "dr", "sx", "fh", "fl"]
SEMAPHORES += ["f" + p for p in PHASES if p[0] == "e"] + sorted(set(GATE.values())) + ["aei%d" % _r for _r in range(N)]
SEMAPHORES += ["a" + p for p in PHASES if p not in ("xj", "ei", "ej")] + ["v%s_%d" % (p, k) for p in PHASES for k in range(2)]


def piece(T, ph, r):
    if ph[1] in "ij":
        lo = r * R + "ij".index(ph[1]) * R // 2
        return (T.XW if ph[0] == "x" else T.EU)[:, lo:lo + R // 2]
    lo = R * r + L * (int(ph[1]) % 3)
    return (T.XW if ph[0] == "w" else T.EW)[:, lo:lo + L]


def stage(T, ph, r, fan=False):
    if ph[1] in "ij":
        return piece(T, ph, r)
    t = int(ph[1])
    if fan:
        return T.EW[:, L * t:L * t + L]
    return (T.G if ph[0] == "w" else T.ES)[:, L * (2 * t + r % 2):L * (2 * t + r % 2 + 1)]


def arrival(T, ph, r):
    return T.sem["aei%d" % r if ph in ("ei", "ej") else "axi" if ph == "xj" else "a" + ph]


def routes(T, topo):
    cores = list(T.cores)
    chips = {}
    for c in cores:
        chips.setdefault(topo.chip(c), []).append(c)
    via = {}
    for ch, rk in chips.items():
        near = lambda c: (topo.die(c) != topo.die(rk[0]), c)
        out = [c for c in topo.cores_of(rk[0]) if c not in cores and all(topo.may_write(c, d) for d in cores)]
        for c in rk:
            via[("fan", cores.index(c))] = out[rk.index(c)]
        own = sorted([c for c in topo.cores_of(rk[0]) if c not in cores and c not in out], key=near)
        rel = sorted([c for c in range(CORES_ALL) if topo.mates(topo.chip(c), ch) and c not in cores
                      and all(topo.may_write(c, d) for d in rk)], key=near)
        src = [r for r in range(N) if topo.chip(cores[r]) != ch]
        for ph in PHASES:
            mode = ROUTE[ph] if ph in ROUTE else ROUTE[ph[0]]
            for n, r in enumerate(src):
                if mode == "own":
                    v = (own[-1:] + out)[n // 2]
                elif mode == "split0":
                    v = own[n // 2] if r % 2 == 0 else rel[n // 2]
                else:
                    v = own[len(own) - 1 - n // 2] if r % 2 == 1 else rel[len(rel) - 1 - n // 2]
                via[(ph, r, ch)] = v
    return chips, via


def turn(chips, chip, r):
    order = list(chips)
    k = order.index(chip)
    rest = order[k + 1:] + order[:k]
    return rest if TURN else [c for c in order if c != chip]


def bits(m):
    return bin(m).count("1")


def masks(topo, core, cores):
    sib = [c for c in cores if c != core and topo.chip(c) == topo.chip(core)][0]
    far = [c for c in cores if topo.chip(c) != topo.chip(core)][0]
    return topo.mask(core, far), topo.mask(core, sib) & ~topo.mask(core, far)


def dst_id(topo, c):
    a = topo.addr(c)
    return DstId(rid=a[0], pnc=a[1])


def write(topo, to, mask, sem, src, dst):
    return RemoteDMATransfer(dst_ids=[dst_id(topo, d) for d in to], dma_engine_mask=mask, remote_sem=sem, src=src, dsts=[dst for d in to])


def writers(T, topo, chips, via, ph, core):
    cores = list(T.cores)
    sib = [c for c in chips[topo.chip(core)] if c != core][0]
    return ({via[(ph, r, topo.chip(core))] for r in range(N) if topo.chip(cores[r]) != topo.chip(core)}
            | {sib if ph[0] == "w" else via[("fan", cores.index(sib))]})


def helper_program(g, core, T, topo, chips, via):
    cores = list(T.cores)
    sent, free = 0, set()

    def call(transfer, mask):
        g.remote_dma_fused([transfer], local_sem=T.sem.ls)
        return bits(mask)

    def cleared(ph):
        if ph in GATE and GATE[ph] not in free:
            g.wait_ge(T.sem[GATE[ph]], len([c for c in cores if core in writers(T, topo, chips, via, ph, c)]))
            free.add(GATE[ph])

    for ph in PHASES:
        mine = [r for r in range(N) if ph[0] == "e" and via[("fan", r)] == core]
        for r in mine:
            off, on = masks(topo, cores[r], cores)
            g.wait_ge(T.sem["f" + ph], bits(on))
            out = [via[(ph, r, ch)] for ch in turn(chips, topo.chip(core), r)]
            sent += call(write(topo, out, off, T.sem["v%s_%d" % (ph, r % 2)], stage(T, ph, r, True), stage(T, ph, r)), off)
            cleared(ph)
            sent += call(write(topo, [c for c in chips[topo.chip(core)] if c != cores[r]], on, arrival(T, ph, r),
                               stage(T, ph, r, True), piece(T, ph, r)), on)
        for r in range(N):
            for ch, rk in chips.items():
                if via.get((ph, r, ch)) == core:
                    g.wait_ge(T.sem["v%s_%d" % (ph, r % 2)], bits(topo.mask(cores[r], core)))
                    cleared(ph)
                    m = topo.mask(core, rk[0])
                    sent += call(write(topo, rk, m, arrival(T, ph, r), stage(T, ph, r), piece(T, ph, r)), m)
    if sent:
        g.wait_ge(T.sem.ls, sent)


def lay_out(calls):
    after = [[] for _ in calls]
    for n, c in enumerate(calls):
        for p, lag in c["pre"].items():
            after[p].append((n, lag))
    left, order = [len(c["pre"]) for c in calls], [n for n, c in enumerate(calls) if not c["pre"]]
    for n in order:
        for k, lag in after[n]:
            left[k] -= 1
            if not left[k]:
                order.append(k)
    assert len(order) == len(calls)
    chain = [0.0] * len(calls)
    for n in reversed(order):
        chain[n] = calls[n]["busy"] + calls[n]["lat"] + max([lag + chain[k] for k, lag in after[n]] + [0.0])
    taken = {}

    def place(queue, t, d):
        slots = taken.setdefault(queue, [])
        k = 0
        while k < len(slots) and slots[k][0] < t + d:
            t = max(t, slots[k][1])
            k += 1
        slots.insert(k, (t, t + d))
        return t

    start, end = {}, {}
    todo = sorted(range(len(calls)), key=lambda n: (-chain[n], n))
    while todo:
        n = todo.pop([all(p in end for p in calls[k]["pre"]) for k in todo].index(True))
        c = calls[n]
        t = max([end[p] + lag for p, lag in c["pre"].items()] + [0.0])
        if c["bytes"]:
            t = place("dma", t + c["busy"], c["bytes"] * BYTE) - c["busy"]
        start[n] = place(c["q"], t, c["busy"])
        end[n] = start[n] + c["busy"] + c["lat"] + c["bytes"] * BYTE
    return sorted(range(len(calls)), key=lambda n: (start[n], n))


def rank_program(g, core, T, topo):
    chips, via = routes(T, topo)
    rank = T.rank_of(core)
    if rank is None:
        helper_program(g, core, T, topo, chips, via)
        return
    cores = list(T.cores)
    chip = topo.chip(core)
    sib = [c for c in chips[chip] if c != core][0]
    off_mask, on_mask = masks(topo, core, cores)

    Q = {"v": g.vector, "s": g.scalar, "p": g.tensor, "g": g, "y": g.sync}
    calls, wrote, read, arrive, behind, tags, now = [], {}, {}, {}, [], {}, [None]

    def follow(n, p):
        if p not in calls[n]["pre"]:
            calls[n]["pre"][p] = -calls[p]["lat"] - calls[p]["bytes"] * BYTE
            calls[n]["soft"].add(p)

    def note(q, fn, rd, wr, sem, inc, busy, lat=0.0, nbytes=0, tag=None):
        pre, ext, soft = {}, [], set()
        for r in rd:
            if r in arrive:
                ext.append(arrive[r][:2])
                for p in wrote[arrive[r][3]]:
                    if p not in pre:
                        soft.add(p)
                    pre[p] = max(pre.get(p, 0.0), arrive[r][2])
            else:
                for p in wrote[r]:
                    pre[p] = max(pre.get(p, 0.0), WAKE)
                    soft.discard(p)
        for r in wr:
            for p in wrote.get(r, []) + read.get(r, []):
                pre[p] = max(pre.get(p, 0.0), WAKE)
                soft.discard(p)
        n = len(calls)
        tags[(now[0], q, tag or (wr[0] if wr else None))] = n
        calls.append({"q": q, "fn": fn, "pre": pre, "soft": soft, "ext": ext, "sem": sem, "inc": inc, "busy": busy, "lat": lat, "bytes": nbytes})
        for r in behind:
            follow(n, wrote[r][0])
        del behind[:]
        for r in rd:
            read.setdefault(r, []).append(n)
        for r in wr:
            wrote[r], read[r] = [n], []

    def issue():
        count, token, seen = {}, {}, {k: {} for k in Q}
        for q in ORDER:
            line = [tags[(None, q, x)] for x in START.get(q, "").split() if (None, q, x) in tags]
            line += [tags[(None if (t, q, x) not in tags else t, q, x)] for t in range(S + 1) for x in ORDERS[t][q].split()
                     if (t, q, x) in tags or (t == 0 and (None, q, x) in tags)]
            for p, n in zip(line, line[1:]):
                follow(n, p)
        for n in lay_out(calls):
            c = calls[n]
            for s, v in dict(sorted([token[p] for p in c["pre"] if p in token and p not in c["soft"]] + c["ext"])).items():
                if seen[c["q"]].get(s, 0) < v:
                    Q[c["q"]].wait_ge(T.sem[s], v)
                    seen[c["q"]][s] = v
            c["fn"](Q[c["q"]])
            count[c["sem"]] = count.get(c["sem"], 0) + c["inc"]
            if c["sem"] not in ("so", "ls"):
                token[n] = (c["sem"], count[c["sem"]])
        return count

    def op(e, fn, rd, wr, cy):
        wr = list(wr) + [r for r in rd if r[0] == "p" and r[1:].isdigit()]
        note(e, lambda q: fn(q).then_inc(T.sem["s" + e], 1), rd, wr, "s" + e, 1, CALL + max(64, cy) * CYC)

    def mm(tag, b, out, terms, cy, first=True, last=True):
        def fn(q):
            for n, (x, y, names) in enumerate(terms):
                ins = q.matmul(out, x, y, first and n == 0, last and n == len(terms) - 1)
            ins.then_inc(T.sem.sp, 1)
        note("p", fn, [r for x, y, names in terms for r in names], [b], "sp", 1, cy * COL, 0.1, tag=tag)

    def dmas(e, sem, pairs, rd, wr, nbytes):
        def fn(q):
            for o, i in pairs:
                q.dma_start(o, i).then_inc(T.sem[sem], 16)
        note(e, fn, rd, wr, sem, 16 * len(pairs), 0.06 * len(pairs), DMA, nbytes)

    def remote(transfers, rd, wr, engines, nbytes, ls="ls", more=0.0):
        note("g", lambda q: q.remote_dma_fused(transfers, local_sem=T.sem[ls]), rd, wr, ls, engines, 0.35 + more, 0.8, nbytes, wr[0][:5])

    def send(ph, src, rd):
        if ph[0] == "e":
            remote([write(topo, [via[("fan", rank)]], on_mask, T.sem["f" + ph], src, stage(T, ph, rank, True))], rd, ["sent" + ph],
                   bits(on_mask), 256 * R)
            return
        out = write(topo, [via[(ph, rank, ch)] for ch in turn(chips, chip, rank)], off_mask, T.sem["v%s_%d" % (ph, rank % 2)], src, stage(T, ph, rank))
        near = write(topo, [sib], on_mask, arrival(T, ph, rank), src, src)
        if ph[0] == "x":
            remote([out, near], rd, ["sent" + ph], bits(off_mask) + bits(on_mask), 256 * R * 3, "lx", 2.0 if ph == "xi" else 0.0)
        elif ph == "w0":
            remote([out], rd, ["sent" + ph], bits(off_mask), 256 * L * 6, "lw")
            remote([near], rd + ["ing" + ph[1]], ["near"], bits(on_mask), 0)
        else:
            remote([out, near], rd + ["ing" + ph[1]], ["sent" + ph], bits(off_mask) + bits(on_mask), 256 * L * 6, "lw")

    def clear(ph, rd):
        to = sorted(writers(T, topo, chips, via, ph, core), key=lambda d: (topo.chip(d) == chip, d))
        engines = topo.engines(core, sib)
        away = len([d for d in to if topo.chip(d) != chip])
        pick = engines[:away] + engines[len(engines) - (len(to) - away):]
        remote([RemoteDMATransfer(dst_ids=[dst_id(topo, d)], dma_engine_mask=1 << e, remote_sem=T.sem[GATE[ph]]) for d, e in zip(to, pick)],
               rd, ["sent" + GATE[ph]], len(to), 0)

    for ph in PHASES:
        each = {r: bits(on_mask if cores[r] == sib else topo.mask(via[(ph, r, chip)], core)) for r in range(N) if r != rank}
        if ph == "ei":
            for r, n in each.items():
                arrive["inei%d" % r] = ("aei%d" % r, 2 * n, WAY[ph] / (2 if cores[r] == sib else 1), "sentej")
        elif ph == "xi":
            arrive["inxi"] = ("axi", 2 * sum(each.values()), WAY[ph], "sentxj")
        elif ph[1] != "j":
            arrive["in" + ph] = ("a" + ph, sum(each.values()), WAY[ph[0]] - 0.8, "sent" + ph)
    for t in range(S - 1):
        arrive["ing%d" % t] = ("g%d" % t, 1, WAY["g"] - 0.8, "sentg%d" % t)

    def ts(out, in0, s1, s2, o0, o1, rd, wr, cy=L):
        if s2 is None:
            op("v", lambda q: q.tensor_scalar(out, in0, s1, None, o0), rd, wr, cy)
        else:
            op("v", lambda q: q.tensor_scalar(out, in0, s1, s2, o0, o1), rd, wr, cy)

    def tt(out, in0, in1, o, rd, wr, cy=L):
        op("v", lambda q: q.tensor_tensor(out, in0, in1, o), rd, wr, cy)

    def cp(out, in0, rd, wr, cy=L):
        op("v", lambda q: q.tensor_copy(out, in0), rd, wr, cy)

    def ms(ap, val, wr, cy=64):
        op("v", lambda q: q.memset(ap, val), [], wr, cy)

    def act(out, in0, rd, wr, cy=L, bias=None, scale=1.0):
        if bias is None and isinstance(scale, float) and scale == 1.0:
            op("s", lambda q: q.activation(out, in0, F.Copy), rd, wr, cy)
        else:
            op("s", lambda q: q.activation(out, in0, F.Identity, bias=0.0 if bias is None else bias, scale=scale), rd, wr, cy)

    def iota(out, pat, base, cm, wr, n, flt=True):
        if flt:
            op("g", lambda q: q.iota(out, pat, base, cm, allow_small_or_imprecise_dtypes=True), [], wr, 100 + 2 * n)
        else:
            op("g", lambda q: q.iota(out, pat, base, cm), [], wr, 100 + 2 * n)

    def scan(out, d0, d1, o0, rd, wr, cy):
        op("v", lambda q: q.tensor_tensor_scan(out, d0, d1, 0.0, o0, A.max), rd, wr, cy)

    copy = {"v": cp, "s": act}
    sc = lambda k: T.sc[:, k:k + 1]
    lt = lambda k: T.lt[:, k:k + 1]
    qL, tL = T.qL[:, 0:L // 16], T.tL[:, 0:L // 16]
    PS, PZ, PV, PL, PE, P0, PR, PD = ["p%d" % k for k in range(8)]
    P = lambda b: T[b][:, 0:L]
    GL = GAT * L

    dmas("y", "dx", [(T.XW[:, rank * R:(rank + 1) * R], T.x0[:])], [], ["xi"], 256 * R)
    dmas("y", "dce", [(T.cei[:], T.ce0[:])], [], ["cei"], 512 * R)
    ms(T.cci[:], 0, ["cci"], R)
    ms(T.c0i[:], 0, ["c0i"], L)
    dmas("y", "dcc", [(T.cci[j::16, :], T.cc0[:]) for j in range(4)], [], ["cci"], 128 * R)
    dmas("s", "de", [(T.e0i[:], T.e0[:])], [], ["e0i"], 512 * L)
    send("xi", piece(T, "xi", rank), ["xi"])
    behind.append("sentxi")
    send("xj", piece(T, "xj", rank), ["xi"])
    loads = [("dc", [(T.c0i[0::16, :], T.c0[:])], [], "c0i", 32 * L),
             ("dk", [(T.kc[:, 0:L // 2], T.ky[:]), (T.kc[:, L // 2:L], T.kid[:])], [], "kc", 64 * C),
             ("dcd", [(T.cdt[:, 0:EARLY], T.cd[:, 0:EARLY])], [], "cd1", 512 * EARLY),
             ("dc2", [(T.cdt[:, EARLY:C], T.cd[:, EARLY:C])], [LATER], "cd2", 512 * (C - EARLY)),
             ("dz", [(T.TZ[:], T.zt[:])], ["sentxj"], "TZ", 256 * C)]
    for n, (sem, pairs, rd, name, nbytes) in enumerate(loads):
        behind.append(loads[n - 1][3] if n else "cci")
        dmas("y", sem, pairs, rd, [name], nbytes)
    wrote["cdt"] = wrote["cd1"] + wrote["cd2"]
    iota(T.sci[:, 0:1], [[0, 1]], 0, 1, ["pi"], 1, flt=False)
    iota(T.dif[:], [[1, 128]], 0, -1, ["dif"], 128)
    iota(T.g16[:], [[1, 8], [0, 16]], 0, 0, ["g16"], 128)
    iota(T.a16[:], [[0, L // 16], [1, 16]], 0, 0, ["a16"], L)
    iota(T.col[:], [[1, L]], 0, 0, ["col"], L)
    ts(T.sci[:, 1:2], T.sci[:, 0:1], 15, None, A.bitwise_and, None, ["pi"], ["i1"], 1)
    ts(T.sci[:, 2:3], T.sci[:, 0:1], 3, None, A.bitwise_and, None, ["pi"], ["i2"], 1)
    ts(T.sci[:, 3:4], T.sci[:, 0:1], 1, None, A.bitwise_and, None, ["pi"], ["i3"], 1)
    ts(T.sci[:, 4:5], T.sci[:, 0:1], 1, 1, A.logical_shift_right, A.bitwise_and, ["pi"], ["i4"], 1)
    ts(T.sci[:, 5:6], T.sci[:, 0:1], 4, None, A.logical_shift_right, None, ["pi"], ["i5"], 1)
    cp(T.sc[:, 0:6], T.sci[:, 0:6], ["pi", "i1", "i2", "i3", "i4", "i5"], ["c0"], 1)
    small = [(6, 3, -0.875, 1.0, A.mult, A.add), (7, 4, -63.0 / 64.0, 1.0, A.mult, A.add),
             (8, 6, sc(7), 8192.0, A.mult, A.mult),
             (9, 2, 3.75, sc(0), A.mult, A.add), (10, 1, -0.75, sc(9), A.mult, A.add),
             (14, 3, 7.0, 1.0, A.mult, A.add), (15, 4, 63.0, 1.0, A.mult, A.add),
             (16, 14, sc(15), lt(4), A.mult, A.mult),
             (17, 14, sc(15), lt(8), A.mult, A.mult), (18, 17, sc(16), None, A.subtract, None)]
    ts(T.lt[:], T.col[:, 0:16], sc(1), None, A.is_gt, None, ["col", "c0"], ["lt"], 1)
    uses = {8: ["c7"], 10: ["c9"], 16: ["c15", "lt"], 17: ["c15", "lt"], 18: ["c16"]}
    for k, src, s1, s2, o0, o1 in small:
        ts(sc(k), sc(src), s1, s2, o0, o1, ["c0"] + uses.get(k, []) + (["c%d" % src] if src > 5 else []), ["c%d" % k], 1)
    ts(T.I32[:], T.dif[:], 0.0, None, A.is_equal, None, ["dif"], ["I32"], 128)
    for name, scale in (("Ib", 1.0), ("In", -1.0), ("Id", -8192.0), ("Ip", 8192.0), ("J32", -1.0)):
        act(T[name][:], T.I32[:], ["I32"], [name], 128, scale=scale)
    ts(T.pen[:], T.a16[:], sc(1), -BIG, A.not_equal, A.mult, ["a16", "c0"], ["pen"])
    act(T.colb[:], T.col[:], ["col"], ["colb"])
    kinds = [c for n, c in enumerate(CUT) if c not in CUT[:n]]
    for k, (nt, names, pieces) in enumerate(kinds):
        for a, b, step in [(0, nt, 1.0)] + [(a, b, 16.0) for e, a, b in pieces if a >= nt]:
            if a < b:
                act(T.base[:, k * L + a:k * L + b], T.col[:, 0:b - a], ["col"], ["base%d" % k], b - a, scale=step)
    ts(T.Perm[:], T.col[:, 0:128], sc(10), None, A.is_equal, None, ["col", "c10"], ["Perm"], 128)
    act(T.Perw[:, 0:128], T.Perm[:], ["Perm"], ["Perw"], 128, scale=float(L))
    if CUT[-1][0]:
        act(T.Perw[:, 128:256], T.Perm[:], ["Perm", "Perw"], ["Per2", "Perw"], 128, scale=2.0 * CUT[-1][0])
        act(T.IL[:], T.I32[:], ["I32"], ["IL"], 128, scale=float(CUT[-1][0]))
    ts(T.Blk[:], T.g16[:], sc(5), None, A.is_equal, None, ["g16", "c0"], ["Blk"], 128)
    for name, col, nm in (("Bc0", lt(1), "lt"), ("Wq", sc(16), "c16"), ("Wk", sc(18), "c18")):
        act(T[name][:], T.Blk[:], ["Blk", nm], [name], 128, scale=col)
    act(T.Wqn[:], T.Wq[:], ["Wq"], ["Wqn"], 128, scale=-1.0)
    ts(T.Sh32[:], T.dif[:], 1.0, lt(15), A.is_equal, A.mult, ["dif", "lt"], ["Sh32"], 128)
    act(T.I0[:], T.I32[:], ["I32", "lt"], ["I0"], 128, scale=lt(1))
    act(T.I4[:], T.Ip[:], ["Ip", "lt"], ["I4"], 128, scale=lt(4))
    for b in range(3):
        act(T["In%d" % b][:], T.I0[:], ["I0"], ["In%d" % b], 128, scale=float(rank * R + L * b))
    ms(T.ones[:], 1.0, ["ones"], L // 2)
    act(T.neg[:], T.ones[:], ["ones"], ["neg"], scale=-1.0)
    ms(T.rst[:], 0.0, ["rst"], L)
    ms(T.rst[:, 0::16], -4.0 * BIG, ["rst2", "rst"])
    for name, value in (("k384", 384.0), ("kp", 10240.0), ("kn", -10240.0)):
        act(T[name][:], T.ones[:, 0:128], ["ones"], [name], 128, scale=value)
    ms(T.kq[0:64, :], 1456.0, ["kq1"])
    ms(T.kq[64:128, :], 6.5, ["kq2"])
    lo = rank * R
    for k, h in enumerate("ij"):
        c, own = slice(k * R // 2, (k + 1) * R // 2), T.EW[:, lo + k * R // 2:lo + (k + 1) * R // 2]
        ts(T.cci[:, c], T.cci[:, c], sc(8), None, A.mult, None, ["cci", "c8"], ["c1" + h], R // 2)
        ts(T.cci[:, c], T.cci[:, c], 7 * 8192, None, A.bitwise_and, None, ["c1" + h], ["c2" + h], R // 2)
        tt(own, T.cci[:, c], T.cei[:, c], A.add, ["c2" + h, "cei"], ["own" + h], R)
        cp(piece(T, "e" + h, rank), own, ["own" + h], ["e" + h], R // 2)
        behind.append("sentxj" if k == 0 else "sentei")
        send("e" + h, piece(T, "e" + h, rank), ["e" + h])
    wrote["EW%d" % rank] = wrote["owni"] + wrote["ownj"]
    read["EW%d" % rank] = read["owni"] + read["ownj"]
    for k in range(FLAT // 512):
        act(T.FL[:, 512 * k:512 * (k + 1)], T.XW[:, lo:lo + 512], ["xi"], ["FL%d" % k], 512)
    wrote["Fh"] = wrote["Fl"] = [p for k in range(FLAT // 512) for p in wrote["FL%d" % k]]
    for k in range(4):
        act(T.U[:, 512 * k:512 * (k + 1)], T.XW[:, lo:lo + 512], ["xi"], ["Z%d" % k], 512, scale=0.0)
    wrote["Z"] = [p for k in range(4) for p in wrote["Z%d" % k]]
    ts(T.sc[:, 24:32], T.col[:, 0:8], sc(5), lt(2), A.is_equal, A.mult, ["col", "c0", "lt"], ["c24"], 1)
    for k in range(8):
        act(T.U[:, 16 * k:16 * k + 15 * 129 + 1:129], T.ones[:, 0:16], ["ones", "c24", "Z"], ["U%d" % k], 16, scale=sc(24 + k))
    wrote["U"] = [p for k in range(8) for p in wrote["U%d" % k]]
    now[0] = 0
    for j in range(4):
        ts(T.kd4[:, j * L:(j + 1) * L], T.kc[:], 3 * j, 7, A.logical_shift_right, A.bitwise_and, ["kc"], ["kd%d" % j])
    cp(T.kb[:], T.kd4[:], ["kd%d" % j for j in range(4)], ["kb"], 4 * L)
    now[0] = None
    behind.append("sentej")
    iota(T.keep[:], [[0, KEEP]], 1, 0, ["keep"], KEEP)
    behind.append("keep")
    iota(T.TK[:], [[0, C]], 0, 0, ["TK"], C)
    now[0] = 0
    act(T.keep[:, 0::4], T.keep[:, 1::4], ["keep"], ["keep2", "keep"], KEEP // 4, scale=0.0)
    now[0] = None
    behind.append("TZ")
    dmas("y", "dt", [(T.TK[4 * k + j::16, :], T.kb[:, j * L + k * L // 2:j * L + (k + 1) * L // 2]) for j in range(4) for k in range(2)],
         ["kb"], ["TK"], 128 * 4 * L * 6)

    def widen():
        way = lambda r: (cores[r] != sib, cores[r] != sib and topo.chip(via[("ei", r, chip)]) != chip, r)
        for n, r in enumerate(sorted([r for r in range(N) if r != rank], key=way)):
            cp(T.EW[:, r * R:(r + 1) * R], T.EU[:, r * R:(r + 1) * R], ["inei%d" % r], ["wide%d" % n, "EW%d" % r], R)

    def lane_list(terms, buf, out, name, shift, cy):
        mm(name, PL, P(PL), [(T.Ib[:], T.pen[:], ["Ib", "pen"])] + terms, cy)
        scan(T[buf][:], T.rst[:], P(PL), A.add, ["rst", PL], [buf], L)
        ts(out, T[buf][:, 15::16], shift, None, A.add, None, [buf], [name], 1)

    def environments():
        tt(T.Ye[:], T[PD][:, 0:L], T.msk[:], A.mult, [PD, "msk"], ["Ye"])
        tt(T.Ef[:], P(PE), T.Ye[:], A.add, [PE, "Ye"], ["Ef"])
        if now[0] < S:
            recut(now[0])
            nt = CUT[now[0]][0]
            cp(T.eo[:, nt:L], T.Ef[:, nt:L], ["Ef"], ["eo"], L - nt)

    def recut(t):
        for kinds in (["eo"], ["G"], ["H", "T"], ["X"]):
            names = [k + n for k in kinds for n in ("", "0", "1", "2", "3", "4")]
            users = [p for r in names for p in wrote.get(r, []) + read.get(r, [])]
            for r in names if CUT[t] != CUT[t - 1] else []:
                wrote[r], read[r] = [], list(users)

    def flatten(n):
        dmas("y", "fh", [(T.FL[0::16, 0:16 * n], T.hi[:, 0:n])], ["ha", "hb"], ["Fh"], 256 * n)
        dmas("y", "fl", [(T.FL[1::16, 0:16 * n], T.lo[:, 0:n])], ["la", "lb"], ["Fl"], 256 * n)

    def lists(t):
        nt, names, pieces = CUT[t]
        k = kinds.index(CUT[t])
        cp(T.Vg[:], T.cdt[:, 0:C].indirect(qL), ["cdt", "qL"], ["Vg"], GL)
        mm("vb", PV, P(PV), [(T.Ib[:], T.base[:, k * L:(k + 1) * L], ["Ib", "base%d" % k])], L, last=False)
        if t and nt:
            mm("vm", PV, T[PV][:, 0:nt], [(T.IL[:], T.msk[:, 0:nt], ["IL", "msk"])], nt, first=False, last=False)
        parts = [(T.Perw[:, 128 * min(t, 1):128 * min(t, 1) + 128], 0, nt), (T.Perm[:], nt, L)]
        parts = [x for x in parts if x[1] < x[2]]

        def picks(q):
            for n, (m, a, b) in enumerate(parts):
                ins = q.matmul(T[PV][:, a:b], m, T.Vg[:, a:b], False, n == len(parts) - 1)
            ins.then_inc(T.sem.sp, 1)
        note("p", picks, ["Perw", "Perm", "Vg"], [PV], "sp", 1, L * COL, 0.1, tag="vo")
        cp(T.vo[:], P(PV), [PV], ["vo"])
        for n, (e, a, b) in enumerate(names):
            copy[e](T.H[:, 16 * a:16 * b], T.FL[:, 0:(32 if t else 16) * nt].indirect(T.vo[:, a:b]), ["Fh", "Fl", "vo"], ["T%d" % n], 16 * GAT * (b - a))
            bank = (PS, PZ)[n % 2]
            mm("eo%d" % n, bank, T[bank][:, a:b],
               [(T.U[:, 128 * k:128 * k + 128], T.H[:, 16 * a + k:16 * b:16], ["U", "T%d" % n]) for k in range(16)], 16 * max(64, b - a))
            cp(T.eo[:, a:b], T[bank][:, a:b], [bank], ["eo%d" % n], b - a)
        mm("v0", P0, P(P0), [(T.Bc0[:], T.Vg[:], ["Bc0", "Vg"])], L)
        ts(P(P0), P(P0), sc(1), None, A.is_equal, None, [P0, "c0"], ["oh"])
        tt(T.Pp[:], P(P0), T.Ef[:], A.mult, [P0, "Ef"], ["Pp"])
        lane_list([(T.Blk[:], T.Pp[:], ["Blk", "Pp"])], "scn", tL, "tL", 0.0, 5 * L)
        act(T.zg[:], T.TZ[:, 0:C].indirect(qL), ["TZ", "qL"], ["zg"], GL)
        act(T.Kg[:], T.TK[:, 0:C].indirect(qL), ["TK", "qL"], ["Kg"], GL)
        if t < S - 1:
            es = T.ES[:, t * L:(t + 1) * L]
            mm("es", PR, P(PR), [(T.I32[:], T.Ef[:], ["I32", "Ef"]), (T.I4[:], T.Kg[:], ["I4", "Kg"])], 5 * L)
            act(es, P(PR), [PR], ["es", "es%d" % t])
            send("e%d" % t, es, ["es%d" % t])
        b = "In%d" % (t % 3)
        mm("bind", PD, T[PD][:, 0:L], [(T.kn[:], T.ones[:], ["kn", "ones"]), (T.I0[:], T.colb[:], ["I0", "colb"]), (T[b][:], T.ones[:], [b]),
                                       (T.Sh32[:], T.Ef[:], ["Sh32", "Ef"])], 7 * L, last=False)

    def closure(t):
        win = T.EW[:, 0:M].indirect(tL)
        rd = ["tL"] + ["EW%d" % r for r in range(N)] + ["ine%d" % u for u in range(t)]
        act(T.Dg[:], win, rd, ["Dg"], GL, bias=160.0 - 0.28125, scale=1.0 / 8192.0)
        act(T.Ra[:], win, rd, ["Ra"], GL)
        if t < S - 1:
            clear("e%d" % t, ["Dg", "Ra"])
            dmas("y", "dr", [(piece(T, "e%d" % t, rank), T.ES[:, t * L:(t + 1) * L])], ["es%d" % t], ["put", "EW%d" % rank], 512 * L)
        mm("dq", PR, P(PR), [(T.kq[:], T.ones[:], ["kq1", "kq2", "ones"]), (T.Wk[:], T.Kg[:], ["Wk", "Kg"]),
                             (T.Wqn[:], T.Dg[:], ["Wqn", "Dg"])], 3 * L)
        mm("de", PD, T[PD][:, 0:L], [(T.Ip[:], T.Dg[:], ["Ip", "Dg"]), (T.J32[:], T.Ra[:], ["J32", "Ra"])], 5 * L, first=False)
        mm("apply", PE, P(PE), [(T.kp[:], T.ones[:], ["kp", "ones"]), (T.Id[:], T.Dg[:], ["Id", "Dg"]), (T.I32[:], T.Ra[:], ["I32", "Ra"])],
           6 * L)
        if t == S - 1:
            mm("qa", PL, P(PL), [(T.kq[:], T.neg[:], ["kq1", "kq2", "neg"]), (T.Wq[:], T.Dg[:], ["Wq", "Dg"])], 2 * L)
        nt = CUT[t + 1][0] if t < S - 1 else 0
        if nt:
            b = "In%d" % (t % 3)
            bind = [(T.I0[:], T.colb[:, 0:nt], ["I0", "colb"]), (T[b][:], T.ones[:, 0:nt], [b, "ones"]), (T.Sh32[:], T.Ef[:, 0:nt], ["Sh32", "Ef"])]
            mm("hb", P0, T[P0][:, 0:nt], bind, 6 * nt)
            act(T.hi[:, nt:2 * nt], T[P0][:, 0:nt], [P0], ["hb"], nt)
            mm("lb", P0, T[P0][:, 0:nt], bind + [(T.In[:], T.hi[:, nt:2 * nt], ["In", "hb"])], 7 * nt)
            act(T.lo[:, nt:2 * nt], T[P0][:, 0:nt], [P0], ["lb"], nt)
            act(T.hi[:, 0:nt], T[PE][:, 0:nt], [PE], ["ha"], nt)

    def low_parts(t):
        nt = CUT[t][0]
        if nt:
            mm("la", PS, T[PS][:, 0:nt], [(T.kp[:], T.ones[:, 0:nt], ["kp", "ones"]), (T.Id[:], T.Dg[:, 0:nt], ["Id", "Dg"]),
                                          (T.I32[:], T.Ra[:, 0:nt], ["I32", "Ra"]), (T.In[:], T.hi[:, 0:nt], ["In", "ha"])], 7 * nt)
            act(T.lo[:, 0:nt], T[PS][:, 0:nt], [PS], ["la"], nt)
            flatten(2 * nt)

    def values(t):
        rd = ["xi", "inxi"] + ["inw%d" % u for u in range(t)]
        nt, names, pieces = CUT[t]
        for n, (e, a, b) in enumerate(pieces):
            lists = ["eo"] if a >= nt else ["eo%d" % k for k, (e2, a2, b2) in enumerate(names) if a2 < b and a < b2]
            copy[e](T.G[:, 16 * a:16 * b], T.XW[:, 0:M].indirect(T.eo[:, a:b]), rd + lists, ["G%d" % n], 16 * GAT * (b - a))
        if t < S - 1:
            clear("w%d" % t, ["G%d" % n for n in range(len(pieces))])
        for n, (e, a, b) in enumerate(pieces):
            src, name = T.G, "G%d" % n
            if a >= nt:
                src, name = T.H, "H%d" % n
                copy[e](T.H[:, 16 * a:16 * b], T.G[:, 16 * a:16 * b].indirect(T.vo[:, a:b]), ["G%d" % n, "vo"], [name], 16 * GAT * (b - a))
            scan(T.X[:, 16 * a:16 * b], T.keep[:, 0:16 * (b - a)], src[:, 16 * a:16 * b], A.mult, ["keep", name], ["X%d" % n], 8 * (b - a))
            four = [(T.k384[:], T.ones[:, a:b], ["k384", "ones"])] + [
                (T.Ib[:], T.X[:, 16 * a + 4 * p + 3:16 * b:16], ["Ib", "X%d" % n]) for p in range(4)]
            mm("s%d" % n, PS, T[PS][:, a:b], four, 5 * max(64, b - a))
            mm("z%d" % n, PZ, T[PZ][:, a:b], [(T.In[:], T.zg[:, a:b], ["In", "zg"])] + four, 6 * max(64, b - a))
        w = piece(T, "w%d" % t, rank) if t < S - 1 else T.wl[:]
        ts(T.tq[:], P(PS), -127.5, None, A.add, None, [PS], ["tq"])
        tt(w, P(PS), T.tq[:], A.subtract, [PS, "tq"], ["xi"])
        if t < S - 1:
            send("w%d" % t, w, ["xi"])
        dmas("y", "so" if t else "sx", [(T.yx[:, t * L:(t + 1) * L], w)], ["xi"] + (["sentw%d" % t] if t < S - 1 else []), ["out"], 256 * L)
        tt(T.yes[:], P(PZ), T.tq[:], A.is_ge, [PZ, "tq"], ["yes"])
        mm("msk", PV, P(PV), [(T.ones[:, 0:128], T.yes[:], ["ones", "yes"])], L)
        ts(T.msk[:], P(PV), 59.5, None, A.is_ge, None, [PV], ["msk"])

    cp(T.c16[:], T.c0i[:], ["c0i"], ["q0"])
    cp(T.Ef[:], T.e0i[:], ["e0i"], ["Ef"])
    act(T.hi[:, 0:L], T.Ef[:], ["Ef"], ["ha", "hb"])
    mm("lo", PE, P(PE), [(T.I32[:], T.Ef[:], ["I32", "Ef"]), (T.In[:], T.hi[:, 0:L], ["In", "ha"])], 5 * L)
    act(T.lo[:, 0:L], P(PE), [PE], ["lo", "la", "lb"])
    behind.append("cd2")
    if CUT[0][0]:
        flatten(L)
    else:
        cp(T.eo[:], T.Ef[:], ["Ef"], ["eo"])
    now[0] = 0
    lane_list([(T.Bc0[:], T.c16[:], ["Bc0", "q0"])], "scq", qL, "qL", 0.0, 2 * L)
    for t in range(S):
        lists(t)
        if t == 0:
            values(t)
            widen()
            closure(t)
        else:
            closure(t)
            values(t)
        now[0] = t + 1
        tt(T.Yq[:], P(PR), T.msk[:], A.mult, [PR, "msk"], ["Yq"])
        code = [(T.Wq[:], T.Dg[:], ["Wq", "Dg"]), (T.Ib[:], T.Yq[:], ["Ib", "Yq"])]
        environments()
        if t < S - 1:
            lane_list(code, "scq", qL, "qL", -93600.0, 3 * L)
            low_parts(t + 1)
    tt(T.qf[:], P(PL), T.Yq[:], A.add, [PL, "Yq"], ["qf"])
    dmas("y", "so", [(T.yc[:], T.qf[0::16, :])], ["qf"], [], 32 * L)
    dmas("s", "so", [(T.ye[:], T.Ef[:])], ["Ef"], [], 512 * L)

    count = issue()
    for s in ("sv", "ss", "sp", "sg", "so"):
        g.sync.wait_ge(T.sem[s], count[s])
    g.wait_ge(T.sem.ls, count["ls"])
